import numpy as np, ml_dtypes
CORES = [40,41,42,43,44,45,46,47]
N = 8
import mx_ref
BF = ml_dtypes.bfloat16
def entries(a):
    return np.ascontiguousarray(a.T).reshape(-1)
def table(e):
    return np.ascontiguousarray(np.reshape(e, (-1, 16)).T).astype(np.int32)
def gcols(t, e):
    v = np.concatenate([t.reshape(8, 16, -1, 4), np.zeros((8, 16, 1, 4), BF)], axis=2)
    return np.ascontiguousarray(np.stack([v[g][:, e[g]] for g in range(8)])).reshape(128, -1)
def gpick(z, e):
    return np.concatenate([z[16 * g:16 * g + 16][:, e[g]] for g in range(8)])
def tile(rs):
    return np.stack(rs, axis=2).reshape(128, -1).astype(BF)
def pick(q, e):
    c = np.concatenate([q[0].reshape(128, -1, 4), np.zeros((128, 1, 4), np.uint8)], axis=1); s = np.concatenate([q[1], np.ones((16, 1), np.uint8)], axis=1)
    return (np.ascontiguousarray(c[:, e].reshape(128, -1)), np.ascontiguousarray(s[:, e]))
def join(*qs):
    return (np.concatenate([q[0] for q in qs], axis=1), np.concatenate([q[1] for q in qs], axis=1))
def put(q, e, v):
    c, s = q[0].reshape(128, -1, 4).copy(), q[1].copy(); c[:, e] = v[0].reshape(128, -1, 4); s[:, e] = v[1]
    return (c.reshape(128, -1), s)
def pk(c, s):
    return (np.ascontiguousarray(c), mx_ref.live(s))
def emit(q):
    return q[0], q[1]
def packed(v, rng):
    q = [mx_ref.quantize(np.ascontiguousarray(v[r])) for r in range(N)]
    return np.stack([a for a, b in q]), np.stack([mx_ref.plane(b, rng) for a, b in q])
def values_of_codes():
    e, c = np.zeros((128, 128, 4), np.float32), np.zeros((128, 2, 4), np.uint8)
    e[np.arange(128), np.arange(128), 0] = 1
    c[:127, :, 0] = np.arange(256).reshape(2, 128).T[:127]
    return mx_ref.matmul(mx_ref.quantize(e.reshape(128, 512).astype(BF)), (c.reshape(128, 8), np.full((16, 2), 127, np.uint8))).T.reshape(-1).astype(np.float64)
CODE_VALUE, SCALE_VALUE = values_of_codes(), 2.0 ** (np.arange(256) - 127.0)
def decode(q):
    return (CODE_VALUE[q[0]].reshape(16, 8, -1, 4) * SCALE_VALUE[q[1]][:, None, :, None] + 0.0).reshape(128, -1).astype(np.float32)
def f(rng, *shape):
    return mx_ref.flush((rng.standard_normal(shape, dtype=np.float32) * np.exp2(rng.integers(-2, 3, shape[:-1] + (1,)))).astype(BF))
def wide(rng, *shape, cols=0):
    v = rng.standard_normal(shape, dtype=np.float32) * np.exp2(rng.integers(-12, 13, shape)).astype(np.float32)
    if cols: v *= np.repeat(np.exp2(rng.integers(-cols, cols + 1, shape[:-2] + (1, shape[-1] // 4))) * (rng.random(shape[:-2] + (1, shape[-1] // 4)) > 0.0625), 4, axis=-1).astype(np.float32)
    return mx_ref.flush(v.astype(BF))
C, H, R = 384, 192, 3
WIDTH = [1, 3, 6, 12, 24, 48, 96, 192]
def big(v):
    v = v.astype(np.float32)
    v[np.abs(v) < np.float32(2.0 ** -16)] = 0
    return v.astype(BF)
def numbers_of(rng):
    return {"x": big(f(rng, N, 128, 4 * C)), "u": np.array(f(rng, N, 128, 512)), "v": np.array(f(rng, N, 128, 512))}
def bases(rng):
    return np.stack([table(rng.permutation(C)) for r in range(N)])
def layers(rng):
    return big(f(rng, N, 128, 2048)).reshape(N, 8, 16, 4, 8, 16, 4)
def weights(rng, w):
    c, s = packed(np.ascontiguousarray(w).reshape(N, 128, 2048), rng)
    return {"wc": c, "ws": s}
def setup_inputs(rng):
    return {**numbers_of(rng), "p": bases(rng), **weights(rng, layers(rng))}
def setup_inputs_ties(rng):
    d = numbers_of(rng)
    p = bases(rng)
    o = rng.permutation(N)
    x = d["x"].astype(np.float32).reshape(N, 8, 16, C, 4)
    n = (N, 8, 8, C, 4)
    x[:, :, 8:] = (1.125 + 0.25 * rng.integers(0, 4, n)) * np.exp2(-1.0 * rng.integers(8, 15, n)) * rng.choice([-1.0, 1.0], n)
    x[:, :, 8, :, 0] = 1.96875
    x[:, :, :8] = 0
    u = d["u"].reshape(N, 128, 128, 4)
    u[:, :, ::16] = 0
    for r in range(N):
        if o[r] % 2 == 1: x[r, :, 0, :, 0] = rng.integers(0, 4, (8, C))
        else: x[r, :, 0, :, 0] = rng.integers(0, 7, (1, C)) + rng.integers(0, 2, (8, C))
        for h in range(0, 128, 16): u[r, h, h, 0] = 0.0 if o[r] == 0 else -1.0 if o[r] == 1 else 1.0
        if o[r] == 0:
            x[r, 7, 0, :, 0] = 0
            x[r, 7, 0, p[r, 0, 0], 0] = 1
            u[r, 112, 112, 0] = 1.0
    w = layers(rng)
    w[:, :, :, :, :, :8] = 0
    return {"x": x.reshape(N, 128, 4 * C).astype(BF), "u": u.reshape(N, 128, 512), "v": d["v"], "p": p, **weights(rng, w)}
def setup_inputs_near(rng):
    d = numbers_of(rng)
    x = d["x"].astype(np.float32).reshape(N, 8, 16, C, 4)
    u = d["u"].reshape(N, 128, 128, 4)
    o = rng.permutation(N) % 4
    x[:, :, 0] = 0
    x[:, :, 8:] = 0
    u[:, :, ::16] = 0
    for r in range(N):
        k = 1.0 if o[r] == 0 else 2.0 ** -30
        if o[r] < 3:
            s = rng.integers(0, 252, (1, C)) + rng.integers(0, 4, (8, C))
            for i in range(2): x[r, :, 8 + i] = ((s[:, :, None] >> (4 * i + np.arange(4))) & 1) * np.exp2(4 * i + np.arange(4) - 23.0)
            if o[r] < 2:
                x[r, :, 0, :, 0] = rng.choice([-1.0, 1.0], C)
                x[r, :, 11, :, 0] = 2.0 ** -10
            for g in rng.permutation(8)[:4]: x[r, g, 0, rng.integers(C), 0] = 2.0 ** 29 * rng.choice([-1.0, 1.0])
        else:
            for i in (10, 12): x[r, :, i, :, 0] = (1.0 + 0.125 * rng.integers(0, 2, (8, C))) * 2.0 ** -30
        for h in range(0, 128, 16):
            if o[r] < 3:
                u[r, h, h, 0] = k
                u[r, h + 8:h + 10, h] = k
                u[r, h + 11, h, 0] = k
            else:
                a = rng.choice([-1.0, 1.0])
                u[r, h + 10, h, 0] = 1.125 * k * a
                u[r, h + 12, h, 0] = -k * a
    w = layers(rng)
    for i in (0, 8, 9, 10, 11, 12, 13, 14, 15):
        w[:, :, i] = 0
        w[:, :, :, :, :, i] = 0
    return {"x": x.reshape(N, 128, 4 * C).astype(BF), "u": u.reshape(N, 128, 512), "v": d["v"], "p": bases(rng), **weights(rng, w)}
def setup_inputs_huge(rng):
    d = numbers_of(rng)
    o = rng.permutation(N)
    x = 0.6 + 0.06 * rng.random((N, 8, 16, C, 4)) + 0.03 * rng.random((N, 1, 1, C, 1))
    a = 1.0 - 0.1 * rng.random((N, 128, 8, 4))
    for r in range(N):
        if o[r] < N // 2: a[r] *= -1.0
        else:
            x[r] *= rng.choice([-1.0, 1.0], (1, 1, C, 1))
            a[r] *= rng.choice([-1.0, 1.0], (1, 8, 1))
    u = d["u"].reshape(N, 128, 128, 4)
    u[:, :, ::16] = (2.0 ** 30 * a).astype(np.float32).astype(BF)
    w = np.zeros((N, 128, 4, 128, 4), np.float32)
    i = np.arange(128)
    for b in range(4): w[:, i, b, i, b] = -4
    return {"x": (2.0 ** 30 * x).astype(np.float32).reshape(N, 128, 4 * C).astype(BF), "u": u.reshape(N, 128, 512), "v": d["v"], "p": bases(rng), **weights(rng, w.astype(BF))}
def setup_inputs_ends(rng):
    v = np.array(f(rng, N, 128, 512))
    o = rng.permutation(N) % 4
    x, u = np.zeros((N, 128, C, 4), np.float32), np.zeros((N, 128, 128, 4), np.float32)
    w, e = np.zeros((N, 128, 4, 128, 4), np.float32), []
    i = np.arange(128)
    for r in range(N):
        c = rng.choice([-1.0, 1.0], (1, C, 1))
        a = rng.choice([-1.0, 1.0], (1, 128, 1))
        if o[r] == 0:
            x[r] = 2.0 ** 30
            x[r, 64:] *= rng.choice([0.5, 1.0], (64, C, 4))
            x[r, 64:, ::4] = 2.0 ** 30
            u[r] = -2.0 ** 30
            u[r, 64:, :64] = 0
        elif o[r] == 1:
            x[r] = 2.0 ** 30 * c
            u[r] = 2.0 ** 30 * a
        elif o[r] == 2:
            x[r] = 2.0 ** -29 * rng.choice([-1.0, 1.0], (128, C, 4))
            u[r] = 2.0 ** -30 * rng.choice([-1.0, 1.0], (128, 128, 4))
        else:
            x[r] = 2.0 ** -29 * c
            u[r] = 2.0 ** -30 * a
        if o[r] > 1:
            for b in range(4): w[r, i, b, i, b] = 2.0 ** -20
        e.append(table(np.arange(C) if o[r] % 2 == 0 else C - 1 - np.arange(C)))
    v = (np.where(v < 0, -1.0, 1.0) * np.where(rng.permutation(N) % 2, 2.0 ** -30, 2.0 ** 30)[:, None, None]).astype(np.float32).astype(BF)
    return {"x": x.reshape(N, 128, 4 * C).astype(BF), "u": u.reshape(N, 128, 512).astype(BF), "v": v, "p": np.stack(e), **weights(rng, w.astype(BF))}
def setup_inputs_spread(rng):
    d = setup_inputs(rng)
    d["x"] = big(wide(rng, N, 128, 4 * C, cols=6))
    return d
def check_inputs(d):
    bad = []
    for k in ("x", "u", "v"):
        a = np.abs(d[k].astype(np.float32))
        if not (np.isfinite(a).all() and ((a == 0) | (a >= 2.0 ** -30) & (a <= 2.0 ** 30)).all()): bad.append("a value of " + k)
    none, least, most = [emit(mx_ref.quantize(np.full((128, 16), k, np.float32).astype(BF)))[1][0, 0] for k in (0.0, 2.0 ** -30, 2.0 ** 30)]
    for r in range(N):
        if not np.array_equal(np.sort(d["p"][r].reshape(-1)), np.arange(C)): bad.append("p: not every column once")
        if ((d["wc"][r] == 0x7F) | (d["wc"][r] == 0xFF)).any(): bad.append("wc: a code that is no number")
        s = mx_ref.live(d["ws"][r])
        if ((s != none) & ((s < least) | (s > most))).any(): bad.append("ws: a scale out of range")
    return bad
def reference(x, u, v, p, wc, ws):
    qu = [mx_ref.quantize(u[r]) for r in range(N)]
    lay = [pk(wc[r], ws[r]) for r in range(N)]
    now = [x[r] for r in range(N)]
    base = [entries(p[r]) for r in range(N)]
    order = np.zeros((N, 8, C), np.int64)
    for t in range(R):
        own, sent = [], []
        for r in range(N):
            q = mx_ref.quantize(now[r])
            own.append(decode(q))
            s = mx_ref.matmul(qu[r], q)[::16] + np.float32(0.0)
            o = base[r]
            for g in range(8):
                key = np.maximum.accumulate(s[g][o].reshape(-1, WIDTH[g]), axis=1).reshape(-1, 2 * WIDTH[g])
                o = np.take_along_axis(o.reshape(-1, 2 * WIDTH[g]), np.argsort(key, axis=1, kind="stable"), axis=1).reshape(-1)
                order[r, g] = o
            base[r] = o
            a = own[r].astype(BF)
            z = (gcols(a, order[r, :, :H]).astype(np.float32) + gcols(a, order[r, :, H:]).astype(np.float32)) * np.float32(0.5)
            sent.append(mx_ref.quantize(z.astype(BF)))
        for r in range(N):
            q = sent[(r - 1) % N]
            place = np.argsort(order[r], axis=1) % H
            now[r] = tile([gpick(mx_ref.matmul(pick(lay[r], np.arange(128 * b, 128 * b + 128)), q), place) * np.float32(0.03125) + own[r][:, b::4] for b in range(4)])
    y, od = np.zeros((N, 128, C), np.float32), np.zeros((N, 8, C), np.float32)
    oc, osc = np.zeros((N, 128, 4 * C), np.uint8), np.zeros((N, 16, C), np.uint8)
    for r in range(N):
        q = mx_ref.quantize(now[r])
        y[r] = mx_ref.matmul(mx_ref.quantize(v[r]), q)
        od[r] = order[r]
        oc[r], osc[r] = emit(q)
    return {"y": y, "od": od, "oc": oc, "osc": osc}

@@ -1,0 +1,520 @@
+from concourse.mybir import dt, AluOpType as A, ActivationFunctionType as F_
+
+NR, H = 3, 192
+BIG = 1e29
+MAG = 201326592.0
+W = [1, 3, 6, 12, 24, 48, 96, 192]
+SCRATCH = {"ps": ("psum", [128, 4096], "float32")}
+ALIAS = {}
+for _d, _s in (
+    ("float32", "cc:64 bof:3 bxf:3 bdf:3 b0:96 b1:48 bb:48 own:96 dd:3 os:3 pg:18 hm:18 ad:18 ldm:24 xm:24 x1:3 ow:24 h2:24 aj:24 iw:24 odf:384 odx:384 psb:768 g3:384 yb:384 sgb:3072 mk:48 a24f:24"),
+    ("bfloat16", "ioc:384 km:384 on:128 m4:147 m6:291 m7:579 idt:384 ea:2048 eb:2560 ut:512 vt:512 xt:1536 fb:1536 fh:1536 cm:147 c4:147 cm6:291 c6:291 cm7:579 c7:579 tx5:512 tx6:512 tx7:512 bc:384 "
+                 "w1:768 t1:768 w2:768 t2:768 az:768 zt:768"),
+    ("int32", "pi:1 pw:16 bi:8 uli:64 a24:24 pin:24"),
+    ("uint16", "ul:64 stl:48 lp0:24 lbox:6 lbp:3 brow:384 lb5:3 lb6:12 lb7:24 pl:4 plo:4 l6:12 l7:24 plu:24 lz:24 lj:24 lr:24"),
+    ("float8_e4m3fn_x4", "eac:512 ebc:640 uc:128 uqc:1024 vc:128 wq:512 xc:384 tc:128 zc0:192 zc1:192 zc2:192 lc0:192 lc1:192 lc2:192"),
+    ("uint8", "eas:512 ebs:640 us:128 uqs:1024 vs:128 wsc:512 xs:384 tsc:128 zs0:192 zs1:192 zs2:192 ls0:192 ls1:192 ls2:192"),
+):
+    for _w in _s.split():
+        SCRATCH[_w.split(":")[0]] = ("sbuf", [128, int(_w.split(":")[1])], _d)
+for _b, _s in (("kc", "fi:48 posr:48 aa:96 r2:48 r3:48 r4:48 r5:48 r6:192 r7:384 x8:16 mx4:16 mx8:16 mx8s:16 pst:16 psl:16 tmp:144 om:384 om0:96 ng:48 bm:192"),
+               ("sc", "sc1:48 sc2:48 sc3:48 sc4:48 sc5:48 sc5o:48 sc6:192 sc7:384"), ("so", "so:48 so5:48 so6:192 so7:384"), ("key", "key:48 key5:48 key6:192 key7:384")):
+    _o = 0
+    for _w in _s.split():
+        ALIAS[_w.split(":")[0]] = (_b, _o)
+        _o += int(_w.split(":")[1])
+    SCRATCH[_b] = ("sbuf", [128, _o], "float32")
+SEMAPHORES = ["sv", "ss", "st", "sg", "ar0", "ar1", "ar2", "lsem", "dp", "dxin", "du", "dv", "dwc", "dws", "db5", "db6", "db7", "dbr", "dl", "dbo", "dbx", "dout"]
+
+
+def rank_program(g, core, T, topo):
+    rank = T.rank_of(core)
+    if rank is None:
+        return
+    Q = {"v": g.vector, "s": g.scalar, "t": g.tensor, "g": g, "y": g.sync}
+    SEM = {"v": "sv", "s": "ss", "t": "st", "g": "sg"}
+    cnt, hist, dmh, acc = {}, {}, {}, {}
+    known = {e: {} for e in Q}
+    late, mode = [], {"defer": False, "mix": False}
+
+    def hit(r, q):
+        if r[2] <= q[1] or q[2] <= r[1] or r[5] <= q[4] or q[5] <= r[4]:
+            return False
+        return not (r[3] == q[3] and r[3] > 1 and (r[1] - q[1]) % r[3])
+
+    def need(e, sem, val):
+        k = known[e]
+        if k.get(sem, 0) >= val:
+            return
+        Q[e].wait_ge(T.sem[sem], val)
+        for s_, v_ in hist.get((sem, val), {}).items():
+            k[s_] = max(k.get(s_, 0), v_)
+        k[sem] = max(k.get(sem, 0), val)
+
+    def op(e, make, writes, reads, sem=None, pre=()):
+        if mode["defer"]:
+            late.append((e, make, writes, reads))
+            return
+        own = SEM.get(e) if sem is None else None
+        s = own if sem is None else sem
+        todo = {}
+        both = [(r, True) for r in writes] + [(r, False) for r in reads]
+        for r, wr in both:
+            bank = r[0] == "ps"
+            for q, qw, qs, qv in acc.get(r[0], []):
+                if bank and r[1] // 512 != q[1] // 512 or not bank and not hit(r, q) or not (wr or qw or bank):
+                    continue
+                if qs == own and (not hit(r, q) or not (wr or qw) or (e == "t" and wr)):
+                    continue
+                todo[qs] = max(todo.get(qs, 0), qv)
+        for a_, b_ in sorted(todo.items(), key=lambda z: z[0] in dmh) + list(pre):
+            if known[e].get(a_, 0) < b_:
+                need(e, a_, cnt[a_] if a_ in dmh else b_)
+        inc = 1 if sem is None else 16
+        make().then_inc(T.sem[s], inc)
+        cnt[s] = cnt.get(s, 0) + inc
+        h = dict(known[e])
+        if sem is not None:
+            old = dmh.setdefault(s, {})
+            for a_, b_ in h.items():
+                old[a_] = max(old.get(a_, 0), b_)
+            h = dict(old)
+        h[s] = cnt[s]
+        hist[(s, cnt[s])] = h
+        for r, wr in both:
+            keep = []
+            for x in acc.get(r[0], []):
+                q = x[0]
+                same = q == r and (wr or (not x[1] and x[2] == s))
+                if not (same or wr and r[3] == 1 and r[1] <= q[1] and q[2] <= r[2] and r[4] <= q[4] and q[5] <= r[5]):
+                    keep.append(x)
+            acc[r[0]] = keep + [(r, wr, s, cnt[s])]
+        if e == "v" and mode["mix"] and late:
+            mode["mix"] = False
+            op(*late.pop(0))
+            mode["mix"] = True
+
+    def P(name, a, b, st=1, p0=0, p1=128):
+        if name in ALIAS:
+            name, o = ALIAS[name]
+            a, b = a + o, b + o
+        t, c = T[name], slice(a, b) if st == 1 else slice(a, b, st)
+        ap = t[:, c] if (p0, p1) == (0, 128) else t[p0:p1, c]
+        return (ap, [(name, a, b, st, p0, p1)], [])
+
+    def IND(w, o):
+        return (w[0].indirect(o[0]), w[1], o[1])
+
+    def PS(bank, a, b, p0=0, p1=128):
+        return P("ps", 512 * bank + a, 512 * bank + b, 1, p0, p1)
+
+    def scl(s):
+        return (s[0], s[1]) if isinstance(s, tuple) else (s, [])
+
+    def tc(o, i):
+        op("v", lambda: g.vector.tensor_copy(o[0], i[0]), o[1], i[1] + i[2] + o[2])
+
+    def tt(o, i, j, k):
+        op("v", lambda: g.vector.tensor_tensor(o[0], i[0], j[0], k), o[1], i[1] + i[2] + j[1])
+
+    def ts(o, i, s1, s2, k1, k2=None):
+        (a, ra), (b, rb) = scl(s1), scl(s2)
+        op("v", lambda: g.vector.tensor_scalar(o[0], i[0], a, b, k1, k2) if k2 else g.vector.tensor_scalar(o[0], i[0], a, None, k1), o[1], i[1] + i[2] + ra + rb)
+
+    def scan(o, d0, d1, init, k0, k1):
+        op("v", lambda: g.vector.tensor_tensor_scan(o[0], d0[0], d1[0], init, k0, k1), o[1], d0[1] + d1[1])
+
+    def fill(o, c):
+        op("v", lambda: g.vector.memset(o[0], c), o[1], [])
+
+    def tr(o, i):
+        op("v", lambda: g.vector.transpose(o[0], i[0]), o[1], i[1])
+
+    def quant(c, s, i):
+        op("v", lambda: g.vector.quantize_mx(c[0], s[0], i[0]), c[1] + s[1], i[1])
+
+    def act(o, i, func=F_.Copy, bias=None, scale=None):
+        kw, rr = {}, []
+        for n, v in (("bias", bias), ("scale", scale)):
+            if v is not None:
+                kw[n], ra = scl(v)
+                rr = rr + ra
+        op("s", lambda: g.scalar.activation(o[0], i[0], func, **kw), o[1], i[1] + i[2] + rr)
+
+    def mm(o, l, ls, r, rs, start=True, stop=True, pre=()):
+        op("t", lambda: g.tensor.matmul_mx(o[0], l[0], ls[0], r[0], rs[0], start, stop), o[1], l[1] + ls[1] + r[1] + rs[1], pre=pre)
+
+    def dma(e, sem, o, i, wr, rd):
+        op(e, lambda: Q[e].dma_start(o, i), wr, rd, sem=sem)
+
+    def io(o, pat, base=0, cm=0, small=True):
+        op("g", lambda: g.iota(o[0], pat, base, cm, allow_small_or_imprecise_dtypes=True) if small else g.iota(o[0], pat, base, cm), o[1], [])
+
+    def sel(o, i, pat, cmp, base, cm):
+        op("g", lambda: g.affine_select(o[0], i[0], pat, cmp, 0.0, base, cm), o[1], i[1])
+
+    col = lambda k: P("cc", k, k + 1)
+    BFC, SGC, S29, SSC = 0, 8, 16, 22
+    PM, PM3, PM7, PM31, PMX, K6L, K7L, K5O, A6, A7, AF, Q96, O16, T0 = 30, 31, 32, 33, 34, 36, 37, 38, 40, 41, 42, 43, 44, 48
+    bit = lambda b: col(BFC + b)
+    sg = lambda k: col(SGC + k - 1)
+    TA, TB = col(T0 + 6), col(T0 + 7)
+
+    for q in range(8):
+        dma("y", "dp", T.pin[16 * q:16 * q + 16, :], T.p[:, :], P("pin", 0, 24, 1, 16 * q, 16 * q + 16)[1], [])
+    dma("s", "dxin", T.xt[:, :], T.x[:, :], P("xt", 0, 1536)[1], [])
+    dma("y", "du", T.ut[:, :], T.u[:, :], P("ut", 0, 512)[1], [])
+    io(P("pi", 0, 1), [[0, 1]], 0, 1, False)
+    io(P("uli", 0, 64), [[16, 8], [0, 8]], small=False)
+    io(P("fi", 0, 48), [[0, 3], [1, 16]])
+    io(P("pst", 0, 3), [[1, 3]], 0, 3)
+    io(P("ioc", 0, 384), [[1, 384]], -192)
+    io(P("posr", 0, 48), [[1, 48]])
+    io(P("x8", 0, 8), [[1, 8]])
+    io(P("a24", 0, 24), [[32, 24]], small=False)
+    ON, o6, o7 = P("on", 0, 128), P("idt", 128, 256), P("idt", 256, 384)
+    fill(ON, 1.0)
+    fill(P("ea", 0, 2048), 0.0)
+    for b in range(4):
+        sel(P("ea", 512 * b + b, 512 * b + 512, 4), ON, [[-1, 128]], A.is_equal, 0, 1)
+    sel(P("idt", 0, 128), ON, [[-32, 4], [16, 2], [-1, 16]], A.is_equal, -16, 1)
+    sel(o6, ON, [[-64, 2], [0, 4], [-4, 16]], A.is_ge, 0, 1)
+    sel(o7, ON, [[0, 8], [-8, 16]], A.is_ge, 0, 1)
+    sel(o6, o6, [[64, 2], [0, 4], [4, 16]], A.is_ge, 3, -1)
+    sel(o7, o7, [[0, 8], [8, 16]], A.is_ge, 7, -1)
+    for n, w, c in (("eb", 2560, 0), ("tx5", 512, 0), ("r6", 576, 0), ("tx6", 512, 0), ("m6", 291, 1), ("tx7", 512, 0), ("m7", 579, 1), ("w1", 768, 0), ("w2", 768, 0)):
+        io(P(n, 0, w), [[0, w]], c)
+    io(P("km", 0, 384), [[0, 2], [1, 192]])
+    for b in range(7):
+        ts(P("bi", b, b + 1), P("pi", 0, 1), b, 1, A.logical_shift_right, A.bitwise_and)
+    for k, m in ((0, 15), (1, 3), (2, 7), (3, 31)):
+        ts(P("pw", k, k + 1), P("pi", 0, 1), m, None, A.bitwise_and)
+    ts(P("pw", 8, 9), P("pi", 0, 1), 4, None, A.logical_shift_right)
+    for k in (1, 2, 3):
+        ts(P("pw", 4 + k, 5 + k), P("pw", 0, 1), k, None, A.logical_shift_right)
+    tc(P("cc", BFC, BFC + 7), P("bi", 0, 7))
+    tc(P("cc", PM, PM + 4), P("pw", 0, 4))
+    tc(P("ul", 0, 64), P("uli", 0, 64))
+    tc(P("cc", T0, T0 + 4), P("pw", 5, 9))
+    ts(P("cc", SGC, SGC + 7), P("cc", BFC, BFC + 7), -2.0, 1.0, A.mult, A.add)
+
+    def base_out(e="odf", sem="dbo", to="bof", p=112):
+        dma("y", sem, T[to][:, :], T[e][p:p + 1, :], P(to, 0, 3)[1], P(e, 0, 384)[1])
+
+    tc(P("lp0", 0, 24), P("pin", 0, 24))
+    act(P("odf", 0, 384), IND(P("ioc", 0, 384), P("lp0", 0, 24)), F_.Identity, bias=192.0)
+    base_out()
+    ts(P("cc", S29, S29 + 4), P("cc", SGC, SGC + 4), BIG, None, A.mult)
+    tt(P("cc", SSC, SSC + 6), P("cc", SGC, SGC + 6), P("cc", SGC + 1, SGC + 7), A.mult)
+    uw, uo, ul = P("uc", 0, 128), P("uqc", 0, 1024), P("ul", 0, 64)
+    quant(uw, P("us", 0, 128), P("ut", 0, 512))
+    tc(P("odx", 0, 384, 2), P("odf", 1, 384, 2))
+    tc(P("odx", 1, 384, 2), P("odf", 0, 384, 2))
+    base_out("odx", "dbx", "bxf")
+    dma("y", "dwc", T.wq[:, :].bitcast(dt.uint8), T.wc[:, :], P("wq", 0, 512)[1], [])
+    dma("y", "dws", T.wsc[:, :], T.ws[:, :], P("wsc", 0, 512)[1], [])
+    dma("y", "dv", T.vt[:, :], T.v[:, :], P("vt", 0, 512)[1], [])
+    act(P("uqs", 0, 1024), IND(P("us", 0, 128), ul))
+    op("v", lambda: g.vector.tensor_copy(uo[0].bitcast(dt.uint32), uw[0].bitcast(dt.uint32).indirect(ul[0])), uo[1], uw[1] + ul[1])
+
+    def scores_in():
+        quant(P("xc", 0, 192), P("xs", 0, 192), P("xt", 0, 768))
+        quant(P("xc", 192, 384), P("xs", 192, 384), P("xt", 768, 1536))
+
+    def smm(gr, bank, a=0, b=384):
+        mm(PS(bank, 0, b - a), P("uqc", 128 * gr, 128 * gr + 128), P("uqs", 128 * gr, 128 * gr + 128), P("xc", a, b), P("xs", a, b))
+
+    def fmm(b, bank):
+        mm(PS(bank, 0, 384), P("eac", 128 * b, 128 * b + 128), P("eas", 128 * b, 128 * b + 128), P("xc", 0, 384), P("xs", 0, 384))
+
+    def xmm(k, bank, start=True, stop=True):
+        mm(PS(bank, 0, 128), P("ebc", 128 * k, 128 * k + 128), P("ebs", 128 * k, 128 * k + 128), P("tc", 0, 128), P("tsc", 0, 128), start, stop)
+
+    own = P("tmp", 0, 48)
+    ts(own, P("fi", 0, 48), col(PM), None, A.is_equal)
+    ts(TB, col(T0 + 3), -48.0, None, A.mult)
+    ts(TA, col(PM), sg(1), None, A.add)
+    fill(P("m4", 0, 147), 1.0)
+    for h in (0, 48):
+        ts(P("aa", h, h + 48), own, -1.0, 1.0, A.mult, A.add)
+        for t in range(3):
+            ts(P("om0", h + 16 * t, h + 16 * t + 16), P("tmp", 16 * t, 16 * t + 16), sg(1), 1.0 if t != 1 else -1.0, A.mult, A.mult)
+    ts(P("pg", 0, 3), P("pst", 0, 3), TB, None, A.add)
+    ts(P("tmp", 48, 96), P("fi", 0, 48), TA, None, A.is_equal)
+    ts(P("ng", 0, 48), P("aa", 0, 48), -BIG, None, A.mult)
+    fill(P("m4", 0, 147, 49), 0.0)
+    ts(P("psl", 0, 3), P("pg", 0, 3), sg(1), None, A.mult)
+    ts(P("bm", 0, 48), P("tmp", 48, 96), 0.0, col(S29), A.is_equal, A.mult)
+    scores_in()
+    mode["defer"] = True
+    fill(P("r2", 0, 192), 0.0)
+    for k in (2, 3, 4, 5, 6, 7):
+        ts(P("om", 48 * k, 48 * k + 48), own, sg(k), None, A.mult)
+    for k in (2, 3, 4):
+        ts(TA, col(T0 + k - 2), sg(k), float(W[k]), A.add, A.mult)
+        ts(TB, TA, float(W[k]), None, A.add)
+        ts(P("tmp", 48, 96), P("posr", 0, 48), TA, None, A.is_ge)
+        ts(P("tmp", 96, 144), P("posr", 0, 48), TB, None, A.is_ge)
+        fill(P("r%d" % k, 0, 48, W[k]), -BIG)
+        tt(P("tmp", 48, 96), P("tmp", 48, 96), P("tmp", 96, 144), A.subtract)
+        ts(P("bm", 48 * k - 48, 48 * k), P("tmp", 48, 96), 0.0, col(S29 + k - 1), A.is_equal, A.mult)
+    quant(P("eac", 0, 512), P("eas", 0, 512), P("ea", 0, 2048))
+    for n in (5, 6, 7):
+        fill(P("r%d" % n, 0, 48 if n < 6 else 2 * W[n], W[n]), -BIG)
+    ts(col(Q96), col(T0 + 3), 96.0, None, A.mult)
+    ts(col(O16), bit(4), 16.0, None, A.mult)
+    ts(TA, bit(4), 48.0, sg(6), A.mult, A.mult)
+    ts(TB, bit(5), 111.0, -103.5, A.mult, A.add)
+    ts(col(K6L), TA, TB, None, A.add)
+    ts(col(K5O), bit(4), 48.0, None, A.mult)
+    ts(TA, sg(4), sg(6), -48.0, A.mult, A.mult)
+    ts(TB, bit(2), 48.0, 48.0, A.mult, A.add)
+    ts(col(A6), TA, TB, None, A.add)
+    ts(P("mx4", 0, 4), P("x8", 0, 4), col(PM3), None, A.is_equal)
+    ts(P("mx8", 0, 8), P("x8", 0, 8), col(PM7), None, A.is_equal)
+    for k, (src, a, b, wt) in enumerate(((0, 0, 128, 1.0), (128, 0, 128, 1.0), (256, 0, 128, 1.0), (256, 96, 112, 2.0), (256, 112, 128, 2.0))):
+        for d in range(2):
+            ts(P("eb", 512 * k + 4 * a + d, 512 * k + 4 * b, 4), P("idt", src + a, src + b), wt if d == 0 else 1.0, None, A.mult)
+    quant(P("ebc", 0, 512), P("ebs", 0, 512), P("eb", 0, 2048))
+    quant(P("ebc", 512, 640), P("ebs", 512, 640), P("eb", 2048, 2560))
+    for n, w in (("m6", 96), ("m7", 192)):
+        fill(P(n, 0, 3 * w + 3, w + 1), 0.0)
+    ts(P("mx8s", 0, 8), P("mx8", 0, 8), sg(6), None, A.mult)
+    ts(TA, sg(7), 103.5, None, A.mult)
+    ts(TB, bit(6), 192.0, -192.0, A.mult, A.add)
+    ts(col(K7L), TA, TB, None, A.add)
+    ts(TA, sg(4), sg(7), -96.0, A.mult, A.mult)
+    ts(col(A7), TA, 199.5, None, A.add)
+    ts(TA, bit(3), 384.0, 199.5, A.mult, A.add)
+    ts(TB, bit(3), -384.0, 208.0, A.mult, A.add)
+    ts(col(AF), TB, bit(4), TA, A.mult, A.add)
+    tc(P("a24f", 0, 24), P("a24", 0, 24))
+    tt(col(PMX), col(PM31), sg(1), A.add)
+    ts(P("stl", 0, 24), P("a24f", 0, 24), col(PM31), None, A.add)
+    ts(P("stl", 24, 48), P("a24f", 0, 24), col(PMX), None, A.add)
+    mode["defer"], mode["mix"] = False, True
+
+    def flush(n):
+        while len(late) > n:
+            op(*late.pop(0))
+
+    SGR = lambda k: P("sgb", 384 * k, 384 * k + 384)
+    EX, FIN, BF3 = 4, 5, 6
+    nxt = T.cores[(rank + 1) % len(T.cores)]
+    rid, pid = topo.addr(nxt)[0], topo.addr(nxt)[1]
+    eng = topo.engines(core, nxt)
+    half = len(eng) // 2
+    mask_c, mask_s = sum(1 << e for e in eng[:half]), sum(1 << e for e in eng[half:])
+    ends = lambda cn, w: P(cn, w, 3 * w + 3, w + 1)
+    heads = lambda cn, w: P(cn, 0, 3 * w + 3, w + 1)
+
+    def keys(so, key, n, res, sc, lst):
+        tc(IND(P(so, 0, n), lst), P(sc, 0, n))
+        scan(P(key, 0, n), P(res, 0, n), P(so, 0, n), -BIG, A.add, A.max)
+
+    def halves(so, key, res, w):
+        for h in (0, w):
+            scan(P(key, h, h + w), P(res, h, h + w), P(so, h, h + w), -BIG, A.add, A.max)
+
+    def owned(k, src):
+        tt(P("bb", 0, 48), src, P("om", 48 * k, 48 * k + 48), A.mult)
+        if k in (2, 3, 4):
+            tt(P("mk", 0, 48), P("key", 0, 48), P("bm", 48 * k - 48, 48 * k), A.add)
+        scan(P("own", 0, 48), P("aa", 0, 48), P("bb", 0, 48), 0.0, A.mult, A.add)
+
+    def count(k, cmn, cn, mn, w, other, mine=("own", 15, 16), parts=1):
+        for t in range(3):
+            o = mine[1] + mine[2] * t
+            ts(P(cmn, (w + 1) * t + 1, (w + 1) * t + w + 1), other, sg(k), P(mine[0], o, o + 1), A.mult, A.is_lt)
+        n = (3 * w + 3) // parts
+        for a in range(0, 3 * w + 3, n):
+            scan(P(cn, a, a + n), P(mn, a, a + n), P(cmn, a, a + n), 0.0, A.mult, A.add)
+
+    def lay(n, xs, tile, mask):
+        for t in range(3):
+            ts(P("xm", t, 3 * n, 3), P(mask, 0, n), xs[t], None, A.mult)
+        ts(P(tile, 0, 12 * n, 4), P("xm", 0, 3 * n), MAG, MAG, A.add, A.subtract)
+        tt(P(tile, 1, 12 * n, 4), P("xm", 0, 3 * n), P(tile, 0, 12 * n, 4), A.subtract)
+        quant(P("tc", 0, 128), P("tsc", 0, 128), P(tile, 0, 512))
+
+    pl, plo = P("pl", 0, 3), P("plo", 0, 3)
+    for r in range(NR):
+        last = r == NR - 1
+        if r:
+            scores_in()
+        smm(0, 0, 0, 192)
+        smm(0, 1, 192, 384)
+        smm(1, 2)
+        smm(2, 3)
+        tc(P("lbox", 0, 3), P("bof", 0, 3))
+        tc(P("lbox", 3, 6), P("bxf", 0, 3))
+        tt(P("bdf", 0, 3), P("bxf", 0, 3), P("bof", 0, 3), A.subtract)
+        act(P("sgb", 0, 192), PS(0, 0, 192))
+        tc(P("sgb", 192, 384), PS(1, 0, 192))
+        smm(3, 0)
+        smm(4, 1)
+        tt(P("b0", 0, 96), IND(SGR(0), P("lbox", 0, 6)), P("om0", 0, 96), A.mult)
+        scan(P("own", 0, 96), P("aa", 0, 96), P("b0", 0, 96), 0.0, A.mult, A.add)
+        tt(P("dd", 0, 3), P("own", 15, 48, 16), P("own", 63, 96, 16), A.is_gt)
+        for t in range(3):
+            ts(P("lbp", t, t + 1), P("dd", t, t + 1), P("bdf", t, t + 1), P("bof", t, t + 1), A.mult, A.add)
+        lp = P("lbp", 0, 3)
+        dma("y", "dbr", T.brow[0:1, 0:384], T.lbp[:, :], P("brow", 0, 384, 1, 0, 1)[1], lp[1])
+        for name, n, src in (("lb5", 3, lambda q: (16 * (q + 1 - 2 * (q % 2)), 16)), ("lb6", 12, lambda q: (64 * (q // 4), 64))):
+            for q in range(8):
+                a, m = src(q)
+                dma("y", "db" + name[2], T[name][16 * q:16 * q + 16, 0:n], T.lbp[a:a + m, 0:3], P(name, 0, n, 1, 16 * q, 16 * q + 16)[1], P("lbp", 0, 3, 1, a, a + m)[1])
+        for q in range(8):
+            dma("y", "db7", T.lb7[16 * q:16 * q + 16, 0:24], T.brow[0:1, 0:384], P("lb7", 0, 24, 1, 16 * q, 16 * q + 16)[1], P("brow", 0, 384, 1, 0, 1)[1])
+        act(SGR(1), PS(2, 0, 384))
+        act(heads("cm", 48), P("psl", 0, 3))
+        smm(5, 2)
+        act(SGR(2), PS(3, 0, 384))
+        act(P("sc2", 0, 48), IND(SGR(2), lp))
+        smm(6, 3)
+        s1, b1 = P("sc1", 0, 48), P("b1", 0, 48)
+        tt(s1, IND(SGR(1), lp), P("bm", 0, 48), A.add)
+        tt(b1, IND(SGR(1), lp), P("ng", 0, 48), A.add)
+        tt(P("sc1", 16, 32), P("sc1", 16, 32), P("sc1", 0, 16), A.max)
+        scan(P("own", 0, 48), b1, b1, -BIG, A.max, A.max)
+        tt(P("sc1", 32, 48), P("sc1", 32, 48), P("sc1", 16, 32), A.max)
+        ts(P("os", 0, 3), P("own", 15, 48, 16), sg(1), None, A.mult)
+        count(1, "cm", "c4", "m4", 48, s1, ("os", 0, 1))
+        for k in (2, 3, 4):
+            ts(pl, ends("c4", 48), sg(k - 1), None, A.mult)
+            act(heads("cm", 48), ends("c4", 48), scale=col(SSC + k - 2))
+            act(P("pg", 3 * k - 3, 3 * k), ends("c4", 48), scale=sg(k - 1))
+            keys("so", "key", 48, "r%d" % k, "sc%d" % k, pl)
+            owned(k, IND(P("key", 0, 48), pl))
+            count(k, "cm", "c4", "m4", 48, P("mk", 0, 48))
+            act(SGR(k + 1), PS(k - 2, 0, 384))
+            act(P("sc%d" % (k + 1), 0, 48), IND(SGR(k + 1), lp))
+            if k == 2:
+                smm(7, 0)
+            elif k == 3:
+                fmm(0, 1)
+            else:
+                act(P("sc5o", 0, 48), IND(SGR(5), P("lb5", 0, 3)))
+        flush(15)
+        ts(P("tx5", 0, 12, 4), ends("c4", 48), MAG, MAG, A.add, A.subtract)
+        tt(P("tx5", 1, 12, 4), ends("c4", 48), P("tx5", 0, 12, 4), A.subtract)
+        quant(P("tc", 0, 128), P("tsc", 0, 128), P("tx5", 0, 512))
+        xmm(0, EX)
+        fmm(1, 2)
+        act(heads("cm", 48), ends("c4", 48), scale=col(SSC + 3))
+        act(P("pg", 12, 15), ends("c4", 48), scale=sg(4))
+        act(SGR(6), PS(3, 0, 384))
+        fmm(2, 3)
+        act(P("sc6", 0, 192), IND(SGR(6), P("lb6", 0, 12)))
+        act(P("fb", 0, 384), PS(1, 0, 384))
+        ts(pl, ends("c4", 48), sg(4), None, A.mult)
+        keys("so", "key", 48, "r5", "sc5", pl)
+        ts(plo, PS(EX, 0, 3), sg(4), None, A.mult)
+        tt(P("bb", 0, 48), IND(P("key", 0, 48), pl), P("om", 240, 288), A.mult)
+        tc(IND(P("so5", 0, 48), plo), P("sc5o", 0, 48))
+        scan(P("own", 0, 48), P("aa", 0, 48), P("bb", 0, 48), 0.0, A.mult, A.add)
+        scan(P("key5", 0, 48), P("r5", 0, 48), P("so5", 0, 48), -BIG, A.add, A.max)
+        count(5, "cm", "c4", "m4", 48, P("key5", 0, 48))
+        flush(0)
+        lay(4, [P("c4", 49 * t + 48, 49 * t + 49) for t in range(3)], "tx6", "mx4")
+        xmm(1, EX)
+        fmm(3, 1)
+        act(heads("cm6", 96), ends("c4", 48), F_.Identity, bias=col(K6L), scale=col(SSC + 4))
+        act(P("pg", 15, 18), ends("c4", 48), scale=sg(5))
+        act(SGR(7), PS(0, 0, 384))
+        act(P("sc7", 0, 384), IND(SGR(7), P("lb7", 0, 24)))
+        act(P("fb", 384, 768), PS(2, 0, 384))
+        ts(pl, ends("c4", 48), sg(5), col(K5O), A.mult, A.add)
+        a = 3 if r else 0
+        hm, pg, ad = P("hm", a, 18), P("pg", a, 18), P("ad", a, 18)
+        ts(hm, pg, -7.5, MAG, A.add, A.add)
+        ts(P("l6", 0, 12), PS(EX, 0, 12), sg(3), col(A6), A.mult, A.add)
+        tc(IND(P("so6", 0, 192), P("l6", 0, 12)), P("sc6", 0, 192))
+        ts(hm, hm, MAG, col(Q96), A.subtract, A.add)
+        halves("so6", "key6", "r6", 96)
+        tt(P("bb", 0, 48), IND(P("key6", 0, 96), pl), P("om", 288, 336), A.mult)
+        tt(ad, hm, pg, A.add)
+        for gr in range(a // 3, 6):
+            dma("y", "dl", T.ldm[16 * gr:16 * gr + 16, 0:24], T.ad[:, 3 * gr:3 * gr + 3], P("ldm", 0, 24, 1, 16 * gr, 16 * gr + 16)[1], P("ad", 3 * gr, 3 * gr + 3)[1])
+        scan(P("own", 0, 48), P("aa", 0, 48), P("bb", 0, 48), 0.0, A.mult, A.add)
+        count(6, "cm6", "c6", "m6", 96, P("key6", 96, 192), parts=3)
+        lay(8, [P("c6", 97 * t + 96, 97 * t + 97) for t in range(3)], "tx7", "mx8s")
+        xmm(2, EX)
+        xmm(3, FIN, True, False)
+        act(heads("cm7", 192), ends("c6", 96), F_.Identity, bias=col(K7L), scale=col(SSC + 5))
+        act(P("fb", 768, 1152), PS(3, 0, 384))
+        act(P("bc", 0, 384), IND(P("ioc", 0, 384), P("lb7", 0, 24)))
+        act(P("fb", 1152, 1536), PS(1, 0, 384))
+        for b in range(4):
+            act(P("fh", 384 * b, 384 * b + 384), P("fb", 384 * b, 384 * b + 384), scale=0.5)
+        ts(pl, ends("c6", 96), sg(6), 103.5, A.mult, A.add)
+        ts(P("l7", 0, 24), PS(EX, 0, 24), col(A7), None, A.add)
+        tc(IND(P("so7", 0, 384), P("l7", 0, 24)), P("sc7", 0, 384))
+        halves("so7", "key7", "r7", 192)
+        owned(7, IND(P("key7", 0, 192), pl))
+        count(7, "cm7", "c7", "m7", 192, P("key7", 192, 384), parts=3)
+        x1 = [P("x1", t, t + 1) for t in range(3)]
+        for t in range(3):
+            ts(x1[t], P("c7", 193 * t + 192, 193 * t + 193), sg(7), -7.5, A.mult, A.add)
+        lay(8, x1, "tx7", "mx8")
+        xmm(4, FIN, False, True)
+        ts(P("plu", 0, 24, 1, 0, 96), P("ldm", 0, 24, 1, 0, 96), P("cc", O16, O16 + 1, 1, 0, 96), None, A.add)
+        ts(P("plu", 0, 24, 1, 96, 128), PS(FIN, 0, 24, 96, 128), P("cc", AF, AF + 1, 1, 96, 128), None, A.add)
+        tc(IND(P("w1", 0, 768), P("plu", 0, 24)), P("bc", 0, 384))
+        tr(P("t1", 0, 768), P("w1", 0, 768))
+        tt(P("ow", 0, 24), P("t1", 0, 768, 32), P("t1", 16, 768, 32), A.add)
+        ts(P("lz", 0, 24), P("ow", 0, 24), 192.0, None, A.add)
+        tc(P("az", 0, 192), IND(P("fh", 0, 384), P("lz", 0, 12)))
+        for b in range(1, 4):
+            act(P("az", 192 * b, 192 * b + 192), IND(P("fb", 384 * b, 384 * b + 384), P("lz", 0, 12)), scale=0.5)
+        for b in range(4):
+            tt(P("zt", b, 768, 4), IND(P("fh", 384 * b, 384 * b + 384), P("lz", 12, 24)), P("az", 192 * b, 192 * b + 192), A.add)
+        zc, zs = P("zc%d" % r, 0, H), P("zs%d" % r, 0, H)
+        quant(zc, zs, P("zt", 0, 768))
+        need("g", "sv", cnt["sv"])
+        g.remote_dma(T["lc%d" % r][:, 0:H].bitcast(dt.uint8), zc[0].bitcast(dt.uint8), T.sem["ar%d" % r], T.sem.lsem, pid, rid, mask_c)
+        g.remote_dma(T["ls%d" % r][:, 0:H], zs[0], T.sem["ar%d" % r], T.sem.lsem, pid, rid, mask_s)
+        act(P("odf", 0, 384), IND(P("w1", 0, 768), P("stl", 0, 24)), F_.Identity, bias=192.0)
+        if last:
+            dma("y", "dout", T.od[:, :], T.odf[0:128:16, :], [], P("odf", 0, 384)[1])
+        else:
+            base_out()
+            act(P("odx", 0, 384), IND(P("w1", 0, 768), P("stl", 24, 48)), F_.Identity, bias=192.0)
+            base_out("odx", "dbx", "bxf")
+        ts(P("h2", 0, 24), P("ow", 0, 24), 184.5, MAG, A.add, A.add)
+        ts(P("h2", 0, 24), P("h2", 0, 24), MAG - 192.0, col(O16), A.subtract, A.add)
+        tt(P("aj", 0, 24), P("h2", 0, 24), P("ow", 0, 24), A.add)
+        tc(P("lj", 0, 24), P("aj", 0, 24))
+        tc(IND(P("w2", 0, 768), P("lj", 0, 24)), P("km", 0, 384))
+        tr(P("t2", 0, 768), P("w2", 0, 768))
+        tt(P("iw", 0, 24), P("t2", 0, 768, 32), P("t2", 16, 768, 32), A.add)
+        tc(P("lr", 0, 24), P("iw", 0, 24))
+        fmm(3, BF3)
+        if r == 0:
+            quant(P("vc", 0, 128), P("vs", 0, 128), P("vt", 0, 512))
+        pb = lambda b: P("psb", 192 * b, 192 * b + 192)
+        for b in range(4):
+            mm(PS(b, 0, H), P("wq", 128 * b, 128 * b + 128), P("wsc", 128 * b, 128 * b + 128), P("lc%d" % r, 0, H), P("ls%d" % r, 0, H), pre=[("ar%d" % r, 2 * half)])
+        ts(pb(0), PS(0, 0, H), 0.03125, None, A.mult)
+        for b in range(1, 4):
+            act(pb(b), PS(b, 0, H), scale=0.03125)
+        act(P("g3", 0, 384), IND(pb(3), P("lr", 0, 24)))
+        for b in range(3):
+            tt(P("xt", b, 1536, 4), IND(pb(b), P("lr", 0, 24)), P("fb", 384 * b, 384 * b + 384), A.add)
+        tt(P("xt", 3, 1536, 4), P("g3", 0, 384), PS(BF3, 0, 384), A.add)
+    scores_in()
+    for h in range(2):
+        a, b = 192 * h, 192 * h + 192
+        q = P("xc", a, b)
+        dma("y", "dout", T.oc[:, 4 * a:4 * b], q[0].bitcast(dt.uint8), [], q[1])
+        mm(PS(h, 0, 192), P("vc", 0, 128), P("vs", 0, 128), q, P("xs", a, b))
+        if h == 0:
+            tc(P("yb", a, b), PS(h, 0, 192))
+        else:
+            act(P("yb", a, b), PS(h, 0, 192))
+        dma("y", "dout", T.y[:, a:b], T.yb[:, a:b], [], P("yb", a, b)[1])
+    for k in range(4):
+        dma("y", "dout", T.osc[4 * k:4 * k + 4, :], T.xs[32 * k:32 * k + 4, :], [], P("xs", 0, 384)[1])
+    g.wait_ge(T.sem.lsem, 2 * half * NR)
+    for s in list(cnt):
+        need("g", s, cnt[s])

@@ -3,28 +3,33 @@ from concourse.mybir import dt, AluOpType as A, ActivationFunctionType as F_
 NR, H = 3, 192
 BIG = 1e29
 MAG = 201326592.0
+UP, TINY = 0.6 * 2.0 ** -23, 2.0 ** -124
 W = [1, 3, 6, 12, 24, 48, 96, 192]
+SIDE = {1: 0, 2: 1, 3: 2, 4: 3, 5: 6, 6: 5, 7: 4}
+QX = [0, 2, 1, 3]
 SCRATCH = {"ps": ("psum", [128, 4096], "float32")}
 ALIAS = {}
 for _d, _s in (
-    ("float32", "cc:64 bof:3 bxf:3 bdf:3 b0:96 b1:48 bb:48 own:96 dd:3 os:3 pg:18 hm:18 ad:18 ldm:24 xm:24 x1:3 ow:24 h2:24 aj:24 iw:24 odf:384 odx:384 psb:768 g3:384 yb:384 sgb:3072 mk:48 a24f:24"),
-    ("bfloat16", "ioc:384 km:384 on:128 m4:147 m6:291 m7:579 idt:384 ea:2048 eb:2560 ut:512 vt:512 xt:1536 fb:1536 fh:1536 cm:147 c4:147 cm6:291 c6:291 cm7:579 c7:579 tx5:512 tx6:512 tx7:512 bc:384 "
-                 "w1:768 t1:768 w2:768 t2:768 az:768 zt:768"),
-    ("int32", "pi:1 pw:16 bi:8 uli:64 a24:24 pin:24"),
-    ("uint16", "ul:64 stl:48 lp0:24 lbox:6 lbp:3 brow:384 lb5:3 lb6:12 lb7:24 pl:4 plo:4 l6:12 l7:24 plu:24 lz:24 lj:24 lr:24"),
-    ("float8_e4m3fn_x4", "eac:512 ebc:640 uc:128 uqc:1024 vc:128 wq:512 xc:384 tc:128 zc0:192 zc1:192 zc2:192 lc0:192 lc1:192 lc2:192"),
-    ("uint8", "eas:512 ebs:640 us:128 uqs:1024 vs:128 wsc:512 xs:384 tsc:128 zs0:192 zs1:192 zs2:192 ls0:192 ls1:192 ls2:192"),
+    ("float32", "cc:64 bof:3 bxf:3 bdf:3 b0:96 o0:96 dd:3 pg:21 hm:21 ad:21 ldm:24 gs:24 hid:3 h7:8 ow:24 iw:24 odf:384 odp:384 odx:384 psb:768 g3:384 yb:384 sgb:3072 "
+                "rr:288 own:288 sab:448 key7:224 tk:224 uk:192 row0:48"),
+    ("bfloat16", "ioc:384 kma:768 on:128 m1:21 m4:147 m6:291 m7:579 ea:2048 ut:512 vt:512 xt:1536 fb:1536 fh:1536 cm1:21 c1:21 cm:147 c4:147 cm6:291 c6:291 cm7:579 c7:579 "
+                 "bc:192 val:384 w1:768 t1:768 w2:768 t2:768 az:768 zt:768"),
+    ("int32", "pi:1 bi:11 uli:64 pin:3"),
+    ("uint16", "ul:64 stl:48 l3:4 l0:6 lbox:6 lbp:4 lb7:12 lbt:12 lida:24 pl:6 pl7:4 l7:12 plu:24 lz:24 lr:24"),
+    ("float8_e4m3fn_x4", "eac:512 uc:128 uqc:1024 vc:128 wq:512 xc:384 zc0:192 zc1:192 zc2:192 lc0:192 lc1:192 lc2:192"),
+    ("uint8", "eas:512 us:128 uqs:1024 vs:128 wsc:512 xs:384 zs0:192 zs1:192 zs2:192 ls0:192 ls1:192 ls2:192"),
 ):
     for _w in _s.split():
         SCRATCH[_w.split(":")[0]] = ("sbuf", [128, int(_w.split(":")[1])], _d)
-for _b, _s in (("kc", "fi:48 posr:48 aa:96 r2:48 r3:48 r4:48 r5:48 r6:192 r7:384 x8:16 mx4:16 mx8:16 mx8s:16 pst:16 psl:16 tmp:144 om:384 om0:96 ng:48 bm:192"),
-               ("sc", "sc1:48 sc2:48 sc3:48 sc4:48 sc5:48 sc5o:48 sc6:192 sc7:384"), ("so", "so:48 so5:48 so6:192 so7:384"), ("key", "key:48 key5:48 key6:192 key7:384")):
+for _b, _s in (("kc", "fi:96 posr:96 aa:96 om:96 om0:96 omn:48 f2:48 f3:48 f4:48 mn1:48 mn2:48 mn3:48 mn4:48 mo1:48 mo2:48 mo3:48 mo4:48 x3:8 lpl:8 st:24"),
+               ("sc", "so1:48 so2:48 so3:48 so4:48 so5:48 so6:96 so7:192 sn1:48 sn2:48 sn3:48 sn4:48 sn5:48 sn6:96 sm:48 ab2:48 ab3:48 ab4:48 ab5:48 ab6:96"),
+               ("wn", "wo:96 wp:96 key:96")):
     _o = 0
     for _w in _s.split():
         ALIAS[_w.split(":")[0]] = (_b, _o)
         _o += int(_w.split(":")[1])
     SCRATCH[_b] = ("sbuf", [128, _o], "float32")
-SEMAPHORES = ["sv", "ss", "st", "sg", "ar0", "ar1", "ar2", "lsem", "dp", "dxin", "du", "dv", "dwc", "dws", "db5", "db6", "db7", "dbr", "dl", "dbo", "dbx", "dout"]
+SEMAPHORES = ["sv", "ss", "st", "sg", "ar0", "ar1", "ar2", "lsem", "dp", "dxin", "du", "dv", "dwc", "dws", "dbo", "dbx", "dout"]
 
 
 def rank_program(g, core, T, topo):
@@ -102,11 +107,20 @@ def rank_program(g, core, T, topo):
         ap = t[:, c] if (p0, p1) == (0, 128) else t[p0:p1, c]
         return (ap, [(name, a, b, st, p0, p1)], [])
 
+    def REV(name, a, b):
+        if name in ALIAS:
+            name, o = ALIAS[name]
+            a, b = a + o, b + o
+        return (T[name][:, slice(b - 1, a - 1 if a else None, -1)], [(name, a, b, 1, 0, 128)], [])
+
+    def QD(name, a, b, st, q, n=1):
+        return P(name, a, b, st, 32 * q, 32 * (q + n))
+
     def IND(w, o):
         return (w[0].indirect(o[0]), w[1], o[1])
 
-    def PS(bank, a, b, p0=0, p1=128):
-        return P("ps", 512 * bank + a, 512 * bank + b, 1, p0, p1)
+    def PS(bank, a, b):
+        return P("ps", 512 * bank + a, 512 * bank + b)
 
     def scl(s):
         return (s[0], s[1]) if isinstance(s, tuple) else (s, [])
@@ -122,7 +136,8 @@ def rank_program(g, core, T, topo):
         op("v", lambda: g.vector.tensor_scalar(o[0], i[0], a, b, k1, k2) if k2 else g.vector.tensor_scalar(o[0], i[0], a, None, k1), o[1], i[1] + i[2] + ra + rb)
 
     def scan(o, d0, d1, init, k0, k1):
-        op("v", lambda: g.vector.tensor_tensor_scan(o[0], d0[0], d1[0], init, k0, k1), o[1], d0[1] + d1[1])
+        a, ra = scl(init)
+        op("v", lambda: g.vector.tensor_tensor_scan(o[0], d0[0], d1[0], a, k0, k1), o[1], d0[1] + d1[1] + ra)
 
     def fill(o, c):
         op("v", lambda: g.vector.memset(o[0], c), o[1], [])
@@ -153,69 +168,93 @@ def rank_program(g, core, T, topo):
     def sel(o, i, pat, cmp, base, cm):
         op("g", lambda: g.affine_select(o[0], i[0], pat, cmp, 0.0, base, cm), o[1], i[1])
 
-    col = lambda k: P("cc", k, k + 1)
-    BFC, SGC, S29, SSC = 0, 8, 16, 22
-    PM, PM3, PM7, PM31, PMX, K6L, K7L, K5O, A6, A7, AF, Q96, O16, T0 = 30, 31, 32, 33, 34, 36, 37, 38, 40, 41, 42, 43, 44, 48
-    bit = lambda b: col(BFC + b)
-    sg = lambda k: col(SGC + k - 1)
-    TA, TB = col(T0 + 6), col(T0 + 7)
+    col = lambda k, p0=0, p1=128: P("cc", k, k + 1, 1, p0, p1)
+    BIT, IS, SG, CK, TK, JS, HC = 0, 7, 11, 18, 25, 32, 36
+    PB4, PB5, PB6, NB0, I3, I6, OF7, OP7, HD7, IN7, NS7 = range(40, 51)
+    bit = lambda b: col(BIT + b)
+    sg = lambda b: col(SG + b)
 
-    for q in range(8):
-        dma("y", "dp", T.pin[16 * q:16 * q + 16, :], T.p[:, :], P("pin", 0, 24, 1, 16 * q, 16 * q + 16)[1], [])
+    for gr in range(8):
+        s = 4 * (gr % 2) + (gr & 2) + gr // 4
+        dma("y", "dp", T.pin[16 * gr:16 * gr + 16, :], T.p[:, 3 * s:3 * s + 3], P("pin", 0, 3, 1, 16 * gr, 16 * gr + 16)[1], [])
     dma("s", "dxin", T.xt[:, :], T.x[:, :], P("xt", 0, 1536)[1], [])
     dma("y", "du", T.ut[:, :], T.u[:, :], P("ut", 0, 512)[1], [])
+    dma("y", "dwc", T.wq[:, :].bitcast(dt.uint8), T.wc[:, :], P("wq", 0, 512)[1], [])
+    dma("y", "dws", T.wsc[:, :], T.ws[:, :], P("wsc", 0, 512)[1], [])
+    dma("y", "dv", T.vt[:, :], T.v[:, :], P("vt", 0, 512)[1], [])
     io(P("pi", 0, 1), [[0, 1]], 0, 1, False)
     io(P("uli", 0, 64), [[16, 8], [0, 8]], small=False)
-    io(P("fi", 0, 48), [[0, 3], [1, 16]])
-    io(P("pst", 0, 3), [[1, 3]], 0, 3)
+    io(P("x3", 0, 3), [[1, 3]])
+    io(P("fi", 0, 96), [[0, 6], [1, 16]])
     io(P("ioc", 0, 384), [[1, 384]], -192)
-    io(P("posr", 0, 48), [[1, 48]])
-    io(P("x8", 0, 8), [[1, 8]])
-    io(P("a24", 0, 24), [[32, 24]], small=False)
-    ON, o6, o7 = P("on", 0, 128), P("idt", 128, 256), P("idt", 256, 384)
+    for k in (2, 3, 4):
+        io(P("f%d" % k, 0, 48), [[0, 3], [1, 32 >> k], [0, 1 << (k - 1)]])
+    io(P("posr", 0, 96), [[1, 96]])
+    ON = P("on", 0, 128)
     fill(ON, 1.0)
     fill(P("ea", 0, 2048), 0.0)
     for b in range(4):
         sel(P("ea", 512 * b + b, 512 * b + 512, 4), ON, [[-1, 128]], A.is_equal, 0, 1)
-    sel(P("idt", 0, 128), ON, [[-32, 4], [16, 2], [-1, 16]], A.is_equal, -16, 1)
-    sel(o6, ON, [[-64, 2], [0, 4], [-4, 16]], A.is_ge, 0, 1)
-    sel(o7, ON, [[0, 8], [-8, 16]], A.is_ge, 0, 1)
-    sel(o6, o6, [[64, 2], [0, 4], [4, 16]], A.is_ge, 3, -1)
-    sel(o7, o7, [[0, 8], [8, 16]], A.is_ge, 7, -1)
-    for n, w, c in (("eb", 2560, 0), ("tx5", 512, 0), ("r6", 576, 0), ("tx6", 512, 0), ("m6", 291, 1), ("tx7", 512, 0), ("m7", 579, 1), ("w1", 768, 0), ("w2", 768, 0)):
-        io(P(n, 0, w), [[0, w]], c)
-    io(P("km", 0, 384), [[0, 2], [1, 192]])
+    for n, w in (("m6", 291), ("m7", 579)):
+        io(P(n, 0, w), [[0, w]], 1)
+    io(P("w1", 0, 768), [[0, 768]])
+    for h in range(2):
+        io(P("kma", 384 * h, 384 * h + 384), [[16, 12], [0, 2], [1, 16]])
+        io(P("st", 12 * h, 12 * h + 12), [[96, 2], [192, 2], [16, 3]], 48 * h)
+    io(P("w2", 0, 768), [[0, 768]])
     for b in range(7):
         ts(P("bi", b, b + 1), P("pi", 0, 1), b, 1, A.logical_shift_right, A.bitwise_and)
-    for k, m in ((0, 15), (1, 3), (2, 7), (3, 31)):
-        ts(P("pw", k, k + 1), P("pi", 0, 1), m, None, A.bitwise_and)
-    ts(P("pw", 8, 9), P("pi", 0, 1), 4, None, A.logical_shift_right)
-    for k in (1, 2, 3):
-        ts(P("pw", 4 + k, 5 + k), P("pw", 0, 1), k, None, A.logical_shift_right)
-    tc(P("cc", BFC, BFC + 7), P("bi", 0, 7))
-    tc(P("cc", PM, PM + 4), P("pw", 0, 4))
+    for k in range(4):
+        ts(P("bi", IS + k, IS + k + 1), P("pi", 0, 1), k, 15 >> k, A.logical_shift_right, A.bitwise_and)
     tc(P("ul", 0, 64), P("uli", 0, 64))
-    tc(P("cc", T0, T0 + 4), P("pw", 5, 9))
-    ts(P("cc", SGC, SGC + 7), P("cc", BFC, BFC + 7), -2.0, 1.0, A.mult, A.add)
-
-    def base_out(e="odf", sem="dbo", to="bof", p=112):
-        dma("y", sem, T[to][:, :], T[e][p:p + 1, :], P(to, 0, 3)[1], P(e, 0, 384)[1])
-
-    tc(P("lp0", 0, 24), P("pin", 0, 24))
-    act(P("odf", 0, 384), IND(P("ioc", 0, 384), P("lp0", 0, 24)), F_.Identity, bias=192.0)
-    base_out()
-    ts(P("cc", S29, S29 + 4), P("cc", SGC, SGC + 4), BIG, None, A.mult)
-    tt(P("cc", SSC, SSC + 6), P("cc", SGC, SGC + 6), P("cc", SGC + 1, SGC + 7), A.mult)
-    uw, uo, ul = P("uc", 0, 128), P("uqc", 0, 1024), P("ul", 0, 64)
+    tc(P("cc", 0, 11), P("bi", 0, 11))
+    fill(P("m1", 0, 21), 1.0)
+    fill(P("m4", 0, 147), 1.0)
+    ts(P("cc", SG, SG + 7), P("cc", BIT, BIT + 7), -2.0, 1.0, A.mult, A.add)
+    ts(P("cc", CK, CK + 7), P("cc", BIT, BIT + 7), UP, None, A.mult)
+    ts(P("cc", TK, TK + 7), P("cc", BIT, BIT + 7), TINY, None, A.mult)
+    ts(col(I3), col(IS), 3.0, None, A.mult)
+    ts(col(I6), col(IS + 1), 6.0, None, A.mult)
+    ts(col(NB0), bit(0), -1.0, 1.0, A.mult, A.add)
+    ts(col(PB6), bit(4), 192.0, -7.5, A.mult, A.add)
+    ts(P("om", 0, 96), P("fi", 0, 96), col(IS), None, A.is_equal)
+    ts(P("aa", 0, 96), P("fi", 0, 96), col(IS), None, A.not_equal)
+    tt(P("cc", JS, JS + 4), P("cc", IS, IS + 4), P("cc", SG, SG + 4), A.add)
+    ts(P("lpl", 0, 3), P("x3", 0, 3), col(I3), None, A.add)
+    ts(col(PB5), bit(5), 96.0, col(PB6), A.mult, A.add)
+    fill(P("m1", 0, 21, 7), 0.0)
+    fill(P("m4", 0, 147, 49), 0.0)
+    ts(P("cm1", 0, 21, 7), P("x3", 0, 3), col(I6), None, A.add)
+    tc(P("l0", 0, 3), P("lpl", 0, 3))
+    for t in range(3):
+        ts(P("l0", 3 + t, 4 + t), P("lpl", t, t + 1), sg(0), None, A.subtract if t == 1 else A.add)
+    ts(col(PB4), bit(6), 48.0, col(PB5), A.mult, A.add)
+    uw, ul = P("uc", 0, 128), P("ul", 0, 64)
     quant(uw, P("us", 0, 128), P("ut", 0, 512))
-    tc(P("odx", 0, 384, 2), P("odf", 1, 384, 2))
-    tc(P("odx", 1, 384, 2), P("odf", 0, 384, 2))
-    base_out("odx", "dbx", "bxf")
-    dma("y", "dwc", T.wq[:, :].bitcast(dt.uint8), T.wc[:, :], P("wq", 0, 512)[1], [])
-    dma("y", "dws", T.wsc[:, :], T.ws[:, :], P("wsc", 0, 512)[1], [])
-    dma("y", "dv", T.vt[:, :], T.v[:, :], P("vt", 0, 512)[1], [])
-    act(P("uqs", 0, 1024), IND(P("us", 0, 128), ul))
-    op("v", lambda: g.vector.tensor_copy(uo[0].bitcast(dt.uint32), uw[0].bitcast(dt.uint32).indirect(ul[0])), uo[1], uw[1] + ul[1])
+    tc(P("l3", 0, 3), P("pin", 0, 3))
+    act(P("row0", 0, 48), IND(P("ioc", 0, 384), P("l3", 0, 3)), F_.Identity, bias=192.0)
+
+    def spread_u(a, b):
+        uo, l = P("uqc", 128 * a, 128 * b), P("ul", 8 * a, 8 * b)
+        act(P("uqs", 128 * a, 128 * b), IND(P("us", 0, 128), l))
+        op("v", lambda: g.vector.tensor_copy(uo[0].bitcast(dt.uint32), uw[0].bitcast(dt.uint32).indirect(l[0])), uo[1], uw[1] + l[1])
+
+    spread_u(0, 2)
+    for h in (0, 48):
+        for t in range(3):
+            ts(P("om0", h + 16 * t, h + 16 * t + 16), P("om", 16 * t, 16 * t + 16), sg(0), 1.0 if t != 1 else -1.0, A.mult, A.mult)
+    tt(P("b0", 0, 96), IND(P("row0", 0, 48), P("l0", 0, 6)), P("om", 0, 96), A.mult)
+    ts(P("mn1", 0, 48), P("fi", 0, 48), col(IS), -BIG, A.not_equal, A.mult)
+    ts(P("mo1", 0, 48), P("fi", 0, 48), col(JS), -BIG, A.not_equal, A.mult)
+    scan(P("o0", 0, 96), P("aa", 0, 96), P("b0", 0, 96), 0.0, A.mult, A.add)
+    spread_u(2, 8)
+    tc(P("bof", 0, 3), P("o0", 15, 48, 16))
+    tc(P("bxf", 0, 3), P("o0", 63, 96, 16))
+    for k in (2, 3, 4):
+        f = P("f%d" % k, 0, 48)
+        ts(P("mn%d" % k, 0, 48), f, col(IS + k - 1), -BIG, A.not_equal, A.mult)
+        ts(P("mo%d" % k, 0, 48), f, col(JS + k - 1), BIG, A.subtract, A.mult)
+        ts(col(HC + k - 2), col(JS + k - 1), bit(k - 1), -float(W[k]), A.add, A.mult)
 
     def scores_in():
         quant(P("xc", 0, 192), P("xs", 0, 192), P("xt", 0, 768))
@@ -227,240 +266,220 @@ def rank_program(g, core, T, topo):
     def fmm(b, bank):
         mm(PS(bank, 0, 384), P("eac", 128 * b, 128 * b + 128), P("eas", 128 * b, 128 * b + 128), P("xc", 0, 384), P("xs", 0, 384))
 
-    def xmm(k, bank, start=True, stop=True):
-        mm(PS(bank, 0, 128), P("ebc", 128 * k, 128 * k + 128), P("ebs", 128 * k, 128 * k + 128), P("tc", 0, 128), P("tsc", 0, 128), start, stop)
-
-    own = P("tmp", 0, 48)
-    ts(own, P("fi", 0, 48), col(PM), None, A.is_equal)
-    ts(TB, col(T0 + 3), -48.0, None, A.mult)
-    ts(TA, col(PM), sg(1), None, A.add)
-    fill(P("m4", 0, 147), 1.0)
-    for h in (0, 48):
-        ts(P("aa", h, h + 48), own, -1.0, 1.0, A.mult, A.add)
-        for t in range(3):
-            ts(P("om0", h + 16 * t, h + 16 * t + 16), P("tmp", 16 * t, 16 * t + 16), sg(1), 1.0 if t != 1 else -1.0, A.mult, A.mult)
-    ts(P("pg", 0, 3), P("pst", 0, 3), TB, None, A.add)
-    ts(P("tmp", 48, 96), P("fi", 0, 48), TA, None, A.is_equal)
-    ts(P("ng", 0, 48), P("aa", 0, 48), -BIG, None, A.mult)
-    fill(P("m4", 0, 147, 49), 0.0)
-    ts(P("psl", 0, 3), P("pg", 0, 3), sg(1), None, A.mult)
-    ts(P("bm", 0, 48), P("tmp", 48, 96), 0.0, col(S29), A.is_equal, A.mult)
     scores_in()
     mode["defer"] = True
-    fill(P("r2", 0, 192), 0.0)
-    for k in (2, 3, 4, 5, 6, 7):
-        ts(P("om", 48 * k, 48 * k + 48), own, sg(k), None, A.mult)
-    for k in (2, 3, 4):
-        ts(TA, col(T0 + k - 2), sg(k), float(W[k]), A.add, A.mult)
-        ts(TB, TA, float(W[k]), None, A.add)
-        ts(P("tmp", 48, 96), P("posr", 0, 48), TA, None, A.is_ge)
-        ts(P("tmp", 96, 144), P("posr", 0, 48), TB, None, A.is_ge)
-        fill(P("r%d" % k, 0, 48, W[k]), -BIG)
-        tt(P("tmp", 48, 96), P("tmp", 48, 96), P("tmp", 96, 144), A.subtract)
-        ts(P("bm", 48 * k - 48, 48 * k), P("tmp", 48, 96), 0.0, col(S29 + k - 1), A.is_equal, A.mult)
+    ts(P("pg", 0, 3), P("lpl", 0, 3), col(PB4), None, A.add)
     quant(P("eac", 0, 512), P("eas", 0, 512), P("ea", 0, 2048))
-    for n in (5, 6, 7):
-        fill(P("r%d" % n, 0, 48 if n < 6 else 2 * W[n], W[n]), -BIG)
-    ts(col(Q96), col(T0 + 3), 96.0, None, A.mult)
-    ts(col(O16), bit(4), 16.0, None, A.mult)
-    ts(TA, bit(4), 48.0, sg(6), A.mult, A.mult)
-    ts(TB, bit(5), 111.0, -103.5, A.mult, A.add)
-    ts(col(K6L), TA, TB, None, A.add)
-    ts(col(K5O), bit(4), 48.0, None, A.mult)
-    ts(TA, sg(4), sg(6), -48.0, A.mult, A.mult)
-    ts(TB, bit(2), 48.0, 48.0, A.mult, A.add)
-    ts(col(A6), TA, TB, None, A.add)
-    ts(P("mx4", 0, 4), P("x8", 0, 4), col(PM3), None, A.is_equal)
-    ts(P("mx8", 0, 8), P("x8", 0, 8), col(PM7), None, A.is_equal)
-    for k, (src, a, b, wt) in enumerate(((0, 0, 128, 1.0), (128, 0, 128, 1.0), (256, 0, 128, 1.0), (256, 96, 112, 2.0), (256, 112, 128, 2.0))):
-        for d in range(2):
-            ts(P("eb", 512 * k + 4 * a + d, 512 * k + 4 * b, 4), P("idt", src + a, src + b), wt if d == 0 else 1.0, None, A.mult)
-    quant(P("ebc", 0, 512), P("ebs", 0, 512), P("eb", 0, 2048))
-    quant(P("ebc", 512, 640), P("ebs", 512, 640), P("eb", 2048, 2560))
     for n, w in (("m6", 96), ("m7", 192)):
         fill(P(n, 0, 3 * w + 3, w + 1), 0.0)
-    ts(P("mx8s", 0, 8), P("mx8", 0, 8), sg(6), None, A.mult)
-    ts(TA, sg(7), 103.5, None, A.mult)
-    ts(TB, bit(6), 192.0, -192.0, A.mult, A.add)
-    ts(col(K7L), TA, TB, None, A.add)
-    ts(TA, sg(4), sg(7), -96.0, A.mult, A.mult)
-    ts(col(A7), TA, 199.5, None, A.add)
-    ts(TA, bit(3), 384.0, 199.5, A.mult, A.add)
-    ts(TB, bit(3), -384.0, 208.0, A.mult, A.add)
-    ts(col(AF), TB, bit(4), TA, A.mult, A.add)
-    tc(P("a24f", 0, 24), P("a24", 0, 24))
-    tt(col(PMX), col(PM31), sg(1), A.add)
-    ts(P("stl", 0, 24), P("a24f", 0, 24), col(PM31), None, A.add)
-    ts(P("stl", 24, 48), P("a24f", 0, 24), col(PMX), None, A.add)
+    fill(P("sab", 0, 224), BIG)
+    fill(P("sab", 224, 448), -BIG)
+    ts(P("omn", 0, 48), P("om", 0, 48), -1.0, None, A.mult)
+    ts(col(OF7), bit(4), 192.0, 32.0, A.mult, A.add)
+    ts(col(OP7), bit(4), -32.0, 32.0, A.mult, A.add)
+    ts(col(HD7), bit(4), 192.0, -192.0, A.mult, A.add)
+    ts(col(IN7), sg(4), BIG, None, A.mult)
+    ts(col(NS7), sg(4), -1.0, None, A.mult)
+    ts(P("stl", 0, 24), P("st", 0, 24), col(IS), None, A.add)
+    ts(P("stl", 24, 48), P("st", 0, 24), col(JS), None, A.add)
     mode["defer"], mode["mix"] = False, True
 
-    def flush(n):
-        while len(late) > n:
-            op(*late.pop(0))
-
     SGR = lambda k: P("sgb", 384 * k, 384 * k + 384)
-    EX, FIN, BF3 = 4, 5, 6
+    BANK = {1: 2, 2: 3, 3: 4, 4: 5, 5: 6, 6: 7, 7: 0}
     nxt = T.cores[(rank + 1) % len(T.cores)]
     rid, pid = topo.addr(nxt)[0], topo.addr(nxt)[1]
     eng = topo.engines(core, nxt)
     half = len(eng) // 2
     mask_c, mask_s = sum(1 << e for e in eng[:half]), sum(1 << e for e in eng[half:])
     ends = lambda cn, w: P(cn, w, 3 * w + 3, w + 1)
+    end = lambda cn, w, t, p0=0, p1=128: P(cn, (w + 1) * t + w, (w + 1) * t + w + 1, 1, p0, p1)
     heads = lambda cn, w: P(cn, 0, 3 * w + 3, w + 1)
+    lp = P("lbp", 0, 3)
+    row = lambda n, k: P("%s%d" % (n, k), 0, 48 if k < 6 else 96)
 
-    def keys(so, key, n, res, sc, lst):
-        tc(IND(P(so, 0, n), lst), P(sc, 0, n))
-        scan(P(key, 0, n), P(res, 0, n), P(so, 0, n), -BIG, A.add, A.max)
+    def scores_out(k):
+        act(SGR(k), PS(BANK[k], 0, 384))
 
-    def halves(so, key, res, w):
-        for h in (0, w):
-            scan(P(key, h, h + w), P(res, h, h + w), P(so, h, h + w), -BIG, A.add, A.max)
+    def masked(k):
+        tt(row("so", k), IND(SGR(k), lp), P("mo%d" % k, 0, 48), A.add)
+        tt(P("sm", 0, 48) if k > 1 else row("sn", k), IND(SGR(k), lp), P("mn%d" % k, 0, 48), A.add)
 
-    def owned(k, src):
-        tt(P("bb", 0, 48), src, P("om", 48 * k, 48 * k + 48), A.mult)
-        if k in (2, 3, 4):
-            tt(P("mk", 0, 48), P("key", 0, 48), P("bm", 48 * k - 48, 48 * k), A.add)
-        scan(P("own", 0, 48), P("aa", 0, 48), P("bb", 0, 48), 0.0, A.mult, A.add)
+    def step_up(k):
+        n = 48 if k < 6 else 96
+        act(row("ab", k), IND(SGR(k), lp if k < 6 else P("lb7", 0, 6)), F_.Abs, bias=col(TK + SIDE[k]), scale=col(CK + SIDE[k]))
 
-    def count(k, cmn, cn, mn, w, other, mine=("own", 15, 16), parts=1):
+    def stepped(k):
+        tt(row("sn", k), P("sm", 0, 48) if k < 5 else row("so", k), row("ab", k), A.add)
+
+    def after(k, cn, w, cmn, wn, bias):
+        if bias is None:
+            act(heads(cmn, wn), ends(cn, w))
+        else:
+            act(heads(cmn, wn), ends(cn, w), F_.Identity, bias=bias)
+        if k < 6:
+            act(P("pg", 3 * k, 3 * k + 3), ends(cn, w), F_.Identity, bias=col(PB4 if k < 5 else PB5))
+
+    def merge(k, cn, w, gaps):
+        n, (cmn, co, mn) = (48, ("cm", "c4", "m4")) if k < 6 else (96, ("cm6", "c6", "m6"))
+        lst = P("pl", 0, n // 16)
+        tc(P("pl", 0, 3), ends(cn, w))
+        if k == 6:
+            for q in (0, 2):
+                tc(QD("pl", 3, 6, 1, q, 2), QD(cn, w, 3 * w + 3, w + 1, 2 - q, 2))
+        reset = lambda t: ts(P("rr", 96 * t, 96 * t + n), P("posr", 0, n), end(cn, w, t), -BIG, A.is_equal, A.mult)
+        for t in range(3 if k < 6 else 2):
+            reset(t)
+        tc(IND(P("wo", 0, n), lst), row("so", k))
+        tc(IND(P("wp", 0, n), lst), row("sn", k))
+        if k == 6:
+            reset(2)
+            gaps[3]()
+        m, x = {5: (2, 2), 6: (1, 1)}.get(k, (4, 0))
+        for q in range(0, 4, m):
+            wo = QD("wo", 0, n, 1, q, m)
+            scan(QD("key", 0, n, 1, q ^ x, m), wo, wo, -9 * BIG, A.max, A.max)
         for t in range(3):
-            o = mine[1] + mine[2] * t
-            ts(P(cmn, (w + 1) * t + 1, (w + 1) * t + w + 1), other, sg(k), P(mine[0], o, o + 1), A.mult, A.is_lt)
+            scan(P("own", 96 * t, 96 * t + n), REV("rr", 96 * t, 96 * t + n), REV("wp", 0, n), -BIG, A.add, A.max)
+        gaps[0]()
+        for t in range(3):
+            ts(P(cmn, (n + 1) * t + 1, (n + 1) * t + n + 1), P("key", 0, n), P("own", 96 * t + n - 1, 96 * t + n), None, A.is_lt)
+        gaps[1]()
+        parts = 1 if k < 6 else 3
+        count(cmn, co, mn, n, parts)
+        gaps[2]()
+
+    def count(cmn, cn, mn, w, parts):
         n = (3 * w + 3) // parts
         for a in range(0, 3 * w + 3, n):
             scan(P(cn, a, a + n), P(mn, a, a + n), P(cmn, a, a + n), 0.0, A.mult, A.add)
 
-    def lay(n, xs, tile, mask):
-        for t in range(3):
-            ts(P("xm", t, 3 * n, 3), P(mask, 0, n), xs[t], None, A.mult)
-        ts(P(tile, 0, 12 * n, 4), P("xm", 0, 3 * n), MAG, MAG, A.add, A.subtract)
-        tt(P(tile, 1, 12 * n, 4), P("xm", 0, 3 * n), P(tile, 0, 12 * n, 4), A.subtract)
-        quant(P("tc", 0, 128), P("tsc", 0, 128), P(tile, 0, 512))
+    def address(a, b):
+        ts(P("hm", a, b), P("pg", a, b), MAG, MAG, A.add, A.subtract)
+        return lambda: tt(P("ad", a, b), P("hm", a, b), P("pg", a, b), A.add)
 
-    pl, plo = P("pl", 0, 3), P("plo", 0, 3)
+    nothing = lambda: None
     for r in range(NR):
         last = r == NR - 1
         if r:
             scores_in()
         smm(0, 0, 0, 192)
         smm(0, 1, 192, 384)
-        smm(1, 2)
-        smm(2, 3)
+        for k in range(1, 7):
+            smm(k, BANK[k])
         tc(P("lbox", 0, 3), P("bof", 0, 3))
         tc(P("lbox", 3, 6), P("bxf", 0, 3))
         tt(P("bdf", 0, 3), P("bxf", 0, 3), P("bof", 0, 3), A.subtract)
         act(P("sgb", 0, 192), PS(0, 0, 192))
         tc(P("sgb", 192, 384), PS(1, 0, 192))
-        smm(3, 0)
-        smm(4, 1)
+        smm(7, 0)
+        scores_out(1)
+        scores_out(2)
         tt(P("b0", 0, 96), IND(SGR(0), P("lbox", 0, 6)), P("om0", 0, 96), A.mult)
-        scan(P("own", 0, 96), P("aa", 0, 96), P("b0", 0, 96), 0.0, A.mult, A.add)
-        tt(P("dd", 0, 3), P("own", 15, 48, 16), P("own", 63, 96, 16), A.is_gt)
+        scan(P("o0", 0, 96), P("aa", 0, 96), P("b0", 0, 96), 0.0, A.mult, A.add)
+        tt(P("dd", 0, 3), P("o0", 15, 48, 16), P("o0", 63, 96, 16), A.is_gt)
         for t in range(3):
             ts(P("lbp", t, t + 1), P("dd", t, t + 1), P("bdf", t, t + 1), P("bof", t, t + 1), A.mult, A.add)
-        lp = P("lbp", 0, 3)
-        dma("y", "dbr", T.brow[0:1, 0:384], T.lbp[:, :], P("brow", 0, 384, 1, 0, 1)[1], lp[1])
-        for name, n, src in (("lb5", 3, lambda q: (16 * (q + 1 - 2 * (q % 2)), 16)), ("lb6", 12, lambda q: (64 * (q // 4), 64))):
-            for q in range(8):
-                a, m = src(q)
-                dma("y", "db" + name[2], T[name][16 * q:16 * q + 16, 0:n], T.lbp[a:a + m, 0:3], P(name, 0, n, 1, 16 * q, 16 * q + 16)[1], P("lbp", 0, 3, 1, a, a + m)[1])
-        for q in range(8):
-            dma("y", "db7", T.lb7[16 * q:16 * q + 16, 0:24], T.brow[0:1, 0:384], P("lb7", 0, 24, 1, 16 * q, 16 * q + 16)[1], P("brow", 0, 384, 1, 0, 1)[1])
-        act(SGR(1), PS(2, 0, 384))
-        act(heads("cm", 48), P("psl", 0, 3))
-        smm(5, 2)
-        act(SGR(2), PS(3, 0, 384))
-        act(P("sc2", 0, 48), IND(SGR(2), lp))
-        smm(6, 3)
-        s1, b1 = P("sc1", 0, 48), P("b1", 0, 48)
-        tt(s1, IND(SGR(1), lp), P("bm", 0, 48), A.add)
-        tt(b1, IND(SGR(1), lp), P("ng", 0, 48), A.add)
-        tt(P("sc1", 16, 32), P("sc1", 16, 32), P("sc1", 0, 16), A.max)
-        scan(P("own", 0, 48), b1, b1, -BIG, A.max, A.max)
-        tt(P("sc1", 32, 48), P("sc1", 32, 48), P("sc1", 16, 32), A.max)
-        ts(P("os", 0, 3), P("own", 15, 48, 16), sg(1), None, A.mult)
-        count(1, "cm", "c4", "m4", 48, s1, ("os", 0, 1))
-        for k in (2, 3, 4):
-            ts(pl, ends("c4", 48), sg(k - 1), None, A.mult)
-            act(heads("cm", 48), ends("c4", 48), scale=col(SSC + k - 2))
-            act(P("pg", 3 * k - 3, 3 * k), ends("c4", 48), scale=sg(k - 1))
-            keys("so", "key", 48, "r%d" % k, "sc%d" % k, pl)
-            owned(k, IND(P("key", 0, 48), pl))
-            count(k, "cm", "c4", "m4", 48, P("mk", 0, 48))
-            act(SGR(k + 1), PS(k - 2, 0, 384))
-            act(P("sc%d" % (k + 1), 0, 48), IND(SGR(k + 1), lp))
-            if k == 2:
-                smm(7, 0)
-            elif k == 3:
-                fmm(0, 1)
-            else:
-                act(P("sc5o", 0, 48), IND(SGR(5), P("lb5", 0, 3)))
-        flush(15)
-        ts(P("tx5", 0, 12, 4), ends("c4", 48), MAG, MAG, A.add, A.subtract)
-        tt(P("tx5", 1, 12, 4), ends("c4", 48), P("tx5", 0, 12, 4), A.subtract)
-        quant(P("tc", 0, 128), P("tsc", 0, 128), P("tx5", 0, 512))
-        xmm(0, EX)
+        masked(1)
+        tc(P("gs", 0, 12, 4), lp)
+        for n, o in (("so", 96), ("sn", 0)):
+            scan(P("own", o, o + 48), row(n, 1), row(n, 1), -BIG, A.max, A.max)
+        step_up(2)
+        scores_out(3)
+        step_up(3)
+        masked(2)
+        for t in range(3):
+            for o, c, m in ((1, A.is_lt, col(NB0)), (4, A.is_le, bit(0))):
+                ts(P("cm1", 7 * t + o, 7 * t + o + 3), P("own", 111, 144, 16), P("own", 16 * t + 15, 16 * t + 16), m, c, A.mult)
+        ts(P("hid", 0, 3), P("gs", 0, 12, 4), -7.5, MAG, A.add, A.add)
+        stepped(2)
+        count("cm1", "c1", "m1", 6, 1)
+        ts(P("hid", 0, 3), P("hid", 0, 3), MAG, None, A.subtract)
+        after(1, "c1", 6, "cm", 48, col(HC))
+        scores_out(4)
+        step_up(4)
+
+        def ids_out():
+            tt(P("gs", 12, 24, 4), P("hid", 0, 3), P("gs", 0, 12, 4), A.add)
+            for q in (0, 2):
+                act(QD("gs", 1, 24, 4, q, 2), QD("gs", 0, 24, 4, 2 - q, 2))
+            for rr in (2, 3):
+                for q in range(4):
+                    act(QD("gs", rr, 24, 4, q), QD("gs", 0, 24, 4, q ^ QX[rr]))
+
+        merge(2, "c1", 6, (nothing, lambda: masked(3), lambda: (ids_out(), stepped(3))))
+        after(2, "c4", 48, "cm", 48, col(HC + 1))
+        scores_out(5)
+        fmm(0, 1)
         fmm(1, 2)
-        act(heads("cm", 48), ends("c4", 48), scale=col(SSC + 3))
-        act(P("pg", 12, 15), ends("c4", 48), scale=sg(4))
-        act(SGR(6), PS(3, 0, 384))
         fmm(2, 3)
-        act(P("sc6", 0, 192), IND(SGR(6), P("lb6", 0, 12)))
+        fmm(3, 4)
+        merge(3, "c4", 48, (nothing, lambda: masked(4), lambda: stepped(4)))
+        after(3, "c4", 48, "cm", 48, col(HC + 2))
+        act(row("so", 5), IND(SGR(5), lp))
+        step_up(5)
+        scores_out(6)
+        merge(4, "c4", 48, (nothing, lambda: [tc(P("lb7", 3 * rr, 3 * rr + 3), P("gs", rr, 12, 4)) for rr in range(4)], lambda: (stepped(5), tc(P("lbt", 0, 12), P("gs", 0, 12)))))
+        after(4, "c4", 48, "cm", 48, None)
+        act(row("so", 6), IND(SGR(6), P("lb7", 0, 6)))
+        step_up(6)
+        scores_out(7)
+        act(P("so7", 0, 192), IND(SGR(7), P("lb7", 0, 12)), scale=col(NS7))
+        merge(5, "c4", 48, (nothing, lambda: [ts(P("lida", 12 * h, 12 * h + 12), P("gs", 12, 24), 16.0 * h, None, A.add) for h in range(2)], lambda: stepped(6)))
+        after(5, "c4", 48, "cm6", 96, None)
+        act(P("bc", 0, 192), IND(P("ioc", 0, 384), P("lbt", 0, 12)))
         act(P("fb", 0, 384), PS(1, 0, 384))
-        ts(pl, ends("c4", 48), sg(4), None, A.mult)
-        keys("so", "key", 48, "r5", "sc5", pl)
-        ts(plo, PS(EX, 0, 3), sg(4), None, A.mult)
-        tt(P("bb", 0, 48), IND(P("key", 0, 48), pl), P("om", 240, 288), A.mult)
-        tc(IND(P("so5", 0, 48), plo), P("sc5o", 0, 48))
-        scan(P("own", 0, 48), P("aa", 0, 48), P("bb", 0, 48), 0.0, A.mult, A.add)
-        scan(P("key5", 0, 48), P("r5", 0, 48), P("so5", 0, 48), -BIG, A.add, A.max)
-        count(5, "cm", "c4", "m4", 48, P("key5", 0, 48))
-        flush(0)
-        lay(4, [P("c4", 49 * t + 48, 49 * t + 49) for t in range(3)], "tx6", "mx4")
-        xmm(1, EX)
-        fmm(3, 1)
-        act(heads("cm6", 96), ends("c4", 48), F_.Identity, bias=col(K6L), scale=col(SSC + 4))
-        act(P("pg", 15, 18), ends("c4", 48), scale=sg(5))
-        act(SGR(7), PS(0, 0, 384))
-        act(P("sc7", 0, 384), IND(SGR(7), P("lb7", 0, 24)))
-        act(P("fb", 384, 768), PS(2, 0, 384))
-        ts(pl, ends("c4", 48), sg(5), col(K5O), A.mult, A.add)
-        a = 3 if r else 0
-        hm, pg, ad = P("hm", a, 18), P("pg", a, 18), P("ad", a, 18)
-        ts(hm, pg, -7.5, MAG, A.add, A.add)
-        ts(P("l6", 0, 12), PS(EX, 0, 12), sg(3), col(A6), A.mult, A.add)
-        tc(IND(P("so6", 0, 192), P("l6", 0, 12)), P("sc6", 0, 192))
-        ts(hm, hm, MAG, col(Q96), A.subtract, A.add)
-        halves("so6", "key6", "r6", 96)
-        tt(P("bb", 0, 48), IND(P("key6", 0, 96), pl), P("om", 288, 336), A.mult)
-        tt(ad, hm, pg, A.add)
-        for gr in range(a // 3, 6):
-            dma("y", "dl", T.ldm[16 * gr:16 * gr + 16, 0:24], T.ad[:, 3 * gr:3 * gr + 3], P("ldm", 0, 24, 1, 16 * gr, 16 * gr + 16)[1], P("ad", 3 * gr, 3 * gr + 3)[1])
-        scan(P("own", 0, 48), P("aa", 0, 48), P("bb", 0, 48), 0.0, A.mult, A.add)
-        count(6, "cm6", "c6", "m6", 96, P("key6", 96, 192), parts=3)
-        lay(8, [P("c6", 97 * t + 96, 97 * t + 97) for t in range(3)], "tx7", "mx8s")
-        xmm(2, EX)
-        xmm(3, FIN, True, False)
-        act(heads("cm7", 192), ends("c6", 96), F_.Identity, bias=col(K7L), scale=col(SSC + 5))
-        act(P("fb", 768, 1152), PS(3, 0, 384))
-        act(P("bc", 0, 384), IND(P("ioc", 0, 384), P("lb7", 0, 24)))
-        act(P("fb", 1152, 1536), PS(1, 0, 384))
+        add = []
+
+        def lists_out():
+            add[0]()
+            for q in range(3):
+                for rr in range(4):
+                    act(QD("ldm", rr, 24, 4, q), QD("ad", 6 * q, 6 * q + 6, 1, q ^ QX[rr]))
+
+        def lists_in():
+            for h in range(2):
+                ts(QD("plu", 12 * h, 12 * h + 12, 1, 0, 3), QD("ldm", 12 * h, 12 * h + 12, 1, 0, 3), 7.5 + 16 * h, None, A.add)
+
+        merge(6, "c4", 48, (lists_out, nothing, lists_in, lambda: add.append(address(0, 18))))
+        after(6, "c6", 96, "cm7", 192, col(HD7))
+        for b in range(1, 4):
+            act(P("fb", 384 * b, 384 * b + 384), PS(b + 1, 0, 384))
+        ts(P("l7", 0, 3), ends("c6", 96), col(OF7), None, A.add)
+        for q in (0, 2):
+            a = 64 - 32 * q
+            ts(QD("l7", 3, 6, 1, q, 2), QD("c6", 96, 291, 97, 2 - q, 2), col(OF7, a, a + 64), None, A.add)
+        ts(P("pl7", 0, 3), ends("c6", 96), col(OP7), None, A.add)
+        ts(P("hm", 18, 21), ends("c6", 96), col(PB6), MAG, A.add, A.add)
+        for q in range(4):
+            tc(QD("l7", 6, 12, 1, q), QD("l7", 0, 6, 1, q ^ 1))
+        for t in range(3):
+            ts(P("ad", 18 + t, 19 + t), P("hm", 18 + t, 19 + t), MAG - 192.0, end("c6", 96, t), A.subtract, A.add)
+        tc(IND(P("sab", 0, 448), P("l7", 0, 12)), P("so7", 0, 192))
+        for rr in range(4):
+            q = 3 ^ QX[rr]
+            ts(QD("plu", rr, 12, 4, 3), QD("ad", 18, 21, 1, q), col(HD7, 32 * q, 32 * q + 32), None, A.add)
         for b in range(4):
             act(P("fh", 384 * b, 384 * b + 384), P("fb", 384 * b, 384 * b + 384), scale=0.5)
-        ts(pl, ends("c6", 96), sg(6), 103.5, A.mult, A.add)
-        ts(P("l7", 0, 24), PS(EX, 0, 24), col(A7), None, A.add)
-        tc(IND(P("so7", 0, 384), P("l7", 0, 24)), P("sc7", 0, 384))
-        halves("so7", "key7", "r7", 192)
-        owned(7, IND(P("key7", 0, 192), pl))
-        count(7, "cm7", "c7", "m7", 192, P("key7", 192, 384), parts=3)
-        x1 = [P("x1", t, t + 1) for t in range(3)]
+        scan(P("key7", 0, 224), P("sab", 0, 224), P("sab", 224, 448), col(IN7), A.min, A.max)
+        piece = lambda j: tc(IND(P("w1", 0, 768), P("plu", 4 * j, 4 * j + 4)), P("bc", 64 * j, 64 * j + 64))
+        piece(0)
+        tr(P("tk", 0, 224), P("key7", 0, 224))
+        tt(P("b0", 0, 48), IND(P("key7", 0, 224), P("pl7", 0, 3)), P("omn", 0, 48), A.mult)
+        tr(P("uk", 0, 192), P("tk", 16, 208))
+        scan(P("o0", 0, 48), P("aa", 0, 48), P("b0", 0, 48), 0.0, A.mult, A.add)
+        piece(1)
         for t in range(3):
-            ts(x1[t], P("c7", 193 * t + 192, 193 * t + 193), sg(7), -7.5, A.mult, A.add)
-        lay(8, x1, "tx7", "mx8")
-        xmm(4, FIN, False, True)
-        ts(P("plu", 0, 24, 1, 0, 96), P("ldm", 0, 24, 1, 0, 96), P("cc", O16, O16 + 1, 1, 0, 96), None, A.add)
-        ts(P("plu", 0, 24, 1, 96, 128), PS(FIN, 0, 24, 96, 128), P("cc", AF, AF + 1, 1, 96, 128), None, A.add)
-        tc(IND(P("w1", 0, 768), P("plu", 0, 24)), P("bc", 0, 384))
+            ts(P("cm7", 193 * t + 1, 193 * t + 193), P("uk", 0, 192), P("o0", 16 * t + 15, 16 * t + 16), sg(4), A.is_lt, A.mult)
+        count("cm7", "c7", "m7", 192, 3)
+        for t in range(3):
+            ts(P("h7", t, t + 1), end("c7", 192, t), 184.5, MAG, A.add, A.add)
+        for t in range(3):
+            ts(P("h7", 4 + t, 5 + t), P("h7", t, t + 1), MAG - 208.0, end("c7", 192, t), A.subtract, A.add)
+        piece(2)
+        for rr in range(4):
+            tc(QD("plu", 12 + rr, 24, 4, 3), QD("h7", 4, 7, 1, 3 ^ QX[rr]))
+        tc(IND(P("w1", 0, 768), P("plu", 12, 24)), P("bc", 0, 192))
+        act(P("val", 0, 384), IND(P("kma", 0, 768), P("plu", 0, 24)))
         tr(P("t1", 0, 768), P("w1", 0, 768))
         tt(P("ow", 0, 24), P("t1", 0, 768, 32), P("t1", 16, 768, 32), A.add)
         ts(P("lz", 0, 24), P("ow", 0, 24), 192.0, None, A.add)
@@ -474,24 +493,22 @@ def rank_program(g, core, T, topo):
         need("g", "sv", cnt["sv"])
         g.remote_dma(T["lc%d" % r][:, 0:H].bitcast(dt.uint8), zc[0].bitcast(dt.uint8), T.sem["ar%d" % r], T.sem.lsem, pid, rid, mask_c)
         g.remote_dma(T["ls%d" % r][:, 0:H], zs[0], T.sem["ar%d" % r], T.sem.lsem, pid, rid, mask_s)
-        act(P("odf", 0, 384), IND(P("w1", 0, 768), P("stl", 0, 24)), F_.Identity, bias=192.0)
+        tc(IND(P("w2", 0, 768), P("lida", 0, 24)), P("val", 0, 384))
+        act(P("odf", 0, 384), IND(P("ioc", 0, 384), P("lz", 0, 24)), F_.Identity, bias=192.0)
         if last:
             dma("y", "dout", T.od[:, :], T.odf[0:128:16, :], [], P("odf", 0, 384)[1])
         else:
-            base_out()
-            act(P("odx", 0, 384), IND(P("w1", 0, 768), P("stl", 24, 48)), F_.Identity, bias=192.0)
-            base_out("odx", "dbx", "bxf")
-        ts(P("h2", 0, 24), P("ow", 0, 24), 184.5, MAG, A.add, A.add)
-        ts(P("h2", 0, 24), P("h2", 0, 24), MAG - 192.0, col(O16), A.subtract, A.add)
-        tt(P("aj", 0, 24), P("h2", 0, 24), P("ow", 0, 24), A.add)
-        tc(P("lj", 0, 24), P("aj", 0, 24))
-        tc(IND(P("w2", 0, 768), P("lj", 0, 24)), P("km", 0, 384))
+            for n, a, to, sem in (("odp", 0, "bof", "dbo"), ("odx", 24, "bxf", "dbx")):
+                act(P(n, 0, 384), IND(P("odf", 0, 384), P("stl", a, a + 24)))
+                dma("y", sem, T[to][:, :], T[n][112:113, :], P(to, 0, 3)[1], P(n, 0, 384)[1])
         tr(P("t2", 0, 768), P("w2", 0, 768))
-        tt(P("iw", 0, 24), P("t2", 0, 768, 32), P("t2", 16, 768, 32), A.add)
-        tc(P("lr", 0, 24), P("iw", 0, 24))
-        fmm(3, BF3)
         if r == 0:
             quant(P("vc", 0, 128), P("vs", 0, 128), P("vt", 0, 512))
+        tt(P("iw", 0, 24), P("t2", 0, 768, 32), P("t2", 16, 768, 32), A.add)
+        tc(P("lr", 0, 24), P("iw", 0, 24))
+        if not last:
+            io(P("w1", 0, 768), [[0, 768]])
+            io(P("w2", 0, 768), [[0, 768]])
         pb = lambda b: P("psb", 192 * b, 192 * b + 192)
         for b in range(4):
             mm(PS(b, 0, H), P("wq", 128 * b, 128 * b + 128), P("wsc", 128 * b, 128 * b + 128), P("lc%d" % r, 0, H), P("ls%d" % r, 0, H), pre=[("ar%d" % r, 2 * half)])
@@ -501,7 +518,7 @@ def rank_program(g, core, T, topo):
         act(P("g3", 0, 384), IND(pb(3), P("lr", 0, 24)))
         for b in range(3):
             tt(P("xt", b, 1536, 4), IND(pb(b), P("lr", 0, 24)), P("fb", 384 * b, 384 * b + 384), A.add)
-        tt(P("xt", 3, 1536, 4), P("g3", 0, 384), PS(BF3, 0, 384), A.add)
+        tt(P("xt", 3, 1536, 4), P("g3", 0, 384), PS(4, 0, 384), A.add)
     scores_in()
     for h in range(2):
         a, b = 192 * h, 192 * h + 192

@@ -10,18 +10,18 @@ QX = [0, 2, 1, 3]
 SCRATCH = {"ps": ("psum", [128, 4096], "float32")}
 ALIAS = {}
 for _d, _s in (
-    ("float32", "cc:64 bof:3 bxf:3 bdf:3 b0:96 o0:96 dd:3 pg:21 hm:21 ad:21 ldm:24 gs:24 hid:3 h7:8 ow:24 iw:24 odf:384 odp:384 odx:384 psb:768 g3:384 yb:384 sgb:3072 "
-                "rr:288 own:288 sab:448 key7:224 tk:224 uk:192 row0:48"),
-    ("bfloat16", "ioc:384 kma:768 on:128 m1:21 m4:147 m6:291 m7:579 ea:2048 ut:512 vt:512 xt:1536 fb:1536 fh:1536 cm1:21 c1:21 cm:147 c4:147 cm6:291 c6:291 cm7:579 c7:579 "
+    ("float32", "cc:64 bof:3 bxf:3 bdf:3 b0:96 o0:96 ob:96 dd:3 pg:21 hm:21 ad:21 ldm:24 gs:24 hid:3 h7:8 ow:24 iw:24 odf:384 odp:384 odx:384 psb:768 g3:384 yb:384 sgb:3072 "
+                "rr:288 own:288 sab:448 key7:224 tk:224 uk:192 row0:48 g1:96"),
+    ("bfloat16", "ioc:384 kma:768 on:128 m1:21 m4:147 m6:291 m7:579 ea:1032 ut:512 vt:512 xt:1536 fb:1536 fh:1536 cm1:21 c1:21 cm:147 c4:147 cm6:291 c6:291 cm7:579 c7:579 "
                  "bc:192 val:384 w1:768 t1:768 w2:768 t2:768 az:768 zt:768"),
     ("int32", "pi:1 bi:11 uli:64 pin:3"),
-    ("uint16", "ul:64 stl:48 l3:4 l0:6 lbox:6 lbp:4 lb7:12 lbt:12 lida:24 pl:6 pl7:4 l7:12 plu:24 lz:24 lr:24"),
+    ("uint16", "ul:64 stl:48 l3:4 l0:6 lbox:6 lbo:8 l1:4 lbp:4 lb7:12 lbt:12 lida:24 pl:6 pl7:4 l7:12 plu:24 lz:24 lr:24"),
     ("float8_e4m3fn_x4", "eac:512 uc:128 uqc:1024 vc:128 wq:512 xc:384 zc0:192 zc1:192 zc2:192 lc0:192 lc1:192 lc2:192"),
     ("uint8", "eas:512 us:128 uqs:1024 vs:128 wsc:512 xs:384 zs0:192 zs1:192 zs2:192 ls0:192 ls1:192 ls2:192"),
 ):
     for _w in _s.split():
         SCRATCH[_w.split(":")[0]] = ("sbuf", [128, int(_w.split(":")[1])], _d)
-for _b, _s in (("kc", "fi:96 posr:96 aa:96 om:96 om0:96 omn:48 f2:48 f3:48 f4:48 mn1:48 mn2:48 mn3:48 mn4:48 mo1:48 mo2:48 mo3:48 mo4:48 x3:8 lpl:8 st:24"),
+for _b, _s in (("kc", "fi:96 posr:96 aa:96 aa0:96 om:96 om0:96 omn:48 f2:48 f3:48 f4:48 mn1:48 mn2:48 mn3:48 mn4:48 mo1:48 mo2:48 mo3:48 mo4:48 x3:8 lpl:8 st:24"),
                ("sc", "so1:48 so2:48 so3:48 so4:48 so5:48 so6:96 so7:192 sn1:48 sn2:48 sn3:48 sn4:48 sn5:48 sn6:96 sm:48 ab2:48 ab3:48 ab4:48 ab5:48 ab6:96"),
                ("wn", "wo:96 wp:96 key:96")):
     _o = 0
@@ -29,7 +29,7 @@ for _b, _s in (("kc", "fi:96 posr:96 aa:96 om:96 om0:96 omn:48 f2:48 f3:48 f4:48
         ALIAS[_w.split(":")[0]] = (_b, _o)
         _o += int(_w.split(":")[1])
     SCRATCH[_b] = ("sbuf", [128, _o], "float32")
-SEMAPHORES = ["sv", "ss", "st", "sg", "ar0", "ar1", "ar2", "lsem", "dp", "dxin", "du", "dv", "dwc", "dws", "dbo", "dbx", "dout"]
+SEMAPHORES = ["sv", "ss", "st", "sg", "ar0", "ar1", "ar2", "lsem", "dp", "dx0", "dx1", "dx2", "du", "dv", "dwc", "dws", "dbo", "dbx", "dout"]
 
 
 def rank_program(g, core, T, topo):
@@ -72,6 +72,14 @@ def rank_program(g, core, T, topo):
                 if qs == own and (not hit(r, q) or not (wr or qw) or (e == "t" and wr)):
                     continue
                 todo[qs] = max(todo.get(qs, 0), qv)
+        if e == "v" and mode["mix"] and late and todo.get(own, 0) > max(cnt[own] - 2, known[e].get(own, 0)):
+            mode["mix"] = False
+            while late[0][0] != "v":
+                op(*late.pop(0))
+            op(*late.pop(0))
+            op(e, make, writes, reads, sem, pre)
+            mode["mix"] = True
+            return
         for a_, b_ in sorted(todo.items(), key=lambda z: z[0] in dmh) + list(pre):
             if known[e].get(a_, 0) < b_:
                 need(e, a_, cnt[a_] if a_ in dmh else b_)
@@ -94,10 +102,6 @@ def rank_program(g, core, T, topo):
                 if not (same or wr and r[3] == 1 and r[1] <= q[1] and q[2] <= r[2] and r[4] <= q[4] and q[5] <= r[5]):
                     keep.append(x)
             acc[r[0]] = keep + [(r, wr, s, cnt[s])]
-        if e == "v" and mode["mix"] and late:
-            mode["mix"] = False
-            op(*late.pop(0))
-            mode["mix"] = True
 
     def P(name, a, b, st=1, p0=0, p1=128):
         if name in ALIAS:
@@ -165,38 +169,50 @@ def rank_program(g, core, T, topo):
     def io(o, pat, base=0, cm=0, small=True):
         op("g", lambda: g.iota(o[0], pat, base, cm, allow_small_or_imprecise_dtypes=True) if small else g.iota(o[0], pat, base, cm), o[1], [])
 
-    def sel(o, i, pat, cmp, base, cm):
-        op("g", lambda: g.affine_select(o[0], i[0], pat, cmp, 0.0, base, cm), o[1], i[1])
+    def sel(o, i, pat, cmp, base, cm, other=0.0):
+        op("g", lambda: g.affine_select(o[0], i[0], pat, cmp, other, base, cm), o[1], i[1])
+
+    def lin(o, i, scale, bias):
+        act(o, i, F_.Identity, bias=bias, scale=scale)
 
     col = lambda k, p0=0, p1=128: P("cc", k, k + 1, 1, p0, p1)
     BIT, IS, SG, CK, TK, JS, HC = 0, 7, 11, 18, 25, 32, 36
-    PB4, PB5, PB6, NB0, I3, I6, OF7, OP7, HD7, IN7, NS7 = range(40, 51)
+    PB4, PB5, PB6, NB0, I3, I6, OF7, OP7, HD7, IN7, NS7, NS0, J2 = range(40, 53)
     bit = lambda b: col(BIT + b)
     sg = lambda b: col(SG + b)
 
+    dma("y", "du", T.ut[:, :], T.u[:, :], P("ut", 0, 512)[1], [])
+    for h in range(3):
+        dma("s", "dx%d" % h, T.xt[:, 512 * h:512 * h + 512], T.x[:, 512 * h:512 * h + 512], P("xt", 512 * h, 512 * h + 512)[1], [])
     for gr in range(8):
         s = 4 * (gr % 2) + (gr & 2) + gr // 4
-        dma("y", "dp", T.pin[16 * gr:16 * gr + 16, :], T.p[:, 3 * s:3 * s + 3], P("pin", 0, 3, 1, 16 * gr, 16 * gr + 16)[1], [])
-    dma("s", "dxin", T.xt[:, :], T.x[:, :], P("xt", 0, 1536)[1], [])
-    dma("y", "du", T.ut[:, :], T.u[:, :], P("ut", 0, 512)[1], [])
+        dma("ys"[gr % 2], "dp", T.pin[16 * gr:16 * gr + 16, :], T.p[:, 3 * s:3 * s + 3], P("pin", 0, 3, 1, 16 * gr, 16 * gr + 16)[1], [])
+    need("y", "dx2", 16)
     dma("y", "dwc", T.wq[:, :].bitcast(dt.uint8), T.wc[:, :], P("wq", 0, 512)[1], [])
     dma("y", "dws", T.wsc[:, :], T.ws[:, :], P("wsc", 0, 512)[1], [])
     dma("y", "dv", T.vt[:, :], T.v[:, :], P("vt", 0, 512)[1], [])
     io(P("pi", 0, 1), [[0, 1]], 0, 1, False)
-    io(P("uli", 0, 64), [[16, 8], [0, 8]], small=False)
     io(P("x3", 0, 3), [[1, 3]])
     io(P("fi", 0, 96), [[0, 6], [1, 16]])
+    io(P("uli", 0, 64), [[16, 8], [0, 8]], small=False)
     io(P("ioc", 0, 384), [[1, 384]], -192)
-    for k in (2, 3, 4):
-        io(P("f%d" % k, 0, 48), [[0, 3], [1, 32 >> k], [0, 1 << (k - 1)]])
-    io(P("posr", 0, 96), [[1, 96]])
+    io(P("f2", 0, 48), [[0, 3], [1, 8], [0, 2]])
     ON = P("on", 0, 128)
     fill(ON, 1.0)
-    fill(P("ea", 0, 2048), 0.0)
-    for b in range(4):
-        sel(P("ea", 512 * b + b, 512 * b + 512, 4), ON, [[-1, 128]], A.is_equal, 0, 1)
-    for n, w in (("m6", 291), ("m7", 579)):
-        io(P(n, 0, w), [[0, w]], 1)
+    fill(P("ea", 0, 1032), 0.0)
+    for h in range(2):
+        sel(P("ea", 516 * h + 2 + h, 516 * h + 514, 4), ON, [[-1, 128]], A.is_equal, 0, 1)
+    io(P("posr", 0, 96), [[1, 96]])
+    for k in (3, 4):
+        io(P("f%d" % k, 0, 48), [[0, 3], [1, 32 >> k], [0, 1 << (k - 1)]])
+    for n, w in (("m6", 96), ("m7", 192)):
+        m = P(n, 0, 3 * w + 3)
+        io(m, [[0, 3 * w + 3]], 1)
+        sel(m, m, [[0, 3], [1, w + 1]], A.not_equal, 0, 0)
+    io(P("sab", 0, 448), [[0, 448]])
+    for h in range(2):
+        m = P("sab", 224 * h, 224 * h + 224)
+        sel(m, m, [[0, 224]], A.not_equal, 0, 0, -BIG if h else BIG)
     io(P("w1", 0, 768), [[0, 768]])
     for h in range(2):
         io(P("kma", 384 * h, 384 * h + 384), [[16, 12], [0, 2], [1, 16]])
@@ -206,59 +222,57 @@ def rank_program(g, core, T, topo):
         ts(P("bi", b, b + 1), P("pi", 0, 1), b, 1, A.logical_shift_right, A.bitwise_and)
     for k in range(4):
         ts(P("bi", IS + k, IS + k + 1), P("pi", 0, 1), k, 15 >> k, A.logical_shift_right, A.bitwise_and)
-    tc(P("ul", 0, 64), P("uli", 0, 64))
-    tc(P("cc", 0, 11), P("bi", 0, 11))
     fill(P("m1", 0, 21), 1.0)
     fill(P("m4", 0, 147), 1.0)
+    fill(P("aa0", 0, 96), 1.0)
+    tc(P("cc", 0, 11), P("bi", 0, 11))
+    tc(P("ul", 0, 64), P("uli", 0, 64))
+    fill(P("aa0", 0, 96, 32), 0.0)
+    fill(P("m1", 0, 21, 7), 0.0)
+    fill(P("m4", 0, 147, 49), 0.0)
     ts(P("cc", SG, SG + 7), P("cc", BIT, BIT + 7), -2.0, 1.0, A.mult, A.add)
-    ts(P("cc", CK, CK + 7), P("cc", BIT, BIT + 7), UP, None, A.mult)
-    ts(P("cc", TK, TK + 7), P("cc", BIT, BIT + 7), TINY, None, A.mult)
     ts(col(I3), col(IS), 3.0, None, A.mult)
-    ts(col(I6), col(IS + 1), 6.0, None, A.mult)
-    ts(col(NB0), bit(0), -1.0, 1.0, A.mult, A.add)
-    ts(col(PB6), bit(4), 192.0, -7.5, A.mult, A.add)
     ts(P("om", 0, 96), P("fi", 0, 96), col(IS), None, A.is_equal)
     ts(P("aa", 0, 96), P("fi", 0, 96), col(IS), None, A.not_equal)
     tt(P("cc", JS, JS + 4), P("cc", IS, IS + 4), P("cc", SG, SG + 4), A.add)
     ts(P("lpl", 0, 3), P("x3", 0, 3), col(I3), None, A.add)
-    ts(col(PB5), bit(5), 96.0, col(PB6), A.mult, A.add)
-    fill(P("m1", 0, 21, 7), 0.0)
-    fill(P("m4", 0, 147, 49), 0.0)
-    ts(P("cm1", 0, 21, 7), P("x3", 0, 3), col(I6), None, A.add)
+    ts(P("mn1", 0, 48), P("fi", 0, 48), col(IS), -BIG, A.not_equal, A.mult)
+    for o, i, sc_, bi_ in ((NS0, 0, 2.0, -1.0), (I6, IS + 1, 6.0, 0.0), (NB0, 0, -1.0, 1.0), (PB6, 4, 192.0, -7.5), (OF7, 4, 192.0, 32.0), (OP7, 4, -32.0, 32.0), (HD7, 4, 192.0, -192.0),
+                           (IN7, 4, -2 * BIG, BIG), (NS7, 4, 2.0, -1.0), (J2, IS, 2.0, 0.0), (J2 + 1, IS, 2.0, 32.0), (J2 + 2, IS, 2.0, 64.0)):
+        lin(col(o), col(i), sc_, bi_)
+    act(P("cc", CK, CK + 7), P("cc", BIT, BIT + 7), scale=UP)
+    act(P("cc", TK, TK + 7), P("cc", BIT, BIT + 7), scale=TINY)
+    lin(col(PB5), bit(5), 96.0, col(PB6))
+    lin(P("cm1", 0, 21, 7), P("x3", 0, 3), 1.0, col(I6))
+    for t in range(6):
+        act(P("om0", 16 * t, 16 * t + 16), P("om", 0, 16), scale=col(NS0) if t % 4 in (1, 2) else sg(0))
+    lin(col(PB4), bit(6), 48.0, col(PB5))
+    act(P("omn", 0, 48), P("om", 0, 48), scale=-1.0)
+    lin(P("pg", 0, 3), P("lpl", 0, 3), 1.0, col(PB4))
+    ts(P("mo1", 0, 48), P("fi", 0, 48), col(JS), -BIG, A.not_equal, A.mult)
     tc(P("l0", 0, 3), P("lpl", 0, 3))
     for t in range(3):
         ts(P("l0", 3 + t, 4 + t), P("lpl", t, t + 1), sg(0), None, A.subtract if t == 1 else A.add)
-    ts(col(PB4), bit(6), 48.0, col(PB5), A.mult, A.add)
+
+    def masks(k):
+        f = P("f%d" % k, 0, 48)
+        ts(P("mn%d" % k, 0, 48), f, col(IS + k - 1), -BIG, A.not_equal, A.mult)
+        ts(P("mo%d" % k, 0, 48), f, col(JS + k - 1), BIG, A.subtract, A.mult)
+        ts(col(HC + k - 2), col(JS + k - 1), bit(k - 1), -float(W[k]), A.add, A.mult)
+
+    masks(2)
     uw, ul = P("uc", 0, 128), P("ul", 0, 64)
     quant(uw, P("us", 0, 128), P("ut", 0, 512))
     tc(P("l3", 0, 3), P("pin", 0, 3))
-    act(P("row0", 0, 48), IND(P("ioc", 0, 384), P("l3", 0, 3)), F_.Identity, bias=192.0)
 
     def spread_u(a, b):
         uo, l = P("uqc", 128 * a, 128 * b), P("ul", 8 * a, 8 * b)
         act(P("uqs", 128 * a, 128 * b), IND(P("us", 0, 128), l))
         op("v", lambda: g.vector.tensor_copy(uo[0].bitcast(dt.uint32), uw[0].bitcast(dt.uint32).indirect(l[0])), uo[1], uw[1] + l[1])
 
-    spread_u(0, 2)
-    for h in (0, 48):
-        for t in range(3):
-            ts(P("om0", h + 16 * t, h + 16 * t + 16), P("om", 16 * t, 16 * t + 16), sg(0), 1.0 if t != 1 else -1.0, A.mult, A.mult)
-    tt(P("b0", 0, 96), IND(P("row0", 0, 48), P("l0", 0, 6)), P("om", 0, 96), A.mult)
-    ts(P("mn1", 0, 48), P("fi", 0, 48), col(IS), -BIG, A.not_equal, A.mult)
-    ts(P("mo1", 0, 48), P("fi", 0, 48), col(JS), -BIG, A.not_equal, A.mult)
-    scan(P("o0", 0, 96), P("aa", 0, 96), P("b0", 0, 96), 0.0, A.mult, A.add)
-    spread_u(2, 8)
-    tc(P("bof", 0, 3), P("o0", 15, 48, 16))
-    tc(P("bxf", 0, 3), P("o0", 63, 96, 16))
-    for k in (2, 3, 4):
-        f = P("f%d" % k, 0, 48)
-        ts(P("mn%d" % k, 0, 48), f, col(IS + k - 1), -BIG, A.not_equal, A.mult)
-        ts(P("mo%d" % k, 0, 48), f, col(JS + k - 1), BIG, A.subtract, A.mult)
-        ts(col(HC + k - 2), col(JS + k - 1), bit(k - 1), -float(W[k]), A.add, A.mult)
-
     def scores_in():
-        quant(P("xc", 0, 192), P("xs", 0, 192), P("xt", 0, 768))
-        quant(P("xc", 192, 384), P("xs", 192, 384), P("xt", 768, 1536))
+        for a in (0, 128, 256):
+            quant(P("xc", a, a + 128), P("xs", a, a + 128), P("xt", 4 * a, 4 * a + 512))
 
     def smm(gr, bank, a=0, b=384):
         mm(PS(bank, 0, b - a), P("uqc", 128 * gr, 128 * gr + 128), P("uqs", 128 * gr, 128 * gr + 128), P("xc", a, b), P("xs", a, b))
@@ -266,31 +280,39 @@ def rank_program(g, core, T, topo):
     def fmm(b, bank):
         mm(PS(bank, 0, 384), P("eac", 128 * b, 128 * b + 128), P("eas", 128 * b, 128 * b + 128), P("xc", 0, 384), P("xs", 0, 384))
 
+    act(P("row0", 0, 48), IND(P("ioc", 0, 384), P("l3", 0, 3)), F_.Identity, bias=192.0)
+    spread_u(0, 2)
+    tt(P("b0", 0, 96), IND(P("row0", 0, 48), P("l0", 0, 6)), P("om", 0, 96), A.mult)
+    spread_u(2, 3)
+    scan(P("ob", 0, 96), P("aa", 0, 96), P("b0", 0, 96), 0.0, A.mult, A.add)
     scores_in()
+    spread_u(3, 4)
     mode["defer"] = True
-    ts(P("pg", 0, 3), P("lpl", 0, 3), col(PB4), None, A.add)
-    quant(P("eac", 0, 512), P("eas", 0, 512), P("ea", 0, 2048))
-    for n, w in (("m6", 96), ("m7", 192)):
-        fill(P(n, 0, 3 * w + 3, w + 1), 0.0)
-    fill(P("sab", 0, 224), BIG)
-    fill(P("sab", 224, 448), -BIG)
-    ts(P("omn", 0, 48), P("om", 0, 48), -1.0, None, A.mult)
-    ts(col(OF7), bit(4), 192.0, 32.0, A.mult, A.add)
-    ts(col(OP7), bit(4), -32.0, 32.0, A.mult, A.add)
-    ts(col(HD7), bit(4), 192.0, -192.0, A.mult, A.add)
-    ts(col(IN7), sg(4), BIG, None, A.mult)
-    ts(col(NS7), sg(4), -1.0, None, A.mult)
-    ts(P("stl", 0, 24), P("st", 0, 24), col(IS), None, A.add)
-    ts(P("stl", 24, 48), P("st", 0, 24), col(JS), None, A.add)
+    mark = {}
+    for k in (4, 5, 6, 7):
+        spread_u(k, k + 1)
+        if k < 6:
+            masks(k - 1)
+        mark[k] = len(late)
+    for b in range(4):
+        a = 516 * (b % 2) + 2 - 2 * (b // 2)
+        quant(P("eac", 128 * b, 128 * b + 128), P("eas", 128 * b, 128 * b + 128), P("ea", a, a + 512))
+    mark[8] = len(late)
     mode["defer"], mode["mix"] = False, True
 
+    def flush(k):
+        mode["mix"] = False
+        while len(late) > mark[8] - mark[k]:
+            op(*late.pop(0))
+        mode["mix"] = True
+
     SGR = lambda k: P("sgb", 384 * k, 384 * k + 384)
-    BANK = {1: 2, 2: 3, 3: 4, 4: 5, 5: 6, 6: 7, 7: 0}
+    BANK = {2: 5, 3: 6, 4: 7, 5: 0, 6: 1, 7: 2}
     nxt = T.cores[(rank + 1) % len(T.cores)]
     rid, pid = topo.addr(nxt)[0], topo.addr(nxt)[1]
     eng = topo.engines(core, nxt)
-    half = len(eng) // 2
-    mask_c, mask_s = sum(1 << e for e in eng[:half]), sum(1 << e for e in eng[half:])
+    half = len(eng)
+    mask_c = mask_s = topo.mask(core, nxt)
     ends = lambda cn, w: P(cn, w, 3 * w + 3, w + 1)
     end = lambda cn, w, t, p0=0, p1=128: P(cn, (w + 1) * t + w, (w + 1) * t + w + 1, 1, p0, p1)
     heads = lambda cn, w: P(cn, 0, 3 * w + 3, w + 1)
@@ -298,11 +320,15 @@ def rank_program(g, core, T, topo):
     row = lambda n, k: P("%s%d" % (n, k), 0, 48 if k < 6 else 96)
 
     def scores_out(k):
+        if k > 3:
+            flush(k)
+            smm(k, BANK[k])
         act(SGR(k), PS(BANK[k], 0, 384))
 
     def masked(k):
-        tt(row("so", k), IND(SGR(k), lp), P("mo%d" % k, 0, 48), A.add)
-        tt(P("sm", 0, 48) if k > 1 else row("sn", k), IND(SGR(k), lp), P("mn%d" % k, 0, 48), A.add)
+        src = IND(SGR(k), lp) if k > 1 else IND(P("g1", 0, 96), P("l1", 0, 3))
+        tt(P("sm", 0, 48) if k > 1 else row("sn", k), src, P("mn%d" % k, 0, 48), A.add)
+        tt(row("so", k), src, P("mo%d" % k, 0, 48), A.add)
 
     def step_up(k):
         n = 48 if k < 6 else 96
@@ -330,6 +356,8 @@ def rank_program(g, core, T, topo):
         for t in range(3 if k < 6 else 2):
             reset(t)
         tc(IND(P("wo", 0, n), lst), row("so", k))
+        if k == 6:
+            gaps[4]()
         tc(IND(P("wp", 0, n), lst), row("sn", k))
         if k == 6:
             reset(2)
@@ -360,28 +388,37 @@ def rank_program(g, core, T, topo):
     nothing = lambda: None
     for r in range(NR):
         last = r == NR - 1
-        if r:
-            scores_in()
-        smm(0, 0, 0, 192)
-        smm(0, 1, 192, 384)
-        for k in range(1, 7):
+        def base(x, a, b):
+            if r:
+                return P("bxf" if x else "bof", a, b)
+            return P("ob", (48 if x else 0) + 16 * a + 15, (48 if x else 0) + 16 * b, 16 if b - a > 1 else 1)
+
+        for h in range(3):
+            smm(0, h, 128 * h, 128 * h + 128)
+        smm(1, 3, 0, 256)
+        smm(1, 4, 256, 384)
+        for k in range(2, 4):
             smm(k, BANK[k])
-        tc(P("lbox", 0, 3), P("bof", 0, 3))
-        tc(P("lbox", 3, 6), P("bxf", 0, 3))
-        tt(P("bdf", 0, 3), P("bxf", 0, 3), P("bof", 0, 3), A.subtract)
-        act(P("sgb", 0, 192), PS(0, 0, 192))
-        tc(P("sgb", 192, 384), PS(1, 0, 192))
-        smm(7, 0)
-        scores_out(1)
+        for n, a, st in (("lbox", 0, 2), ("lbox", 1, 2), ("lbo", 0, 1), ("lbo", 4, 1)):
+            tc(P(n, a, a + 3 * st - st + 1, st), base(a, 0, 3))
+        tt(P("bdf", 0, 3), base(1, 0, 3), base(0, 0, 3), A.subtract)
+        act(P("sgb", 0, 128), PS(0, 0, 128))
+        act(P("sgb", 128, 256), PS(1, 0, 128))
+        tc(P("sgb", 256, 384), PS(2, 0, 128))
+        act(P("sgb", 384, 640), PS(3, 0, 256))
+        act(P("sgb", 640, 768), PS(4, 0, 128))
+        for h in range(2):
+            act(P("g1", h, 96, 2), IND(SGR(1), P("lbo", 4 * h, 4 * h + 3)))
         scores_out(2)
         tt(P("b0", 0, 96), IND(SGR(0), P("lbox", 0, 6)), P("om0", 0, 96), A.mult)
-        scan(P("o0", 0, 96), P("aa", 0, 96), P("b0", 0, 96), 0.0, A.mult, A.add)
-        tt(P("dd", 0, 3), P("o0", 15, 48, 16), P("o0", 63, 96, 16), A.is_gt)
+        scan(P("o0", 0, 96), P("aa0", 0, 96), P("b0", 0, 96), 0.0, A.mult, A.add)
         for t in range(3):
-            ts(P("lbp", t, t + 1), P("dd", t, t + 1), P("bdf", t, t + 1), P("bof", t, t + 1), A.mult, A.add)
+            ts(P("l1", t, t + 1), P("o0", 32 * t + 31, 32 * t + 32), 0.0, col(J2 + t), A.is_gt, A.add)
+        ts(P("dd", 0, 3), P("o0", 31, 96, 32), 0.0, None, A.is_gt)
         masked(1)
-        tc(P("gs", 0, 12, 4), lp)
-        for n, o in (("so", 96), ("sn", 0)):
+        for t in range(3):
+            ts(P("lbp", t, t + 1), P("dd", t, t + 1), P("bdf", t, t + 1), base(0, t, t + 1), A.mult, A.add)
+        for n, o in (("sn", 0), ("so", 96)):
             scan(P("own", o, o + 48), row(n, 1), row(n, 1), -BIG, A.max, A.max)
         step_up(2)
         scores_out(3)
@@ -390,10 +427,10 @@ def rank_program(g, core, T, topo):
         for t in range(3):
             for o, c, m in ((1, A.is_lt, col(NB0)), (4, A.is_le, bit(0))):
                 ts(P("cm1", 7 * t + o, 7 * t + o + 3), P("own", 111, 144, 16), P("own", 16 * t + 15, 16 * t + 16), m, c, A.mult)
-        ts(P("hid", 0, 3), P("gs", 0, 12, 4), -7.5, MAG, A.add, A.add)
+        tc(P("gs", 0, 12, 4), lp)
         stepped(2)
         count("cm1", "c1", "m1", 6, 1)
-        ts(P("hid", 0, 3), P("hid", 0, 3), MAG, None, A.subtract)
+        ts(P("hid", 0, 3), P("gs", 0, 12, 4), -7.5, MAG, A.add, A.add)
         after(1, "c1", 6, "cm", 48, col(HC))
         scores_out(4)
         step_up(4)
@@ -406,13 +443,9 @@ def rank_program(g, core, T, topo):
                 for q in range(4):
                     act(QD("gs", rr, 24, 4, q), QD("gs", 0, 24, 4, q ^ QX[rr]))
 
-        merge(2, "c1", 6, (nothing, lambda: masked(3), lambda: (ids_out(), stepped(3))))
+        merge(2, "c1", 6, (lambda: ts(P("hid", 0, 3), P("hid", 0, 3), MAG, None, A.subtract), lambda: masked(3), lambda: (ids_out(), stepped(3))))
         after(2, "c4", 48, "cm", 48, col(HC + 1))
         scores_out(5)
-        fmm(0, 1)
-        fmm(1, 2)
-        fmm(2, 3)
-        fmm(3, 4)
         merge(3, "c4", 48, (nothing, lambda: masked(4), lambda: stepped(4)))
         after(3, "c4", 48, "cm", 48, col(HC + 2))
         act(row("so", 5), IND(SGR(5), lp))
@@ -423,11 +456,14 @@ def rank_program(g, core, T, topo):
         act(row("so", 6), IND(SGR(6), P("lb7", 0, 6)))
         step_up(6)
         scores_out(7)
+        flush(8)
+        for b in range(4):
+            fmm(b, b + 3)
         act(P("so7", 0, 192), IND(SGR(7), P("lb7", 0, 12)), scale=col(NS7))
         merge(5, "c4", 48, (nothing, lambda: [ts(P("lida", 12 * h, 12 * h + 12), P("gs", 12, 24), 16.0 * h, None, A.add) for h in range(2)], lambda: stepped(6)))
         after(5, "c4", 48, "cm6", 96, None)
         act(P("bc", 0, 192), IND(P("ioc", 0, 384), P("lbt", 0, 12)))
-        act(P("fb", 0, 384), PS(1, 0, 384))
+        act(P("fb", 0, 384), PS(3, 0, 384))
         add = []
 
         def lists_out():
@@ -440,10 +476,10 @@ def rank_program(g, core, T, topo):
             for h in range(2):
                 ts(QD("plu", 12 * h, 12 * h + 12, 1, 0, 3), QD("ldm", 12 * h, 12 * h + 12, 1, 0, 3), 7.5 + 16 * h, None, A.add)
 
-        merge(6, "c4", 48, (lists_out, nothing, lists_in, lambda: add.append(address(0, 18))))
+        merge(6, "c4", 48, (nothing, nothing, lists_in, lists_out, lambda: add.append(address(0, 18))))
         after(6, "c6", 96, "cm7", 192, col(HD7))
         for b in range(1, 4):
-            act(P("fb", 384 * b, 384 * b + 384), PS(b + 1, 0, 384))
+            act(P("fb", 384 * b, 384 * b + 384), PS(b + 3, 0, 384))
         ts(P("l7", 0, 3), ends("c6", 96), col(OF7), None, A.add)
         for q in (0, 2):
             a = 64 - 32 * q
@@ -458,10 +494,12 @@ def rank_program(g, core, T, topo):
         for rr in range(4):
             q = 3 ^ QX[rr]
             ts(QD("plu", rr, 12, 4, 3), QD("ad", 18, 21, 1, q), col(HD7, 32 * q, 32 * q + 32), None, A.add)
+        act(P("val", 0, 192), IND(P("kma", 0, 768), P("plu", 0, 12)))
         for b in range(4):
             act(P("fh", 384 * b, 384 * b + 384), P("fb", 384 * b, 384 * b + 384), scale=0.5)
         scan(P("key7", 0, 224), P("sab", 0, 224), P("sab", 224, 448), col(IN7), A.min, A.max)
         piece = lambda j: tc(IND(P("w1", 0, 768), P("plu", 4 * j, 4 * j + 4)), P("bc", 64 * j, 64 * j + 64))
+        back = lambda j: tc(IND(P("w2", 0, 768), P("lida", 4 * j, 4 * j + 4)), P("val", 64 * j, 64 * j + 64))
         piece(0)
         tr(P("tk", 0, 224), P("key7", 0, 224))
         tt(P("b0", 0, 48), IND(P("key7", 0, 224), P("pl7", 0, 3)), P("omn", 0, 48), A.mult)
@@ -478,22 +516,30 @@ def rank_program(g, core, T, topo):
         piece(2)
         for rr in range(4):
             tc(QD("plu", 12 + rr, 24, 4, 3), QD("h7", 4, 7, 1, 3 ^ QX[rr]))
+        back(0)
         tc(IND(P("w1", 0, 768), P("plu", 12, 24)), P("bc", 0, 192))
-        act(P("val", 0, 384), IND(P("kma", 0, 768), P("plu", 0, 24)))
+        act(P("val", 192, 384), IND(P("kma", 0, 768), P("plu", 12, 24)))
+        back(1)
         tr(P("t1", 0, 768), P("w1", 0, 768))
+        back(2)
         tt(P("ow", 0, 24), P("t1", 0, 768, 32), P("t1", 16, 768, 32), A.add)
         ts(P("lz", 0, 24), P("ow", 0, 24), 192.0, None, A.add)
+        back(3)
         tc(P("az", 0, 192), IND(P("fh", 0, 384), P("lz", 0, 12)))
+        back(4)
         for b in range(1, 4):
             act(P("az", 192 * b, 192 * b + 192), IND(P("fb", 384 * b, 384 * b + 384), P("lz", 0, 12)), scale=0.5)
         for b in range(4):
             tt(P("zt", b, 768, 4), IND(P("fh", 384 * b, 384 * b + 384), P("lz", 12, 24)), P("az", 192 * b, 192 * b + 192), A.add)
+        back(5)
         zc, zs = P("zc%d" % r, 0, H), P("zs%d" % r, 0, H)
         quant(zc, zs, P("zt", 0, 768))
         need("g", "sv", cnt["sv"])
         g.remote_dma(T["lc%d" % r][:, 0:H].bitcast(dt.uint8), zc[0].bitcast(dt.uint8), T.sem["ar%d" % r], T.sem.lsem, pid, rid, mask_c)
         g.remote_dma(T["ls%d" % r][:, 0:H], zs[0], T.sem["ar%d" % r], T.sem.lsem, pid, rid, mask_s)
-        tc(IND(P("w2", 0, 768), P("lida", 0, 24)), P("val", 0, 384))
+        if r == 0:
+            for h in range(2):
+                ts(P("stl", 24 * h, 24 * h + 24), P("st", 0, 24), col(JS if h else IS), None, A.add)
         act(P("odf", 0, 384), IND(P("ioc", 0, 384), P("lz", 0, 24)), F_.Identity, bias=192.0)
         if last:
             dma("y", "dout", T.od[:, :], T.odf[0:128:16, :], [], P("odf", 0, 384)[1])
@@ -518,20 +564,18 @@ def rank_program(g, core, T, topo):
         act(P("g3", 0, 384), IND(pb(3), P("lr", 0, 24)))
         for b in range(3):
             tt(P("xt", b, 1536, 4), IND(pb(b), P("lr", 0, 24)), P("fb", 384 * b, 384 * b + 384), A.add)
-        tt(P("xt", 3, 1536, 4), P("g3", 0, 384), PS(4, 0, 384), A.add)
-    scores_in()
-    for h in range(2):
-        a, b = 192 * h, 192 * h + 192
-        q = P("xc", a, b)
-        dma("y", "dout", T.oc[:, 4 * a:4 * b], q[0].bitcast(dt.uint8), [], q[1])
-        mm(PS(h, 0, 192), P("vc", 0, 128), P("vs", 0, 128), q, P("xs", a, b))
-        if h == 0:
-            tc(P("yb", a, b), PS(h, 0, 192))
-        else:
-            act(P("yb", a, b), PS(h, 0, 192))
-        dma("y", "dout", T.y[:, a:b], T.yb[:, a:b], [], P("yb", a, b)[1])
+        for a in (0, 128, 256):
+            tt(P("xt", 4 * a + 3, 4 * a + 512, 4), P("g3", a, a + 128), PS(6, a, a + 128), A.add)
+        scores_in()
+    q = P("xc", 0, 384)
+    dma("y", "dout", T.oc[:, :], q[0].bitcast(dt.uint8), [], q[1])
     for k in range(4):
         dma("y", "dout", T.osc[4 * k:4 * k + 4, :], T.xs[32 * k:32 * k + 4, :], [], P("xs", 0, 384)[1])
+    for h in range(3):
+        a, b = 128 * h, 128 * h + 128
+        mm(PS(h, 0, 128), P("vc", 0, 128), P("vs", 0, 128), P("xc", a, b), P("xs", a, b))
+        (tc if h == 1 else act)(P("yb", a, b), PS(h, 0, 128))
+        dma("y" if h == 1 else "s", "dout", T.y[:, a:b], T.yb[:, a:b], [], P("yb", a, b)[1])
     g.wait_ge(T.sem.lsem, 2 * half * NR)
     for s in list(cnt):
         need("g", s, cnt[s])

@@ -3,26 +3,27 @@ from concourse.mybir import dt, AluOpType as A, ActivationFunctionType as F_
 NR, H = 3, 192
 BIG = 1e29
 MAG = 201326592.0
-UP, TINY = 0.6 * 2.0 ** -23, 2.0 ** -124
+TINY = 2.0 ** -124
 W = [1, 3, 6, 12, 24, 48, 96, 192]
+ROW = {"c1": (3, 4), "c4": (48, 49), "c6": (96, 100), "c7": (192, 195)}
 SIDE = {1: 0, 2: 1, 3: 2, 4: 3, 5: 6, 6: 5, 7: 4}
 QX = [0, 2, 1, 3]
 SCRATCH = {"ps": ("psum", [128, 4096], "float32")}
 ALIAS = {}
 for _d, _s in (
     ("float32", "cc:64 bof:3 bxf:3 bdf:3 b0:96 o0:96 ob:96 dd:3 pg:21 hm:21 ad:21 ldm:24 gs:24 hid:3 h7:8 ow:24 iw:24 odf:384 odp:384 odx:384 psb:768 g3:384 yb:384 sgb:3072 "
-                "rr:288 own:288 sab:448 key7:224 tk:224 uk:192 row0:48 g1:96"),
-    ("bfloat16", "ioc:384 kma:768 on:128 m1:21 m4:147 m6:291 m7:579 ea:1032 ut:512 vt:512 xt:1536 fb:1536 fh:1536 cm1:21 c1:21 cm:147 c4:147 cm6:291 c6:291 cm7:579 c7:579 "
-                 "bc:192 val:384 w1:768 t1:768 w2:768 t2:768 az:768 zt:768"),
-    ("int32", "pi:1 bi:11 uli:64 pin:3"),
-    ("uint16", "ul:64 stl:48 l3:4 l0:6 lbox:6 lbo:8 l1:4 lbp:4 lb7:12 lbt:12 lida:24 pl:6 pl7:4 l7:12 plu:24 lz:24 lr:24"),
+                "rr:288 own:288 w7:104 prw:208 ar:192 key7:192 tk:224 uk:192 row0:48 g1:96"),
+    ("bfloat16", "ioc:384 kma:768 on:128 m1:12 m4:147 m6:300 m7:585 ea:1032 ut:512 vt:512 xt:1536 fb:1536 fh:1536 cm1:12 c1:12 cm4:147 c4:147 cm6:300 c6:300 cm7:585 c7:585 "
+                 "ad6:2 bc:192 val:384 w1:768 t1:768 w2:768 t2:768 az:768 zt:768"),
+    ("int32", "pi:1 bi:11 uli:64 pin:12"),
+    ("uint16", "ul:64 stl:48 l3:4 l0:6 lbox:6 lbo:8 l1:4 lbp:4 lb7:12 lbt:12 lida:24 pl:6 l7:12 plu:24 lz:24 lr:24"),
     ("float8_e4m3fn_x4", "eac:512 uc:128 uqc:1024 vc:128 wq:512 xc:384 zc0:192 zc1:192 zc2:192 lc0:192 lc1:192 lc2:192"),
     ("uint8", "eas:512 us:128 uqs:1024 vs:128 wsc:512 xs:384 zs0:192 zs1:192 zs2:192 ls0:192 ls1:192 ls2:192"),
 ):
     for _w in _s.split():
         SCRATCH[_w.split(":")[0]] = ("sbuf", [128, int(_w.split(":")[1])], _d)
-for _b, _s in (("kc", "fi:96 posr:96 aa:96 aa0:96 om:96 om0:96 omn:48 f2:48 f3:48 f4:48 mn1:48 mn2:48 mn3:48 mn4:48 mo1:48 mo2:48 mo3:48 mo4:48 x3:8 lpl:8 st:24"),
-               ("sc", "so1:48 so2:48 so3:48 so4:48 so5:48 so6:96 so7:192 sn1:48 sn2:48 sn3:48 sn4:48 sn5:48 sn6:96 sm:48 ab2:48 ab3:48 ab4:48 ab5:48 ab6:96"),
+for _b, _s in (("kc", "fi:96 posr:96 aa:96 aa0:96 om:96 om0:96 f2:48 f3:48 f4:48 mn1:48 mn2:48 mn3:48 mn4:48 mo1:48 mo2:48 mo3:48 mo4:48 x3:8 lpl:8 st:24"),
+               ("sc", "so1:48 so2:48 so3:48 so4:48 so5:48 so6:96 so7:192 sn1:48 sn2:48 sn3:48 sn4:48"),
                ("wn", "wo:96 wp:96 key:96")):
     _o = 0
     for _w in _s.split():
@@ -176,17 +177,16 @@ def rank_program(g, core, T, topo):
         act(o, i, F_.Identity, bias=bias, scale=scale)
 
     col = lambda k, p0=0, p1=128: P("cc", k, k + 1, 1, p0, p1)
-    BIT, IS, SG, CK, TK, JS, HC = 0, 7, 11, 18, 25, 32, 36
-    PB4, PB5, PB6, NB0, I3, I6, OF7, OP7, HD7, IN7, NS7, NS0, J2 = range(40, 53)
+    BIT, IS, SG, TK, JS, HC = 0, 7, 11, 25, 32, 36
+    PB4, PB5, PB6, I3, I6, OP7, TL6, NS0, J2 = range(40, 49)
     bit = lambda b: col(BIT + b)
     sg = lambda b: col(SG + b)
 
+    for h in range(2):
+        dma("ys"[h], "dp", T.pin[16 * h:16 * h + 16, :], T.p[:, 12 * h:12 * h + 12], P("pin", 0, 12, 1, 16 * h, 16 * h + 16)[1], [])
     dma("y", "du", T.ut[:, :], T.u[:, :], P("ut", 0, 512)[1], [])
     for h in range(3):
-        dma("s", "dx%d" % h, T.xt[:, 512 * h:512 * h + 512], T.x[:, 512 * h:512 * h + 512], P("xt", 512 * h, 512 * h + 512)[1], [])
-    for gr in range(8):
-        s = 4 * (gr % 2) + (gr & 2) + gr // 4
-        dma("ys"[gr % 2], "dp", T.pin[16 * gr:16 * gr + 16, :], T.p[:, 3 * s:3 * s + 3], P("pin", 0, 3, 1, 16 * gr, 16 * gr + 16)[1], [])
+        dma("y", "dx%d" % h, T.xt[:, 512 * h:512 * h + 512], T.x[:, 512 * h:512 * h + 512], P("xt", 512 * h, 512 * h + 512)[1], [])
     need("y", "dx2", 16)
     dma("y", "dwc", T.wq[:, :].bitcast(dt.uint8), T.wc[:, :], P("wq", 0, 512)[1], [])
     dma("y", "dws", T.wsc[:, :], T.ws[:, :], P("wsc", 0, 512)[1], [])
@@ -196,63 +196,51 @@ def rank_program(g, core, T, topo):
     io(P("fi", 0, 96), [[0, 6], [1, 16]])
     io(P("uli", 0, 64), [[16, 8], [0, 8]], small=False)
     io(P("ioc", 0, 384), [[1, 384]], -192)
-    io(P("f2", 0, 48), [[0, 3], [1, 8], [0, 2]])
+    for k in (2, 3, 4):
+        io(P("f%d" % k, 0, 48), [[0, 3], [1, 32 >> k], [0, 1 << (k - 1)]])
+    io(P("posr", 0, 96), [[1, 96]])
     ON = P("on", 0, 128)
-    fill(ON, 1.0)
-    fill(P("ea", 0, 1032), 0.0)
+    io(ON, [[0, 128]], 1)
+    io(P("ea", 0, 1032), [[0, 1032]])
     for h in range(2):
         sel(P("ea", 516 * h + 2 + h, 516 * h + 514, 4), ON, [[-1, 128]], A.is_equal, 0, 1)
-    io(P("posr", 0, 96), [[1, 96]])
-    for k in (3, 4):
-        io(P("f%d" % k, 0, 48), [[0, 3], [1, 32 >> k], [0, 1 << (k - 1)]])
-    for n, w in (("m6", 96), ("m7", 192)):
-        m = P(n, 0, 3 * w + 3)
-        io(m, [[0, 3 * w + 3]], 1)
-        sel(m, m, [[0, 3], [1, w + 1]], A.not_equal, 0, 0)
-    io(P("sab", 0, 448), [[0, 448]])
-    for h in range(2):
-        m = P("sab", 224 * h, 224 * h + 224)
-        sel(m, m, [[0, 224]], A.not_equal, 0, 0, -BIG if h else BIG)
+    for n, w in (("m6", 100), ("m7", 195)):
+        m = P(n, 0, 3 * w)
+        io(m, [[0, 3 * w]], 1)
+        sel(m, m, [[0, 3], [1, w]], A.not_equal, 0, 0)
     io(P("w1", 0, 768), [[0, 768]])
     for h in range(2):
         io(P("kma", 384 * h, 384 * h + 384), [[16, 12], [0, 2], [1, 16]])
         io(P("st", 12 * h, 12 * h + 12), [[96, 2], [192, 2], [16, 3]], 48 * h)
     io(P("w2", 0, 768), [[0, 768]])
+    fill(P("m1", 0, 12), 1.0)
+    fill(P("m4", 0, 147), 1.0)
+    fill(P("aa0", 0, 96), 1.0)
     for b in range(7):
         ts(P("bi", b, b + 1), P("pi", 0, 1), b, 1, A.logical_shift_right, A.bitwise_and)
     for k in range(4):
         ts(P("bi", IS + k, IS + k + 1), P("pi", 0, 1), k, 15 >> k, A.logical_shift_right, A.bitwise_and)
-    fill(P("m1", 0, 21), 1.0)
-    fill(P("m4", 0, 147), 1.0)
-    fill(P("aa0", 0, 96), 1.0)
+    fill(P("aa0", 0, 96, 32), 0.0)
+    fill(P("m1", 0, 12, 4), 0.0)
+    fill(P("m4", 0, 147, 49), 0.0)
     tc(P("cc", 0, 11), P("bi", 0, 11))
     tc(P("ul", 0, 64), P("uli", 0, 64))
-    fill(P("aa0", 0, 96, 32), 0.0)
-    fill(P("m1", 0, 21, 7), 0.0)
-    fill(P("m4", 0, 147, 49), 0.0)
-    ts(P("cc", SG, SG + 7), P("cc", BIT, BIT + 7), -2.0, 1.0, A.mult, A.add)
     ts(col(I3), col(IS), 3.0, None, A.mult)
+    ts(P("cc", SG, SG + 7), P("cc", BIT, BIT + 7), -2.0, 1.0, A.mult, A.add)
     ts(P("om", 0, 96), P("fi", 0, 96), col(IS), None, A.is_equal)
     ts(P("aa", 0, 96), P("fi", 0, 96), col(IS), None, A.not_equal)
-    tt(P("cc", JS, JS + 4), P("cc", IS, IS + 4), P("cc", SG, SG + 4), A.add)
     ts(P("lpl", 0, 3), P("x3", 0, 3), col(I3), None, A.add)
+    tt(P("cc", JS, JS + 4), P("cc", IS, IS + 4), P("cc", SG, SG + 4), A.add)
+    for q in range(4):
+        tc(QD("l3", 0, 3, 1, q), QD("pin", 3 * QX[q], 3 * QX[q] + 3, 1, 0))
     ts(P("mn1", 0, 48), P("fi", 0, 48), col(IS), -BIG, A.not_equal, A.mult)
-    for o, i, sc_, bi_ in ((NS0, 0, 2.0, -1.0), (I6, IS + 1, 6.0, 0.0), (NB0, 0, -1.0, 1.0), (PB6, 4, 192.0, -7.5), (OF7, 4, 192.0, 32.0), (OP7, 4, -32.0, 32.0), (HD7, 4, 192.0, -192.0),
-                           (IN7, 4, -2 * BIG, BIG), (NS7, 4, 2.0, -1.0), (J2, IS, 2.0, 0.0), (J2 + 1, IS, 2.0, 32.0), (J2 + 2, IS, 2.0, 64.0)):
-        lin(col(o), col(i), sc_, bi_)
-    act(P("cc", CK, CK + 7), P("cc", BIT, BIT + 7), scale=UP)
-    act(P("cc", TK, TK + 7), P("cc", BIT, BIT + 7), scale=TINY)
-    lin(col(PB5), bit(5), 96.0, col(PB6))
-    lin(P("cm1", 0, 21, 7), P("x3", 0, 3), 1.0, col(I6))
-    for t in range(6):
-        act(P("om0", 16 * t, 16 * t + 16), P("om", 0, 16), scale=col(NS0) if t % 4 in (1, 2) else sg(0))
-    lin(col(PB4), bit(6), 48.0, col(PB5))
-    act(P("omn", 0, 48), P("om", 0, 48), scale=-1.0)
-    lin(P("pg", 0, 3), P("lpl", 0, 3), 1.0, col(PB4))
-    ts(P("mo1", 0, 48), P("fi", 0, 48), col(JS), -BIG, A.not_equal, A.mult)
     tc(P("l0", 0, 3), P("lpl", 0, 3))
     for t in range(3):
         ts(P("l0", 3 + t, 4 + t), P("lpl", t, t + 1), sg(0), None, A.subtract if t == 1 else A.add)
+    cols = lambda *z: [lin(col(o), col(i), sc_, bi_) for o, i, sc_, bi_ in z]
+    cols((NS0, 0, 2.0, -1.0), (J2, IS, 2.0, 0.0), (J2 + 1, IS, 2.0, 32.0), (J2 + 2, IS, 2.0, 64.0), (I6, IS + 1, 6.0, 0.0), (PB6, 4, 192.0, -7.5))
+    for t in range(6):
+        act(P("om0", 16 * t, 16 * t + 16), P("om", 0, 16), scale=col(NS0) if t % 4 in (1, 2) else sg(0))
 
     def masks(k):
         f = P("f%d" % k, 0, 48)
@@ -260,14 +248,14 @@ def rank_program(g, core, T, topo):
         ts(P("mo%d" % k, 0, 48), f, col(JS + k - 1), BIG, A.subtract, A.mult)
         ts(col(HC + k - 2), col(JS + k - 1), bit(k - 1), -float(W[k]), A.add, A.mult)
 
-    masks(2)
     uw, ul = P("uc", 0, 128), P("ul", 0, 64)
-    quant(uw, P("us", 0, 128), P("ut", 0, 512))
-    tc(P("l3", 0, 3), P("pin", 0, 3))
+
+    def spread_s(*ks):
+        for a in ks:
+            act(P("uqs", 128 * a, 128 * a + 128), IND(P("us", 0, 128), P("ul", 8 * a, 8 * a + 8)))
 
     def spread_u(a, b):
         uo, l = P("uqc", 128 * a, 128 * b), P("ul", 8 * a, 8 * b)
-        act(P("uqs", 128 * a, 128 * b), IND(P("us", 0, 128), l))
         op("v", lambda: g.vector.tensor_copy(uo[0].bitcast(dt.uint32), uw[0].bitcast(dt.uint32).indirect(l[0])), uo[1], uw[1] + l[1])
 
     def scores_in():
@@ -281,18 +269,52 @@ def rank_program(g, core, T, topo):
         mm(PS(bank, 0, 384), P("eac", 128 * b, 128 * b + 128), P("eas", 128 * b, 128 * b + 128), P("xc", 0, 384), P("xs", 0, 384))
 
     act(P("row0", 0, 48), IND(P("ioc", 0, 384), P("l3", 0, 3)), F_.Identity, bias=192.0)
-    spread_u(0, 2)
+
+    def base(r, x, a, b):
+        if r:
+            return P("bxf" if x else "bof", a, b)
+        return P("ob", (48 if x else 0) + 16 * a + 15, (48 if x else 0) + 16 * b, 16 if b - a > 1 else 1)
+
+    def base_lists(r):
+        for n, a, st in (("lbox", 0, 2), ("lbox", 1, 2), ("lbo", 0, 1), ("lbo", 4, 1)):
+            tc(P(n, a, a + 3 * st - st + 1, st), base(r, a, 0, 3))
+        tt(P("bdf", 0, 3), base(r, 1, 0, 3), base(r, 0, 0, 3), A.subtract)
+
+    quant(uw, P("us", 0, 128), P("ut", 0, 512))
+    ts(P("mo1", 0, 48), P("fi", 0, 48), col(JS), -BIG, A.not_equal, A.mult)
     tt(P("b0", 0, 96), IND(P("row0", 0, 48), P("l0", 0, 6)), P("om", 0, 96), A.mult)
-    spread_u(2, 3)
+    spread_s(0, 1, 2, 3)
+    spread_u(0, 1)
     scan(P("ob", 0, 96), P("aa", 0, 96), P("b0", 0, 96), 0.0, A.mult, A.add)
+    spread_u(1, 2)
     scores_in()
-    spread_u(3, 4)
+    base_lists(0)
+    spread_u(2, 3)
+    lin(P("cm1", 0, 12, 4), P("x3", 0, 3), 1.0, col(I6))
+    act(P("cc", TK, TK + 7), P("cc", BIT, BIT + 7), scale=TINY)
+
+    def later_columns():
+        lin(col(PB5), bit(5), 96.0, col(PB6))
+        cols((TL6, 4, 192.0, 2064.0))
+        lin(P("cm6", 0, 300, 100), P("x3", 0, 3), 0.0, 111.0)
+        lin(P("w7", 7, 8), P("x3", 0, 1), 0.0, -BIG)
+        lin(P("prw", 0, 16), P("fi", 0, 16), 0.0, 0.0)
+        lin(P("prw", 104, 112), P("fi", 0, 8), 0.0, 0.0)
+        lin(P("ad6", 0, 1), bit(4), 192.0, -2064.0)
+        lin(col(PB4), bit(6), 48.0, col(PB5))
+        lin(P("cm6", 98, 300, 100), P("x3", 0, 3), 0.0, col(TL6))
+        lin(P("cm7", 193, 585, 195), P("x3", 0, 3), 0.0, 2256.0)
+        for n, w in (("cm6", 100), ("cm7", 195)):
+            lin(P(n, w - 1, 3 * w, w), P("x3", 0, 3), 0.0, -7.5)
+        lin(P("pg", 0, 3), P("lpl", 0, 3), 1.0, col(PB4))
+
     mode["defer"] = True
     mark = {}
-    for k in (4, 5, 6, 7):
-        spread_u(k, k + 1)
-        if k < 6:
-            masks(k - 1)
+    for k in range(2, 8):
+        if k > 2:
+            spread_u(k, k + 1)
+        if k in (2, 4, 5):
+            masks(max(2, k - 1))
         mark[k] = len(late)
     for b in range(4):
         a = 516 * (b % 2) + 2 - 2 * (b // 2)
@@ -313,73 +335,64 @@ def rank_program(g, core, T, topo):
     eng = topo.engines(core, nxt)
     half = len(eng)
     mask_c = mask_s = topo.mask(core, nxt)
-    ends = lambda cn, w: P(cn, w, 3 * w + 3, w + 1)
-    end = lambda cn, w, t, p0=0, p1=128: P(cn, (w + 1) * t + w, (w + 1) * t + w + 1, 1, p0, p1)
-    heads = lambda cn, w: P(cn, 0, 3 * w + 3, w + 1)
+    ends = lambda cn, q=0, n=4: QD(cn, ROW[cn][0], 3 * ROW[cn][1], ROW[cn][1], q, n)
+    end = lambda cn, t, o=0: P(cn, ROW[cn][1] * t + ROW[cn][0] + o, ROW[cn][1] * t + ROW[cn][0] + o + 1)
+    heads = lambda cn: P("cm" + cn[1], 0, 3 * ROW[cn][1], ROW[cn][1])
     lp = P("lbp", 0, 3)
     row = lambda n, k: P("%s%d" % (n, k), 0, 48 if k < 6 else 96)
 
     def scores_out(k):
-        if k > 3:
-            flush(k)
-            smm(k, BANK[k])
+        flush(k)
+        smm(k, BANK[k])
         act(SGR(k), PS(BANK[k], 0, 384))
 
-    def masked(k):
+    def masked(k, which="no"):
         src = IND(SGR(k), lp) if k > 1 else IND(P("g1", 0, 96), P("l1", 0, 3))
-        tt(P("sm", 0, 48) if k > 1 else row("sn", k), src, P("mn%d" % k, 0, 48), A.add)
-        tt(row("so", k), src, P("mo%d" % k, 0, 48), A.add)
+        if "n" in which:
+            tt(row("sn", k), src, P("mn%d" % k, 0, 48), A.add)
+        if "o" in which:
+            tt(row("so", k), src, P("mo%d" % k, 0, 48), A.add)
 
-    def step_up(k):
-        n = 48 if k < 6 else 96
-        act(row("ab", k), IND(SGR(k), lp if k < 6 else P("lb7", 0, 6)), F_.Abs, bias=col(TK + SIDE[k]), scale=col(CK + SIDE[k]))
-
-    def stepped(k):
-        tt(row("sn", k), P("sm", 0, 48) if k < 5 else row("so", k), row("ab", k), A.add)
-
-    def after(k, cn, w, cmn, wn, bias):
-        if bias is None:
-            act(heads(cmn, wn), ends(cn, w))
-        else:
-            act(heads(cmn, wn), ends(cn, w), F_.Identity, bias=bias)
+    def after(k, cn, to, bias):
+        lin(heads(to), ends(cn), 1.0, bias)
         if k < 6:
-            act(P("pg", 3 * k, 3 * k + 3), ends(cn, w), F_.Identity, bias=col(PB4 if k < 5 else PB5))
+            lin(P("pg", 3 * k, 3 * k + 3), ends(cn), 1.0, col(PB4 if k < 5 else PB5))
 
-    def merge(k, cn, w, gaps):
-        n, (cmn, co, mn) = (48, ("cm", "c4", "m4")) if k < 6 else (96, ("cm6", "c6", "m6"))
+    def compare(k, cn, keys, own):
+        w, n = ROW[cn]
+        for t in range(3):
+            ts(P("cm" + cn[1], n * t + 1, n * t + w + 1), keys, own(t), col(TK + SIDE[k]), A.subtract, A.is_lt)
+
+    def count(cn, parts):
+        n = 3 * ROW[cn][1] // parts
+        for a in range(0, n * parts, n):
+            scan(P(cn, a, a + n), P("m" + cn[1], a, a + n), P("cm" + cn[1], a, a + n), 0.0, A.mult, A.add)
+
+    def merge(k, cn, gaps):
+        n, co = (48, "c4") if k < 6 else (96, "c6")
         lst = P("pl", 0, n // 16)
-        tc(P("pl", 0, 3), ends(cn, w))
+        tc(P("pl", 0, 3), ends(cn))
         if k == 6:
             for q in (0, 2):
-                tc(QD("pl", 3, 6, 1, q, 2), QD(cn, w, 3 * w + 3, w + 1, 2 - q, 2))
-        reset = lambda t: ts(P("rr", 96 * t, 96 * t + n), P("posr", 0, n), end(cn, w, t), -BIG, A.is_equal, A.mult)
-        for t in range(3 if k < 6 else 2):
+                tc(QD("pl", 3, 6, 1, q, 2), ends(cn, 2 - q, 2))
+        reset = lambda t: ts(P("rr", 96 * t, 96 * t + n), P("posr", 0, n), end(cn, t), -BIG, A.is_equal, A.mult)
+        for t in range(3):
             reset(t)
         tc(IND(P("wo", 0, n), lst), row("so", k))
-        if k == 6:
-            gaps[4]()
-        tc(IND(P("wp", 0, n), lst), row("sn", k))
-        if k == 6:
-            reset(2)
-            gaps[3]()
+        if k < 5:
+            tc(IND(P("wp", 0, n), lst), row("sn", k))
+        gaps[0]()
         m, x = {5: (2, 2), 6: (1, 1)}.get(k, (4, 0))
         for q in range(0, 4, m):
             wo = QD("wo", 0, n, 1, q, m)
             scan(QD("key", 0, n, 1, q ^ x, m), wo, wo, -9 * BIG, A.max, A.max)
         for t in range(3):
-            scan(P("own", 96 * t, 96 * t + n), REV("rr", 96 * t, 96 * t + n), REV("wp", 0, n), -BIG, A.add, A.max)
-        gaps[0]()
-        for t in range(3):
-            ts(P(cmn, (n + 1) * t + 1, (n + 1) * t + n + 1), P("key", 0, n), P("own", 96 * t + n - 1, 96 * t + n), None, A.is_lt)
+            scan(P("own", 96 * t, 96 * t + n), REV("rr", 96 * t, 96 * t + n), REV("wp" if k < 5 else "wo", 0, n), -BIG, A.add, A.max)
         gaps[1]()
-        parts = 1 if k < 6 else 3
-        count(cmn, co, mn, n, parts)
+        compare(k, co, P("key", 0, n), lambda t: P("own", 96 * t + n - 1, 96 * t + n))
         gaps[2]()
-
-    def count(cmn, cn, mn, w, parts):
-        n = (3 * w + 3) // parts
-        for a in range(0, 3 * w + 3, n):
-            scan(P(cn, a, a + n), P(mn, a, a + n), P(cmn, a, a + n), 0.0, A.mult, A.add)
+        count(co, 1 if k < 6 else 3)
+        gaps[3]()
 
     def address(a, b):
         ts(P("hm", a, b), P("pg", a, b), MAG, MAG, A.add, A.subtract)
@@ -388,20 +401,12 @@ def rank_program(g, core, T, topo):
     nothing = lambda: None
     for r in range(NR):
         last = r == NR - 1
-        def base(x, a, b):
-            if r:
-                return P("bxf" if x else "bof", a, b)
-            return P("ob", (48 if x else 0) + 16 * a + 15, (48 if x else 0) + 16 * b, 16 if b - a > 1 else 1)
-
         for h in range(3):
             smm(0, h, 128 * h, 128 * h + 128)
         smm(1, 3, 0, 256)
         smm(1, 4, 256, 384)
-        for k in range(2, 4):
-            smm(k, BANK[k])
-        for n, a, st in (("lbox", 0, 2), ("lbox", 1, 2), ("lbo", 0, 1), ("lbo", 4, 1)):
-            tc(P(n, a, a + 3 * st - st + 1, st), base(a, 0, 3))
-        tt(P("bdf", 0, 3), base(1, 0, 3), base(0, 0, 3), A.subtract)
+        if r:
+            base_lists(r)
         act(P("sgb", 0, 128), PS(0, 0, 128))
         act(P("sgb", 128, 256), PS(1, 0, 128))
         tc(P("sgb", 256, 384), PS(2, 0, 128))
@@ -409,31 +414,32 @@ def rank_program(g, core, T, topo):
         act(P("sgb", 640, 768), PS(4, 0, 128))
         for h in range(2):
             act(P("g1", h, 96, 2), IND(SGR(1), P("lbo", 4 * h, 4 * h + 3)))
-        scores_out(2)
         tt(P("b0", 0, 96), IND(SGR(0), P("lbox", 0, 6)), P("om0", 0, 96), A.mult)
         scan(P("o0", 0, 96), P("aa0", 0, 96), P("b0", 0, 96), 0.0, A.mult, A.add)
         for t in range(3):
             ts(P("l1", t, t + 1), P("o0", 32 * t + 31, 32 * t + 32), 0.0, col(J2 + t), A.is_gt, A.add)
         ts(P("dd", 0, 3), P("o0", 31, 96, 32), 0.0, None, A.is_gt)
+        scores_out(2)
+        if r == 0:
+            spread_s(4)
         masked(1)
         for t in range(3):
-            ts(P("lbp", t, t + 1), P("dd", t, t + 1), P("bdf", t, t + 1), base(0, t, t + 1), A.mult, A.add)
+            ts(P("lbp", t, t + 1), P("dd", t, t + 1), P("bdf", t, t + 1), base(r, 0, t, t + 1), A.mult, A.add)
         for n, o in (("sn", 0), ("so", 96)):
             scan(P("own", o, o + 48), row(n, 1), row(n, 1), -BIG, A.max, A.max)
-        step_up(2)
         scores_out(3)
-        step_up(3)
-        masked(2)
-        for t in range(3):
-            for o, c, m in ((1, A.is_lt, col(NB0)), (4, A.is_le, bit(0))):
-                ts(P("cm1", 7 * t + o, 7 * t + o + 3), P("own", 111, 144, 16), P("own", 16 * t + 15, 16 * t + 16), m, c, A.mult)
+        if r == 0:
+            later_columns()
         tc(P("gs", 0, 12, 4), lp)
-        stepped(2)
-        count("cm1", "c1", "m1", 6, 1)
+        compare(1, "c1", P("own", 111, 144, 16), lambda t: P("own", 16 * t + 15, 16 * t + 16))
+        masked(2, "o")
         ts(P("hid", 0, 3), P("gs", 0, 12, 4), -7.5, MAG, A.add, A.add)
-        after(1, "c1", 6, "cm", 48, col(HC))
+        count("c1", 1)
+        masked(2, "n")
+        after(1, "c1", "c4", col(HC))
         scores_out(4)
-        step_up(4)
+        if r == 0:
+            spread_s(5, 6, 7)
 
         def ids_out():
             tt(P("gs", 12, 24, 4), P("hid", 0, 3), P("gs", 0, 12, 4), A.add)
@@ -443,100 +449,104 @@ def rank_program(g, core, T, topo):
                 for q in range(4):
                     act(QD("gs", rr, 24, 4, q), QD("gs", 0, 24, 4, q ^ QX[rr]))
 
-        merge(2, "c1", 6, (lambda: ts(P("hid", 0, 3), P("hid", 0, 3), MAG, None, A.subtract), lambda: masked(3), lambda: (ids_out(), stepped(3))))
-        after(2, "c4", 48, "cm", 48, col(HC + 1))
+        merge(2, "c1", (nothing, lambda: ts(P("hid", 0, 3), P("hid", 0, 3), MAG, None, A.subtract), lambda: masked(3, "o"), lambda: (masked(3, "n"), ids_out())))
+        after(2, "c4", "c4", col(HC + 1))
         scores_out(5)
-        merge(3, "c4", 48, (nothing, lambda: masked(4), lambda: stepped(4)))
-        after(3, "c4", 48, "cm", 48, col(HC + 2))
+        merge(3, "c4", (nothing, nothing, lambda: masked(4, "o"), lambda: masked(4, "n")))
+        after(3, "c4", "c4", col(HC + 2))
         act(row("so", 5), IND(SGR(5), lp))
-        step_up(5)
         scores_out(6)
-        merge(4, "c4", 48, (nothing, lambda: [tc(P("lb7", 3 * rr, 3 * rr + 3), P("gs", rr, 12, 4)) for rr in range(4)], lambda: (stepped(5), tc(P("lbt", 0, 12), P("gs", 0, 12)))))
-        after(4, "c4", 48, "cm", 48, None)
+        some = lambda *z: [tc(P("lb7", 3 * rr, 3 * rr + 3), P("gs", rr, 12, 4)) for rr in z]
+        merge(4, "c4", (nothing, nothing, lambda: some(0, 1), lambda: tc(P("lbt", 0, 12), P("gs", 0, 12))))
+        after(4, "c4", "c4", 0.0)
         act(row("so", 6), IND(SGR(6), P("lb7", 0, 6)))
-        step_up(6)
         scores_out(7)
         flush(8)
         for b in range(4):
             fmm(b, b + 3)
-        act(P("so7", 0, 192), IND(SGR(7), P("lb7", 0, 12)), scale=col(NS7))
-        merge(5, "c4", 48, (nothing, lambda: [ts(P("lida", 12 * h, 12 * h + 12), P("gs", 12, 24), 16.0 * h, None, A.add) for h in range(2)], lambda: stepped(6)))
-        after(5, "c4", 48, "cm6", 96, None)
-        act(P("bc", 0, 192), IND(P("ioc", 0, 384), P("lbt", 0, 12)))
-        act(P("fb", 0, 384), PS(3, 0, 384))
+        act(P("so7", 0, 96), IND(SGR(7), P("lb7", 0, 6)))
         add = []
 
-        def lists_out():
-            add[0]()
-            for q in range(3):
+        def lists_out(*qs):
+            for q in qs:
                 for rr in range(4):
                     act(QD("ldm", rr, 24, 4, q), QD("ad", 6 * q, 6 * q + 6, 1, q ^ QX[rr]))
+
+        merge(5, "c4", (lambda: add.append(address(0, 15)), nothing, lambda: add[0](), lambda: [ts(P("lida", 12 * h, 12 * h + 12), P("gs", 12, 24), 16.0 * h, None, A.add) for h in range(2)]))
+        lin(P("cm6", 97, 300, 100), ends("c4"), 1.0, -111.0)
+        lin(P("pg", 15, 18), ends("c4"), 1.0, col(PB5))
+        lists_out(0, 1)
+        act(P("bc", 0, 192), IND(P("ioc", 0, 384), P("lbt", 0, 12)))
+
+        def maxima():
+            scan(P("prw", 7, 104), P("w7", 7, 104), P("w7", 7, 104), -BIG, A.max, A.max)
+            for q in range(4):
+                act(QD("prw", 111, 208, 1, q), QD("prw", 7, 104, 1, q ^ 1))
+            act(P("ar", 0, 96), IND(P("prw", 8, 104), P("pl", 0, 6)))
+            for q in range(4):
+                act(QD("ar", 96, 192, 1, q), QD("ar", 0, 96, 1, q ^ 1))
 
         def lists_in():
             for h in range(2):
                 ts(QD("plu", 12 * h, 12 * h + 12, 1, 0, 3), QD("ldm", 12 * h, 12 * h + 12, 1, 0, 3), 7.5 + 16 * h, None, A.add)
 
-        merge(6, "c4", 48, (nothing, nothing, lists_in, lists_out, lambda: add.append(address(0, 18))))
-        after(6, "c6", 96, "cm7", 192, col(HD7))
-        for b in range(1, 4):
-            act(P("fb", 384 * b, 384 * b + 384), PS(b + 3, 0, 384))
-        ts(P("l7", 0, 3), ends("c6", 96), col(OF7), None, A.add)
+        add.append(None)
+        merge(6, "c4", (lambda: tc(IND(P("w7", 8, 104), P("pl", 0, 6)), P("so7", 0, 96)), maxima, lambda: add.append(address(15, 18)), lambda: (add[2](), lists_out(2))))
+        lin(heads("c7"), P("c6", 97, 300, 100), 1.0, -192.0)
+        tc(P("l7", 0, 3), ends("c6"))
         for q in (0, 2):
-            a = 64 - 32 * q
-            ts(QD("l7", 3, 6, 1, q, 2), QD("c6", 96, 291, 97, 2 - q, 2), col(OF7, a, a + 64), None, A.add)
-        ts(P("pl7", 0, 3), ends("c6", 96), col(OP7), None, A.add)
-        ts(P("hm", 18, 21), ends("c6", 96), col(PB6), MAG, A.add, A.add)
-        for q in range(4):
-            tc(QD("l7", 6, 12, 1, q), QD("l7", 0, 6, 1, q ^ 1))
+            tc(QD("l7", 3, 6, 1, q, 2), ends("c6", 2 - q, 2))
         for t in range(3):
-            ts(P("ad", 18 + t, 19 + t), P("hm", 18 + t, 19 + t), MAG - 192.0, end("c6", 96, t), A.subtract, A.add)
-        tc(IND(P("sab", 0, 448), P("l7", 0, 12)), P("so7", 0, 192))
+            ts(P("ad", 18 + t, 19 + t), end("c6", t, 3), end("c6", t, 1), P("ad6", 0, 1), A.add, A.add)
+        for q in range(4):
+            ts(QD("l7", 6, 12, 1, q), QD("l7", 0, 6, 1, q ^ 1), -104.0, None, A.add)
         for rr in range(4):
-            q = 3 ^ QX[rr]
-            ts(QD("plu", rr, 12, 4, 3), QD("ad", 18, 21, 1, q), col(HD7, 32 * q, 32 * q + 32), None, A.add)
+            tc(QD("plu", rr, 12, 4, 3), QD("ad", 18, 21, 1, 3 ^ QX[rr]))
+        tt(P("key7", 0, 192), IND(P("prw", 0, 208), P("l7", 0, 12)), P("ar", 0, 192), A.max)
+        lists_in()
         act(P("val", 0, 192), IND(P("kma", 0, 768), P("plu", 0, 12)))
         for b in range(4):
-            act(P("fh", 384 * b, 384 * b + 384), P("fb", 384 * b, 384 * b + 384), scale=0.5)
-        scan(P("key7", 0, 224), P("sab", 0, 224), P("sab", 224, 448), col(IN7), A.min, A.max)
-        piece = lambda j: tc(IND(P("w1", 0, 768), P("plu", 4 * j, 4 * j + 4)), P("bc", 64 * j, 64 * j + 64))
+            act(P("fb", 384 * b, 384 * b + 384), PS(b + 3, 0, 384))
+            act(P("fh", 384 * b, 384 * b + 384), PS(b + 3, 0, 384), scale=0.5)
+        piece = lambda j: tc(IND(P("w1", 0, 768), P("plu", 6 * j, 6 * j + 6)), P("bc", 96 * j, 96 * j + 96))
         back = lambda j: tc(IND(P("w2", 0, 768), P("lida", 4 * j, 4 * j + 4)), P("val", 64 * j, 64 * j + 64))
-        piece(0)
-        tr(P("tk", 0, 224), P("key7", 0, 224))
-        tt(P("b0", 0, 48), IND(P("key7", 0, 224), P("pl7", 0, 3)), P("omn", 0, 48), A.mult)
-        tr(P("uk", 0, 192), P("tk", 16, 208))
+        tt(P("b0", 0, 48), P("key7", 0, 48), P("om", 0, 48), A.mult)
+        for a, b, c in ((0, 128, 0), (128, 192, 128), (192, 224, 0)):
+            tr(P("tk", a, b), P("key7", c, c + b - a))
         scan(P("o0", 0, 48), P("aa", 0, 48), P("b0", 0, 48), 0.0, A.mult, A.add)
+        for a in (0, 96):
+            tr(P("uk", a, a + 96), P("tk", a + 16, a + 112))
+        piece(0)
+        compare(7, "c7", P("uk", 0, 192), lambda t: P("o0", 16 * t + 15, 16 * t + 16))
+        count("c7", 3)
+        for t in range(3):
+            ts(P("h7", t, t + 1), end("c7", t, 2), end("c7", t), -1856.0, A.add, A.add)
         piece(1)
-        for t in range(3):
-            ts(P("cm7", 193 * t + 1, 193 * t + 193), P("uk", 0, 192), P("o0", 16 * t + 15, 16 * t + 16), sg(4), A.is_lt, A.mult)
-        count("cm7", "c7", "m7", 192, 3)
-        for t in range(3):
-            ts(P("h7", t, t + 1), end("c7", 192, t), 184.5, MAG, A.add, A.add)
-        for t in range(3):
-            ts(P("h7", 4 + t, 5 + t), P("h7", t, t + 1), MAG - 208.0, end("c7", 192, t), A.subtract, A.add)
-        piece(2)
         for rr in range(4):
-            tc(QD("plu", 12 + rr, 24, 4, 3), QD("h7", 4, 7, 1, 3 ^ QX[rr]))
+            tc(QD("plu", 12 + rr, 24, 4, 3), QD("h7", 0, 3, 1, 3 ^ QX[rr]))
         back(0)
         tc(IND(P("w1", 0, 768), P("plu", 12, 24)), P("bc", 0, 192))
         act(P("val", 192, 384), IND(P("kma", 0, 768), P("plu", 12, 24)))
         back(1)
-        tr(P("t1", 0, 768), P("w1", 0, 768))
-        back(2)
-        tt(P("ow", 0, 24), P("t1", 0, 768, 32), P("t1", 16, 768, 32), A.add)
-        ts(P("lz", 0, 24), P("ow", 0, 24), 192.0, None, A.add)
-        back(3)
+        for h in range(2):
+            tr(P("t1", 384 * h, 384 * h + 384), P("w1", 384 * h, 384 * h + 384))
+        for h in range(2):
+            tt(P("ow", 12 * h, 12 * h + 12), P("t1", 384 * h, 384 * h + 384, 32), P("t1", 384 * h + 16, 384 * h + 384, 32), A.add)
+        for h in range(2):
+            ts(P("lz", 12 * h, 12 * h + 12), P("ow", 12 * h, 12 * h + 12), 192.0, None, A.add)
         tc(P("az", 0, 192), IND(P("fh", 0, 384), P("lz", 0, 12)))
-        back(4)
+        back(2)
         for b in range(1, 4):
             act(P("az", 192 * b, 192 * b + 192), IND(P("fb", 384 * b, 384 * b + 384), P("lz", 0, 12)), scale=0.5)
         for b in range(4):
             tt(P("zt", b, 768, 4), IND(P("fh", 384 * b, 384 * b + 384), P("lz", 12, 24)), P("az", 192 * b, 192 * b + 192), A.add)
-        back(5)
+        back(3)
         zc, zs = P("zc%d" % r, 0, H), P("zs%d" % r, 0, H)
         quant(zc, zs, P("zt", 0, 768))
         need("g", "sv", cnt["sv"])
         g.remote_dma(T["lc%d" % r][:, 0:H].bitcast(dt.uint8), zc[0].bitcast(dt.uint8), T.sem["ar%d" % r], T.sem.lsem, pid, rid, mask_c)
         g.remote_dma(T["ls%d" % r][:, 0:H], zs[0], T.sem["ar%d" % r], T.sem.lsem, pid, rid, mask_s)
+        tc(IND(P("w2", 0, 768), P("lida", 16, 24)), P("val", 256, 384))
         if r == 0:
             for h in range(2):
                 ts(P("stl", 24 * h, 24 * h + 24), P("st", 0, 24), col(JS if h else IS), None, A.add)
@@ -571,11 +581,10 @@ def rank_program(g, core, T, topo):
     dma("y", "dout", T.oc[:, :], q[0].bitcast(dt.uint8), [], q[1])
     for k in range(4):
         dma("y", "dout", T.osc[4 * k:4 * k + 4, :], T.xs[32 * k:32 * k + 4, :], [], P("xs", 0, 384)[1])
-    for h in range(3):
-        a, b = 128 * h, 128 * h + 128
-        mm(PS(h, 0, 128), P("vc", 0, 128), P("vs", 0, 128), P("xc", a, b), P("xs", a, b))
-        (tc if h == 1 else act)(P("yb", a, b), PS(h, 0, 128))
-        dma("y" if h == 1 else "s", "dout", T.y[:, a:b], T.yb[:, a:b], [], P("yb", a, b)[1])
+    for a in (0, 128, 256):
+        mm(PS(a // 128, 0, 128), P("vc", 0, 128), P("vs", 0, 128), P("xc", a, a + 128), P("xs", a, a + 128))
+        (act if a == 128 else tc)(P("yb", a, a + 128), PS(a // 128, 0, 128))
+    dma("s", "dout", T.y[:, :], T.yb[:, :], [], P("yb", 0, 384)[1])
     g.wait_ge(T.sem.lsem, 2 * half * NR)
     for s in list(cnt):
         need("g", s, cnt[s])

@@ -5,26 +5,26 @@ BIG = 1e29
 MAG = 201326592.0
 TINY = 2.0 ** -124
 W = [1, 3, 6, 12, 24, 48, 96, 192]
-ROW = {"c1": (3, 4), "c4": (48, 49), "c6": (96, 100), "c7": (192, 195)}
+ROW = {"c1": (3, 4), "c2": (48, 50), "c3": (48, 50), "c4": (48, 49), "c5": (48, 50), "c6": (96, 100), "c7": (192, 195)}
 SIDE = {1: 0, 2: 1, 3: 2, 4: 3, 5: 6, 6: 5, 7: 4}
 QX = [0, 2, 1, 3]
 SCRATCH = {"ps": ("psum", [128, 4096], "float32")}
 ALIAS = {}
 for _d, _s in (
     ("float32", "cc:64 bof:3 bxf:3 bdf:3 b0:96 o0:96 ob:96 dd:3 pg:21 hm:21 ad:21 ldm:24 gs:24 hid:3 h7:8 ow:24 iw:24 odf:384 odp:384 odx:384 psb:768 g3:384 yb:384 sgb:3072 "
-                "rr:288 own:288 w7:104 prw:208 ar:192 key7:192 tk:224 uk:192 row0:48 g1:96"),
-    ("bfloat16", "ioc:384 kma:768 on:128 m1:12 m4:147 m6:300 m7:585 ea:1032 ut:512 vt:512 xt:1536 fb:1536 fh:1536 cm1:12 c1:12 cm4:147 c4:147 cm6:300 c6:300 cm7:585 c7:585 "
+                "rr:288 own:288 w6:56 pr6:112 ar6:48 kr6:48 w7:104 pr7:208 ar7:96 key7:96 tk:128 uk:192 row0:48 g1:96"),
+    ("bfloat16", "ioc:384 kma:768 on:128 m1:12 m4:147 m5:150 cm2:150 c2:150 cm3:150 c3:150 cm5:150 c5:150 m6:300 m7:585 ea:1032 ut:512 vt:512 xt:1536 fb:1536 fh:1536 cm1:12 c1:12 cm4:147 c4:147 cm6:300 c6:300 cm7:585 c7:585 "
                  "ad6:2 bc:192 val:384 w1:768 t1:768 w2:768 t2:768 az:768 zt:768"),
     ("int32", "pi:1 bi:11 uli:64 pin:12"),
-    ("uint16", "ul:64 stl:48 l3:4 l0:6 lbox:6 lbo:8 l1:4 lbp:4 lb7:12 lbt:12 lida:24 pl:6 l7:12 plu:24 lz:24 lr:24"),
+    ("uint16", "ul:64 stl:48 l3:4 l0:6 lbox:6 lbo:8 l1:4 lbp:4 lb7:12 lbt:12 lida:24 pl:4 plp:4 xl:4 l6:4 pl6:6 l7:6 plu:24 lz:24 lr:24"),
     ("float8_e4m3fn_x4", "eac:512 uc:128 uqc:1024 vc:128 wq:512 xc:384 zc0:192 zc1:192 zc2:192 lc0:192 lc1:192 lc2:192"),
     ("uint8", "eas:512 us:128 uqs:1024 vs:128 wsc:512 xs:384 zs0:192 zs1:192 zs2:192 ls0:192 ls1:192 ls2:192"),
 ):
     for _w in _s.split():
         SCRATCH[_w.split(":")[0]] = ("sbuf", [128, int(_w.split(":")[1])], _d)
-for _b, _s in (("kc", "fi:96 posr:96 aa:96 aa0:96 om:96 om0:96 f2:48 f3:48 f4:48 mn1:48 mn2:48 mn3:48 mn4:48 mo1:48 mo2:48 mo3:48 mo4:48 x3:8 lpl:8 st:24"),
+for _b, _s in (("kc", "fi:96 posr:48 aa:96 aa0:96 om:96 om0:96 f2:48 f3:48 f4:48 mn1:48 mn2:48 r3:56 r4:56 mo1:48 mo2:48 mo3:48 mo4:48 x3:8 lpl:8 st:24"),
                ("sc", "so1:48 so2:48 so3:48 so4:48 so5:48 so6:96 so7:192 sn1:48 sn2:48 sn3:48 sn4:48"),
-               ("wn", "wo:96 wp:96 key:96")):
+               ("wn", "wo:48 wp:48 key:96 w3:56 w4:56 pr3:56 pr4:56 gm:48 gg:48 ar:48")):
     _o = 0
     for _w in _s.split():
         ALIAS[_w.split(":")[0]] = (_b, _o)
@@ -46,7 +46,7 @@ def rank_program(g, core, T, topo):
     def hit(r, q):
         if r[2] <= q[1] or q[2] <= r[1] or r[5] <= q[4] or q[5] <= r[4]:
             return False
-        return not (r[3] == q[3] and r[3] > 1 and (r[1] - q[1]) % r[3])
+        return r[3] == q[3] == 1 or not set(range(*r[1:4])).isdisjoint(range(*q[1:4]))
 
     def need(e, sem, val):
         k = known[e]
@@ -177,8 +177,8 @@ def rank_program(g, core, T, topo):
         act(o, i, F_.Identity, bias=bias, scale=scale)
 
     col = lambda k, p0=0, p1=128: P("cc", k, k + 1, 1, p0, p1)
-    BIT, IS, SG, TK, JS, HC = 0, 7, 11, 25, 32, 36
-    PB4, PB5, PB6, I3, I6, OP7, TL6, NS0, J2 = range(40, 49)
+    BIT, IS, SG, TK, JS, T2, T3 = 0, 7, 11, 25, 32, 36, 38
+    PB4, PB5, PB6, I3, I6, H3, H4, P2, PAD2, TL6, NS0, J2 = range(40, 52)
     bit = lambda b: col(BIT + b)
     sg = lambda b: col(SG + b)
 
@@ -198,16 +198,24 @@ def rank_program(g, core, T, topo):
     io(P("ioc", 0, 384), [[1, 384]], -192)
     for k in (2, 3, 4):
         io(P("f%d" % k, 0, 48), [[0, 3], [1, 32 >> k], [0, 1 << (k - 1)]])
-    io(P("posr", 0, 96), [[1, 96]])
+    io(P("posr", 0, 48), [[1, 48]])
     ON = P("on", 0, 128)
     io(ON, [[0, 128]], 1)
+    for n, w in (("m5", 50), ("m6", 100), ("m7", 195)):
+        io(P(n, 0, 3 * w), [[0, 3 * w]], 1)
+        if w == 50:
+            io(P("r3", 0, 112), [[0, 112]])
+    for k in (3, 4):
+        n = 96 // W[k]
+        for a in ("w", "r"):
+            sel(P("%s%d" % (a, k), 0, 48 + n), P("r%d" % k, 0, 48 + n), [[0, n], [1, 48 // n + 1]], A.not_equal, 0, 0, -BIG)
+        if k == 3:
+            sel(P("m5", 0, 150, 50), P("m5", 0, 150, 50), [[0, 3]], A.not_equal, 0, 0)
     io(P("ea", 0, 1032), [[0, 1032]])
+    for n, w in (("m6", 100), ("m7", 195)):
+        sel(P(n, 0, 3 * w, w), P(n, 0, 3 * w, w), [[0, 3]], A.not_equal, 0, 0)
     for h in range(2):
         sel(P("ea", 516 * h + 2 + h, 516 * h + 514, 4), ON, [[-1, 128]], A.is_equal, 0, 1)
-    for n, w in (("m6", 100), ("m7", 195)):
-        m = P(n, 0, 3 * w)
-        io(m, [[0, 3 * w]], 1)
-        sel(m, m, [[0, 3], [1, w]], A.not_equal, 0, 0)
     io(P("w1", 0, 768), [[0, 768]])
     for h in range(2):
         io(P("kma", 384 * h, 384 * h + 384), [[16, 12], [0, 2], [1, 16]])
@@ -244,9 +252,9 @@ def rank_program(g, core, T, topo):
 
     def masks(k):
         f = P("f%d" % k, 0, 48)
-        ts(P("mn%d" % k, 0, 48), f, col(IS + k - 1), -BIG, A.not_equal, A.mult)
-        ts(P("mo%d" % k, 0, 48), f, col(JS + k - 1), BIG, A.subtract, A.mult)
-        ts(col(HC + k - 2), col(JS + k - 1), bit(k - 1), -float(W[k]), A.add, A.mult)
+        if k == 2:
+            ts(P("mn2", 0, 48), f, col(IS + 1), -BIG, A.not_equal, A.mult)
+        ts(P("mo%d" % k, 0, 48), f, col(JS + k - 1), BIG, A.subtract if k == 2 else A.not_equal, A.mult)
 
     uw, ul = P("uc", 0, 128), P("ul", 0, 64)
 
@@ -293,15 +301,27 @@ def rank_program(g, core, T, topo):
     lin(P("cm1", 0, 12, 4), P("x3", 0, 3), 1.0, col(I6))
     act(P("cc", TK, TK + 7), P("cc", BIT, BIT + 7), scale=TINY)
 
-    def later_columns():
+    def first_columns():
+        cols((T2, 1, -6.0, 1.0), (T3, 2, -12.0, -1.0), (H4, 3, -24.0, 0.0), (PAD2, IS + 1, 1.0, 1.0), (H3, JS + 2, 13.0, 0.0))
         lin(col(PB5), bit(5), 96.0, col(PB6))
-        cols((TL6, 4, 192.0, 2064.0))
-        lin(P("cm6", 0, 300, 100), P("x3", 0, 3), 0.0, 111.0)
-        lin(P("w7", 7, 8), P("x3", 0, 1), 0.0, -BIG)
-        lin(P("prw", 0, 16), P("fi", 0, 16), 0.0, 0.0)
-        lin(P("prw", 104, 112), P("fi", 0, 8), 0.0, 0.0)
-        lin(P("ad6", 0, 1), bit(4), 192.0, -2064.0)
+        lin(col(T2 + 1), col(JS + 1), -7.0, col(T2))
+        lin(col(T3 + 1), col(JS + 2), -13.0, col(T3))
+        lin(heads("c2"), P("x3", 0, 3), 0.0, col(JS + 1))
+        lin(heads("c3"), P("x3", 0, 3), 0.0, col(H3))
         lin(col(PB4), bit(6), 48.0, col(PB5))
+        lin(col(T2), col(IS + 2), 1.0, col(T2 + 1))
+        lin(col(T3), col(IS + 2), -1.0, col(T3 + 1))
+        lin(col(H3), col(IS + 2), -1.0, col(PB4))
+
+    def later_columns():
+        cols((TL6, 4, 192.0, 2064.0))
+        for k, n in ((6, 48), (7, 96)):
+            lin(P("cm%d" % (k - 1), 0, 3 * ROW["c%d" % (k - 1)][1], ROW["c%d" % (k - 1)][1]), P("x3", 0, 3), 0.0, n + 15.0)
+            lin(P("w%d" % k, 7, 8), P("x3", 0, 1), 0.0, -BIG)
+            for a in (0, n + 8):
+                lin(P("pr%d" % k, a, a + 7), P("fi", 0, 7), 0.0, 0.0)
+        lin(P("ad6", 0, 1), bit(4), 192.0, -2064.0)
+        lin(col(P2), col(H3), 1.0, -1.0)
         lin(P("cm6", 98, 300, 100), P("x3", 0, 3), 0.0, col(TL6))
         lin(P("cm7", 193, 585, 195), P("x3", 0, 3), 0.0, 2256.0)
         for n, w in (("cm6", 100), ("cm7", 195)):
@@ -339,7 +359,7 @@ def rank_program(g, core, T, topo):
     end = lambda cn, t, o=0: P(cn, ROW[cn][1] * t + ROW[cn][0] + o, ROW[cn][1] * t + ROW[cn][0] + o + 1)
     heads = lambda cn: P("cm" + cn[1], 0, 3 * ROW[cn][1], ROW[cn][1])
     lp = P("lbp", 0, 3)
-    row = lambda n, k: P("%s%d" % (n, k), 0, 48 if k < 6 else 96)
+    row = lambda n, k: P("%s%d" % (n, k), 0, 48)
 
     def scores_out(k):
         flush(k)
@@ -353,10 +373,9 @@ def rank_program(g, core, T, topo):
         if "o" in which:
             tt(row("so", k), src, P("mo%d" % k, 0, 48), A.add)
 
-    def after(k, cn, to, bias):
-        lin(heads(to), ends(cn), 1.0, bias)
-        if k < 6:
-            lin(P("pg", 3 * k, 3 * k + 3), ends(cn), 1.0, col(PB4 if k < 5 else PB5))
+    def after(k, places, to, bias, among):
+        lin(to, places, 1.0, bias)
+        lin(P("pg", 3 * k, 3 * k + 3), places, 1.0, col(among))
 
     def compare(k, cn, keys, own):
         w, n = ROW[cn]
@@ -366,15 +385,35 @@ def rank_program(g, core, T, topo):
     def count(cn, parts):
         n = 3 * ROW[cn][1] // parts
         for a in range(0, n * parts, n):
-            scan(P(cn, a, a + n), P("m" + cn[1], a, a + n), P("cm" + cn[1], a, a + n), 0.0, A.mult, A.add)
+            scan(P(cn, a, a + n), P("m5" if ROW[cn][1] == 50 else "m" + cn[1], a, a + n), P("cm" + cn[1], a, a + n), 0.0, A.mult, A.add)
+
+    tails = lambda cn, q=0, n=4: QD(cn, 49, 150, 50, q, n)
+    padded = lambda n, k: P("%s%d" % (n, k), 0, 48 + 96 // W[k])
+    lay = lambda k: tc(IND(padded("w", k), P("plp", 0, 3)), row("so", k))
+    upto = lambda k: scan(padded("pr", k), padded("r", k), padded("w", k), -BIG, A.add, A.max)
+    mine = lambda k: tt(P("gm", 0, 48), IND(padded("pr", k), P("plp", 0, 3)), P("mn1", 0, 48), A.add)
+    theirs = lambda k: tt(P("ar", 0, 48), IND(padded("pr", k), P("plp", 0, 3)), P("mo%d" % k, 0, 48), A.add)
+
+    def merge_on(k, gaps):
+        lst = P("xl", 0, 3)
+        tc(lst, ends("c%d" % (k - 1)))
+        gaps[0]()
+        tt(P("gg", 0, 48), IND(padded("pr", k), lst), P("mn1", 0, 48), A.add)
+        tt(P("key", 0, 48), IND(padded("pr", k), lst), P("ar", 0, 48), A.max)
+        gaps[1]()
+        for t in range(3):
+            scan(P("own", 16 * t, 16 * t + 16), P("gm", 16 * t, 16 * t + 16), P("gg", 16 * t, 16 * t + 16), -BIG, A.max, A.max)
+        gaps[2]()
+        compare(k, "c%d" % k, P("key", 0, 48), lambda t: P("own", 16 * t + 15, 16 * t + 16))
+        gaps[3]()
+        count("c%d" % k, 1)
+        gaps[4]()
 
     def merge(k, cn, gaps):
-        n, co = (48, "c4") if k < 6 else (96, "c6")
-        lst = P("pl", 0, n // 16)
-        tc(P("pl", 0, 3), ends(cn))
-        if k == 6:
-            for q in (0, 2):
-                tc(QD("pl", 3, 6, 1, q, 2), ends(cn, 2 - q, 2))
+        n, co, lst = 48, "c%d" % k, P("pl", 0, 3)
+        tc(lst, ends(cn))
+        if k == 2:
+            ts(P("plp", 0, 3), ends(cn), col(PAD2), None, A.add)
         reset = lambda t: ts(P("rr", 96 * t, 96 * t + n), P("posr", 0, n), end(cn, t), -BIG, A.is_equal, A.mult)
         for t in range(3):
             reset(t)
@@ -382,7 +421,7 @@ def rank_program(g, core, T, topo):
         if k < 5:
             tc(IND(P("wp", 0, n), lst), row("sn", k))
         gaps[0]()
-        m, x = {5: (2, 2), 6: (1, 1)}.get(k, (4, 0))
+        m, x = (2, 2) if k == 5 else (4, 0)
         for q in range(0, 4, m):
             wo = QD("wo", 0, n, 1, q, m)
             scan(QD("key", 0, n, 1, q ^ x, m), wo, wo, -9 * BIG, A.max, A.max)
@@ -391,7 +430,7 @@ def rank_program(g, core, T, topo):
         gaps[1]()
         compare(k, co, P("key", 0, n), lambda t: P("own", 96 * t + n - 1, 96 * t + n))
         gaps[2]()
-        count(co, 1 if k < 6 else 3)
+        count(co, 1)
         gaps[3]()
 
     def address(a, b):
@@ -428,18 +467,22 @@ def rank_program(g, core, T, topo):
         for n, o in (("sn", 0), ("so", 96)):
             scan(P("own", o, o + 48), row(n, 1), row(n, 1), -BIG, A.max, A.max)
         scores_out(3)
+        act(row("so", 3), IND(SGR(3), lp))
         if r == 0:
-            later_columns()
+            first_columns()
         tc(P("gs", 0, 12, 4), lp)
         compare(1, "c1", P("own", 111, 144, 16), lambda t: P("own", 16 * t + 15, 16 * t + 16))
         masked(2, "o")
         ts(P("hid", 0, 3), P("gs", 0, 12, 4), -7.5, MAG, A.add, A.add)
         count("c1", 1)
         masked(2, "n")
-        after(1, "c1", "c4", col(HC))
+        after(1, ends("c1"), tails("cm2"), col(T2), PB4)
         scores_out(4)
+        act(row("so", 4), IND(SGR(4), lp))
         if r == 0:
-            spread_s(5, 6, 7)
+            spread_s(5)
+            later_columns()
+            spread_s(6, 7)
 
         def ids_out():
             tt(P("gs", 12, 24, 4), P("hid", 0, 3), P("gs", 0, 12, 4), A.add)
@@ -449,17 +492,17 @@ def rank_program(g, core, T, topo):
                 for q in range(4):
                     act(QD("gs", rr, 24, 4, q), QD("gs", 0, 24, 4, q ^ QX[rr]))
 
-        merge(2, "c1", (nothing, lambda: ts(P("hid", 0, 3), P("hid", 0, 3), MAG, None, A.subtract), lambda: masked(3, "o"), lambda: (masked(3, "n"), ids_out())))
-        after(2, "c4", "c4", col(HC + 1))
+        merge(2, "c1", (lambda: lay(3), lambda: upto(3), lambda: (mine(3), theirs(3)), lambda: ts(P("hid", 0, 3), P("hid", 0, 3), MAG, None, A.subtract)))
+        after(2, tails("c2"), tails("cm3"), col(T3), P2)
         scores_out(5)
-        merge(3, "c4", (nothing, nothing, lambda: masked(4, "o"), lambda: masked(4, "n")))
-        after(3, "c4", "c4", col(HC + 2))
         act(row("so", 5), IND(SGR(5), lp))
+        merge_on(3, (lambda: (tc(P("plp", 0, 3), tails("c2")), ids_out()), lambda: lay(4), lambda: upto(4), lambda: mine(4), lambda: theirs(4)))
+        after(3, tails("c3"), heads("c4"), col(H4), PB4)
         scores_out(6)
+        act(row("so", 6), IND(SGR(6), lp))
         some = lambda *z: [tc(P("lb7", 3 * rr, 3 * rr + 3), P("gs", rr, 12, 4)) for rr in z]
-        merge(4, "c4", (nothing, nothing, lambda: some(0, 1), lambda: tc(P("lbt", 0, 12), P("gs", 0, 12))))
-        after(4, "c4", "c4", 0.0)
-        act(row("so", 6), IND(SGR(6), P("lb7", 0, 6)))
+        merge_on(4, (nothing, nothing, nothing, lambda: some(0, 1), lambda: tc(P("lbt", 0, 12), P("gs", 0, 12))))
+        after(4, ends("c4"), tails("cm5"), -63.0, PB4)
         scores_out(7)
         flush(8)
         for b in range(4):
@@ -472,38 +515,50 @@ def rank_program(g, core, T, topo):
                 for rr in range(4):
                     act(QD("ldm", rr, 24, 4, q), QD("ad", 6 * q, 6 * q + 6, 1, q ^ QX[rr]))
 
-        merge(5, "c4", (lambda: add.append(address(0, 15)), nothing, lambda: add[0](), lambda: [ts(P("lida", 12 * h, 12 * h + 12), P("gs", 12, 24), 16.0 * h, None, A.add) for h in range(2)]))
-        lin(P("cm6", 97, 300, 100), ends("c4"), 1.0, -111.0)
-        lin(P("pg", 15, 18), ends("c4"), 1.0, col(PB5))
-        lists_out(0, 1)
-        act(P("bc", 0, 192), IND(P("ioc", 0, 384), P("lbt", 0, 12)))
+        def maxima(k, n, m, x, lst):
+            w, pr = P("w%d" % k, 7, n + 8), "pr%d" % k
+            scan(P(pr, 7, n + 8), w, w, -BIG, A.max, A.max)
+            for q in range(0, 4, m):
+                act(QD(pr, n + 15, 2 * n + 16, 1, q, m), QD(pr, 7, n + 8, 1, q ^ x, m))
+            act(P("ar%d" % k, 0, n), IND(P(pr, 8, n + 8), lst))
 
-        def maxima():
-            scan(P("prw", 7, 104), P("w7", 7, 104), P("w7", 7, 104), -BIG, A.max, A.max)
-            for q in range(4):
-                act(QD("prw", 111, 208, 1, q), QD("prw", 7, 104, 1, q ^ 1))
-            act(P("ar", 0, 96), IND(P("prw", 8, 104), P("pl", 0, 6)))
-            for q in range(4):
-                act(QD("ar", 96, 192, 1, q), QD("ar", 0, 96, 1, q ^ 1))
+        def lists_in(h):
+            ts(QD("plu", 12 * h, 12 * h + 12, 1, 0, 3), QD("ldm", 12 * h, 12 * h + 12, 1, 0, 3), 7.5 + 16 * h, None, A.add)
 
-        def lists_in():
-            for h in range(2):
-                ts(QD("plu", 12 * h, 12 * h + 12, 1, 0, 3), QD("ldm", 12 * h, 12 * h + 12, 1, 0, 3), 7.5 + 16 * h, None, A.add)
-
-        add.append(None)
-        merge(6, "c4", (lambda: tc(IND(P("w7", 8, 104), P("pl", 0, 6)), P("so7", 0, 96)), maxima, lambda: add.append(address(15, 18)), lambda: (add[2](), lists_out(2))))
+        merge(5, "c4", (lambda: (tc(IND(P("w6", 8, 56), P("pl", 0, 3)), row("so", 6)), add.append(address(0, 15))), lambda: maxima(6, 48, 2, 2, P("pl", 0, 3)), lambda: add[0](),
+                        lambda: [ts(P("lida", 12 * h, 12 * h + 12), P("gs", 12, 24), 16.0 * h, None, A.add) for h in range(2)]))
+        places = lambda q=0, n=4: QD("c5", 49, 150, 50, q, n)
+        lin(P("cm6", 97, 300, 100), places(), 1.0, -111.0)
+        lin(P("pg", 15, 18), places(), 1.0, col(PB5))
+        tc(P("l6", 0, 3), ends("c5"))
+        tc(P("pl6", 0, 3), places())
+        for q in (0, 2):
+            tc(QD("pl6", 3, 6, 1, q, 2), places(2 - q, 2))
+        tt(P("kr6", 0, 48), IND(P("pr6", 0, 112), P("l6", 0, 3)), P("ar6", 0, 48), A.max)
+        tc(IND(P("w7", 8, 104), P("pl6", 0, 6)), P("so7", 0, 96))
+        for q in range(4):
+            act(QD("key", 48, 96, 1, q), QD("kr6", 0, 48, 1, q ^ 3))
+        tt(P("b0", 0, 48), P("kr6", 0, 48), P("om", 0, 48), A.mult)
+        for q in range(4):
+            tc(QD("key", 0, 48, 1, q), QD("kr6", 0, 48, 1, q ^ 1))
+        scan(P("o0", 0, 48), P("aa", 0, 48), P("b0", 0, 48), 0.0, A.mult, A.add)
+        maxima(7, 96, 1, 1, P("pl6", 0, 6))
+        add.append(address(15, 18))
+        compare(6, "c6", P("key", 0, 96), lambda t: P("o0", 16 * t + 15, 16 * t + 16))
+        add[1]()
+        lists_out(0, 1, 2)
+        count("c6", 3)
         lin(heads("c7"), P("c6", 97, 300, 100), 1.0, -192.0)
+        act(P("bc", 0, 192), IND(P("ioc", 0, 384), P("lbt", 0, 12)))
         tc(P("l7", 0, 3), ends("c6"))
         for q in (0, 2):
             tc(QD("l7", 3, 6, 1, q, 2), ends("c6", 2 - q, 2))
         for t in range(3):
             ts(P("ad", 18 + t, 19 + t), end("c6", t, 3), end("c6", t, 1), P("ad6", 0, 1), A.add, A.add)
-        for q in range(4):
-            ts(QD("l7", 6, 12, 1, q), QD("l7", 0, 6, 1, q ^ 1), -104.0, None, A.add)
+        tt(P("key7", 0, 96), IND(P("pr7", 0, 208), P("l7", 0, 6)), P("ar7", 0, 96), A.max)
         for rr in range(4):
             tc(QD("plu", rr, 12, 4, 3), QD("ad", 18, 21, 1, 3 ^ QX[rr]))
-        tt(P("key7", 0, 192), IND(P("prw", 0, 208), P("l7", 0, 12)), P("ar", 0, 192), A.max)
-        lists_in()
+        lists_in(0)
         act(P("val", 0, 192), IND(P("kma", 0, 768), P("plu", 0, 12)))
         for b in range(4):
             act(P("fb", 384 * b, 384 * b + 384), PS(b + 3, 0, 384))
@@ -511,13 +566,17 @@ def rank_program(g, core, T, topo):
         piece = lambda j: tc(IND(P("w1", 0, 768), P("plu", 6 * j, 6 * j + 6)), P("bc", 96 * j, 96 * j + 96))
         back = lambda j: tc(IND(P("w2", 0, 768), P("lida", 4 * j, 4 * j + 4)), P("val", 64 * j, 64 * j + 64))
         tt(P("b0", 0, 48), P("key7", 0, 48), P("om", 0, 48), A.mult)
-        for a, b, c in ((0, 128, 0), (128, 192, 128), (192, 224, 0)):
-            tr(P("tk", a, b), P("key7", c, c + b - a))
-        scan(P("o0", 0, 48), P("aa", 0, 48), P("b0", 0, 48), 0.0, A.mult, A.add)
-        for a in (0, 96):
-            tr(P("uk", a, a + 96), P("tk", a + 16, a + 112))
+        tr(P("tk", 0, 96), P("key7", 0, 96))
+        tr(P("tk", 96, 128), P("key7", 0, 32))
         piece(0)
-        compare(7, "c7", P("uk", 0, 192), lambda t: P("o0", 16 * t + 15, 16 * t + 16))
+        scan(P("o0", 0, 48), P("aa", 0, 48), P("b0", 0, 48), 0.0, A.mult, A.add)
+        tr(P("uk", 0, 96), P("tk", 16, 112))
+        for q in range(4):
+            tr(QD("uk", 96, 192, 1, q), QD("tk", 16, 112, 1, q ^ 1))
+        for h in (0, 96):
+            for t in range(3):
+                ts(P("cm7", 195 * t + 1 + h, 195 * t + 97 + h), P("uk", h, h + 96), P("o0", 16 * t + 15, 16 * t + 16), col(TK + SIDE[7]), A.subtract, A.is_lt)
+        lists_in(1)
         count("c7", 3)
         for t in range(3):
             ts(P("h7", t, t + 1), end("c7", t, 2), end("c7", t), -1856.0, A.add, A.add)

from concourse.mybir import dt, AluOpType as A, ActivationFunctionType as F_

NR, H = 3, 192
BIG = 1e29
MAG = 201326592.0
TINY = 2.0 ** -124
W = [1, 3, 6, 12, 24, 48, 96, 192]
ROW = {"c1": (3, 4), "c2": (48, 50), "c3": (48, 50), "c4": (48, 49), "c5": (48, 50), "c6": (96, 100), "c7": (192, 195)}
SIDE = {1: 0, 2: 1, 3: 2, 4: 3, 5: 6, 6: 5, 7: 4}
QX = [0, 2, 1, 3]
SCRATCH = {"ps": ("psum", [128, 4096], "float32")}
ALIAS = {}
for _d, _s in (
    ("float32", "cc:64 bof:3 bxf:3 bdf:3 b0:96 o0:96 ob:96 dd:3 pg:21 hm:21 ad:21 ldm:24 gs:24 hid:3 h7:8 ow:24 iw:24 odf:384 odp:384 odx:384 psb:768 g3:384 yb:384 sgb:3072 "
                "rr:288 own:288 w6:56 pr6:112 ar6:48 kr6:48 w7:104 pr7:208 ar7:96 key7:96 tk:128 uk:192 row0:48 g1:96"),
    ("bfloat16", "ioc:384 kma:768 on:128 m1:12 m4:147 m5:150 cm2:150 c2:150 cm3:150 c3:150 cm5:150 c5:150 m6:300 m7:585 ea:1032 ut:512 vt:512 xt:1536 fb:1536 fh:1536 cm1:12 c1:12 cm4:147 c4:147 cm6:300 c6:300 cm7:585 c7:585 "
                 "ad6:2 bc:192 val:384 w1:768 t1:768 w2:768 t2:768 az:768 zt:768"),
    ("int32", "pi:1 bi:11 uli:64 pin:12"),
    ("uint16", "ul:64 stl:48 l3:4 l0:6 lbox:6 lbo:8 l1:4 lbp:4 lb7:12 lbt:12 lida:24 pl:4 plp:4 xl:4 l6:4 pl6:6 l7:6 plu:24 lz:24 lr:24"),
    ("float8_e4m3fn_x4", "eac:512 uc:128 uqc:1024 vc:128 wq:512 xc:384 zc0:192 zc1:192 zc2:192 lc0:192 lc1:192 lc2:192"),
    ("uint8", "eas:512 us:128 uqs:1024 vs:128 wsc:512 xs:384 zs0:192 zs1:192 zs2:192 ls0:192 ls1:192 ls2:192"),
):
    for _w in _s.split():
        SCRATCH[_w.split(":")[0]] = ("sbuf", [128, int(_w.split(":")[1])], _d)
for _b, _s in (("kc", "fi:96 posr:48 aa:96 aa0:96 om:96 om0:96 f2:48 f3:48 f4:48 mn1:48 mn2:48 r3:56 r4:56 mo1:48 mo2:48 mo3:48 mo4:48 x3:8 lpl:8 st:24"),
               ("sc", "so1:48 so2:48 so3:48 so4:48 so5:48 so6:96 so7:192 sn1:48 sn2:48 sn3:48 sn4:48"),
               ("wn", "wo:48 wp:48 key:96 w3:56 w4:56 pr3:56 pr4:56 gm:48 gg:48 ar:48")):
    _o = 0
    for _w in _s.split():
        ALIAS[_w.split(":")[0]] = (_b, _o)
        _o += int(_w.split(":")[1])
    SCRATCH[_b] = ("sbuf", [128, _o], "float32")
SEMAPHORES = ["sv", "ss", "st", "sg", "ar0", "ar1", "ar2", "lsem", "dp", "dx0", "dx1", "dx2", "du", "dv", "dwc", "dws", "dbo", "dbx", "dout"]


def rank_program(g, core, T, topo):
    rank = T.rank_of(core)
    if rank is None:
        return
    Q = {"v": g.vector, "s": g.scalar, "t": g.tensor, "g": g, "y": g.sync}
    SEM = {"v": "sv", "s": "ss", "t": "st", "g": "sg"}
    cnt, hist, dmh, acc = {}, {}, {}, {}
    known = {e: {} for e in Q}
    late, mode = [], {"defer": False, "mix": False}

    def hit(r, q):
        if r[2] <= q[1] or q[2] <= r[1] or r[5] <= q[4] or q[5] <= r[4]:
            return False
        return r[3] == q[3] == 1 or not set(range(*r[1:4])).isdisjoint(range(*q[1:4]))

    def need(e, sem, val):
        k = known[e]
        if k.get(sem, 0) >= val:
            return
        Q[e].wait_ge(T.sem[sem], val)
        for s_, v_ in hist.get((sem, val), {}).items():
            k[s_] = max(k.get(s_, 0), v_)
        k[sem] = max(k.get(sem, 0), val)

    def op(e, make, writes, reads, sem=None, pre=()):
        if mode["defer"]:
            late.append((e, make, writes, reads))
            return
        own = SEM.get(e) if sem is None else None
        s = own if sem is None else sem
        todo = {}
        both = [(r, True) for r in writes] + [(r, False) for r in reads]
        for r, wr in both:
            bank = r[0] == "ps"
            for q, qw, qs, qv in acc.get(r[0], []):
                if bank and r[1] // 512 != q[1] // 512 or not bank and not hit(r, q) or not (wr or qw or bank):
                    continue
                if qs == own and (not hit(r, q) or not (wr or qw) or (e == "t" and wr)):
                    continue
                todo[qs] = max(todo.get(qs, 0), qv)
        if e == "v" and mode["mix"] and late and todo.get(own, 0) > max(cnt[own] - 2, known[e].get(own, 0)):
            mode["mix"] = False
            while late[0][0] != "v":
                op(*late.pop(0))
            op(*late.pop(0))
            op(e, make, writes, reads, sem, pre)
            mode["mix"] = True
            return
        for a_, b_ in sorted(todo.items(), key=lambda z: z[0] in dmh) + list(pre):
            if known[e].get(a_, 0) < b_:
                need(e, a_, cnt[a_] if a_ in dmh else b_)
        inc = 1 if sem is None else 16
        make().then_inc(T.sem[s], inc)
        cnt[s] = cnt.get(s, 0) + inc
        h = dict(known[e])
        if sem is not None:
            old = dmh.setdefault(s, {})
            for a_, b_ in h.items():
                old[a_] = max(old.get(a_, 0), b_)
            h = dict(old)
        h[s] = cnt[s]
        hist[(s, cnt[s])] = h
        for r, wr in both:
            keep = []
            for x in acc.get(r[0], []):
                q = x[0]
                same = q == r and (wr or (not x[1] and x[2] == s))
                if not (same or wr and r[3] == 1 and r[1] <= q[1] and q[2] <= r[2] and r[4] <= q[4] and q[5] <= r[5]):
                    keep.append(x)
            acc[r[0]] = keep + [(r, wr, s, cnt[s])]

    def P(name, a, b, st=1, p0=0, p1=128):
        if name in ALIAS:
            name, o = ALIAS[name]
            a, b = a + o, b + o
        t, c = T[name], slice(a, b) if st == 1 else slice(a, b, st)
        ap = t[:, c] if (p0, p1) == (0, 128) else t[p0:p1, c]
        return (ap, [(name, a, b, st, p0, p1)], [])

    def REV(name, a, b):
        if name in ALIAS:
            name, o = ALIAS[name]
            a, b = a + o, b + o
        return (T[name][:, slice(b - 1, a - 1 if a else None, -1)], [(name, a, b, 1, 0, 128)], [])

    def QD(name, a, b, st, q, n=1):
        return P(name, a, b, st, 32 * q, 32 * (q + n))

    def IND(w, o):
        return (w[0].indirect(o[0]), w[1], o[1])

    def PS(bank, a, b):
        return P("ps", 512 * bank + a, 512 * bank + b)

    def scl(s):
        return (s[0], s[1]) if isinstance(s, tuple) else (s, [])

    def tc(o, i):
        op("v", lambda: g.vector.tensor_copy(o[0], i[0]), o[1], i[1] + i[2] + o[2])

    def tt(o, i, j, k):
        op("v", lambda: g.vector.tensor_tensor(o[0], i[0], j[0], k), o[1], i[1] + i[2] + j[1])

    def ts(o, i, s1, s2, k1, k2=None):
        (a, ra), (b, rb) = scl(s1), scl(s2)
        op("v", lambda: g.vector.tensor_scalar(o[0], i[0], a, b, k1, k2) if k2 else g.vector.tensor_scalar(o[0], i[0], a, None, k1), o[1], i[1] + i[2] + ra + rb)

    def scan(o, d0, d1, init, k0, k1):
        a, ra = scl(init)
        op("v", lambda: g.vector.tensor_tensor_scan(o[0], d0[0], d1[0], a, k0, k1), o[1], d0[1] + d1[1] + ra)

    def fill(o, c):
        op("v", lambda: g.vector.memset(o[0], c), o[1], [])

    def tr(o, i):
        op("v", lambda: g.vector.transpose(o[0], i[0]), o[1], i[1])

    def quant(c, s, i):
        op("v", lambda: g.vector.quantize_mx(c[0], s[0], i[0]), c[1] + s[1], i[1])

    def act(o, i, func=F_.Copy, bias=None, scale=None):
        kw, rr = {}, []
        for n, v in (("bias", bias), ("scale", scale)):
            if v is not None:
                kw[n], ra = scl(v)
                rr = rr + ra
        op("s", lambda: g.scalar.activation(o[0], i[0], func, **kw), o[1], i[1] + i[2] + rr)

    def mm(o, l, ls, r, rs, start=True, stop=True, pre=()):
        op("t", lambda: g.tensor.matmul_mx(o[0], l[0], ls[0], r[0], rs[0], start, stop), o[1], l[1] + ls[1] + r[1] + rs[1], pre=pre)

    def dma(e, sem, o, i, wr, rd):
        op(e, lambda: Q[e].dma_start(o, i), wr, rd, sem=sem)

    def io(o, pat, base=0, cm=0, small=True):
        op("g", lambda: g.iota(o[0], pat, base, cm, allow_small_or_imprecise_dtypes=True) if small else g.iota(o[0], pat, base, cm), o[1], [])

    def sel(o, i, pat, cmp, base, cm, other=0.0):
        op("g", lambda: g.affine_select(o[0], i[0], pat, cmp, other, base, cm), o[1], i[1])

    def lin(o, i, scale, bias):
        act(o, i, F_.Identity, bias=bias, scale=scale)

    col = lambda k, p0=0, p1=128: P("cc", k, k + 1, 1, p0, p1)
    BIT, IS, SG, TK, JS, T2, T3 = 0, 7, 11, 25, 32, 36, 38
    PB4, PB5, PB6, I3, I6, H3, H4, P2, PAD2, TL6, NS0, J2 = range(40, 52)
    bit = lambda b: col(BIT + b)
    sg = lambda b: col(SG + b)

    for h in range(2):
        dma("ys"[h], "dp", T.pin[16 * h:16 * h + 16, :], T.p[:, 12 * h:12 * h + 12], P("pin", 0, 12, 1, 16 * h, 16 * h + 16)[1], [])
    dma("y", "du", T.ut[:, :], T.u[:, :], P("ut", 0, 512)[1], [])
    for h in range(3):
        dma("y", "dx%d" % h, T.xt[:, 512 * h:512 * h + 512], T.x[:, 512 * h:512 * h + 512], P("xt", 512 * h, 512 * h + 512)[1], [])
    need("y", "dx2", 16)
    dma("y", "dwc", T.wq[:, :].bitcast(dt.uint8), T.wc[:, :], P("wq", 0, 512)[1], [])
    dma("y", "dws", T.wsc[:, :], T.ws[:, :], P("wsc", 0, 512)[1], [])
    dma("y", "dv", T.vt[:, :], T.v[:, :], P("vt", 0, 512)[1], [])
    io(P("pi", 0, 1), [[0, 1]], 0, 1, False)
    io(P("x3", 0, 3), [[1, 3]])
    io(P("fi", 0, 96), [[0, 6], [1, 16]])
    io(P("uli", 0, 64), [[16, 8], [0, 8]], small=False)
    io(P("ioc", 0, 384), [[1, 384]], -192)
    for k in (2, 3, 4):
        io(P("f%d" % k, 0, 48), [[0, 3], [1, 32 >> k], [0, 1 << (k - 1)]])
    io(P("posr", 0, 48), [[1, 48]])
    ON = P("on", 0, 128)
    io(ON, [[0, 128]], 1)
    for n, w in (("m5", 50), ("m6", 100), ("m7", 195)):
        io(P(n, 0, 3 * w), [[0, 3 * w]], 1)
        if w == 50:
            io(P("r3", 0, 112), [[0, 112]])
    for k in (3, 4):
        n = 96 // W[k]
        for a in ("w", "r"):
            sel(P("%s%d" % (a, k), 0, 48 + n), P("r%d" % k, 0, 48 + n), [[0, n], [1, 48 // n + 1]], A.not_equal, 0, 0, -BIG)
        if k == 3:
            sel(P("m5", 0, 150, 50), P("m5", 0, 150, 50), [[0, 3]], A.not_equal, 0, 0)
    io(P("ea", 0, 1032), [[0, 1032]])
    for n, w in (("m6", 100), ("m7", 195)):
        sel(P(n, 0, 3 * w, w), P(n, 0, 3 * w, w), [[0, 3]], A.not_equal, 0, 0)
    for h in range(2):
        sel(P("ea", 516 * h + 2 + h, 516 * h + 514, 4), ON, [[-1, 128]], A.is_equal, 0, 1)
    io(P("w1", 0, 768), [[0, 768]])
    for h in range(2):
        io(P("kma", 384 * h, 384 * h + 384), [[16, 12], [0, 2], [1, 16]])
        io(P("st", 12 * h, 12 * h + 12), [[96, 2], [192, 2], [16, 3]], 48 * h)
    io(P("w2", 0, 768), [[0, 768]])
    fill(P("m1", 0, 12), 1.0)
    fill(P("m4", 0, 147), 1.0)
    fill(P("aa0", 0, 96), 1.0)
    for b in range(7):
        ts(P("bi", b, b + 1), P("pi", 0, 1), b, 1, A.logical_shift_right, A.bitwise_and)
    for k in range(4):
        ts(P("bi", IS + k, IS + k + 1), P("pi", 0, 1), k, 15 >> k, A.logical_shift_right, A.bitwise_and)
    fill(P("aa0", 0, 96, 32), 0.0)
    fill(P("m1", 0, 12, 4), 0.0)
    fill(P("m4", 0, 147, 49), 0.0)
    tc(P("cc", 0, 11), P("bi", 0, 11))
    tc(P("ul", 0, 64), P("uli", 0, 64))
    ts(col(I3), col(IS), 3.0, None, A.mult)
    ts(P("cc", SG, SG + 7), P("cc", BIT, BIT + 7), -2.0, 1.0, A.mult, A.add)
    ts(P("om", 0, 96), P("fi", 0, 96), col(IS), None, A.is_equal)
    ts(P("aa", 0, 96), P("fi", 0, 96), col(IS), None, A.not_equal)
    ts(P("lpl", 0, 3), P("x3", 0, 3), col(I3), None, A.add)
    tt(P("cc", JS, JS + 4), P("cc", IS, IS + 4), P("cc", SG, SG + 4), A.add)
    for q in range(4):
        tc(QD("l3", 0, 3, 1, q), QD("pin", 3 * QX[q], 3 * QX[q] + 3, 1, 0))
    ts(P("mn1", 0, 48), P("fi", 0, 48), col(IS), -BIG, A.not_equal, A.mult)
    tc(P("l0", 0, 3), P("lpl", 0, 3))
    for t in range(3):
        ts(P("l0", 3 + t, 4 + t), P("lpl", t, t + 1), sg(0), None, A.subtract if t == 1 else A.add)
    cols = lambda *z: [lin(col(o), col(i), sc_, bi_) for o, i, sc_, bi_ in z]
    cols((NS0, 0, 2.0, -1.0), (J2, IS, 2.0, 0.0), (J2 + 1, IS, 2.0, 32.0), (J2 + 2, IS, 2.0, 64.0), (I6, IS + 1, 6.0, 0.0), (PB6, 4, 192.0, -7.5))
    for t in range(6):
        act(P("om0", 16 * t, 16 * t + 16), P("om", 0, 16), scale=col(NS0) if t % 4 in (1, 2) else sg(0))

    def masks(k):
        f = P("f%d" % k, 0, 48)
        if k == 2:
            ts(P("mn2", 0, 48), f, col(IS + 1), -BIG, A.not_equal, A.mult)
        ts(P("mo%d" % k, 0, 48), f, col(JS + k - 1), BIG, A.subtract if k == 2 else A.not_equal, A.mult)

    uw, ul = P("uc", 0, 128), P("ul", 0, 64)

    def spread_s(*ks):
        for a in ks:
            act(P("uqs", 128 * a, 128 * a + 128), IND(P("us", 0, 128), P("ul", 8 * a, 8 * a + 8)))

    def spread_u(a, b):
        uo, l = P("uqc", 128 * a, 128 * b), P("ul", 8 * a, 8 * b)
        op("v", lambda: g.vector.tensor_copy(uo[0].bitcast(dt.uint32), uw[0].bitcast(dt.uint32).indirect(l[0])), uo[1], uw[1] + l[1])

    def scores_in():
        for a in (0, 128, 256):
            quant(P("xc", a, a + 128), P("xs", a, a + 128), P("xt", 4 * a, 4 * a + 512))

    def smm(gr, bank, a=0, b=384):
        mm(PS(bank, 0, b - a), P("uqc", 128 * gr, 128 * gr + 128), P("uqs", 128 * gr, 128 * gr + 128), P("xc", a, b), P("xs", a, b))

    def fmm(b, bank):
        mm(PS(bank, 0, 384), P("eac", 128 * b, 128 * b + 128), P("eas", 128 * b, 128 * b + 128), P("xc", 0, 384), P("xs", 0, 384))

    act(P("row0", 0, 48), IND(P("ioc", 0, 384), P("l3", 0, 3)), F_.Identity, bias=192.0)

    def base(r, x, a, b):
        if r:
            return P("bxf" if x else "bof", a, b)
        return P("ob", (48 if x else 0) + 16 * a + 15, (48 if x else 0) + 16 * b, 16 if b - a > 1 else 1)

    def base_lists(r):
        for n, a, st in (("lbox", 0, 2), ("lbox", 1, 2), ("lbo", 0, 1), ("lbo", 4, 1)):
            tc(P(n, a, a + 3 * st - st + 1, st), base(r, a, 0, 3))
        tt(P("bdf", 0, 3), base(r, 1, 0, 3), base(r, 0, 0, 3), A.subtract)

    quant(uw, P("us", 0, 128), P("ut", 0, 512))
    ts(P("mo1", 0, 48), P("fi", 0, 48), col(JS), -BIG, A.not_equal, A.mult)
    tt(P("b0", 0, 96), IND(P("row0", 0, 48), P("l0", 0, 6)), P("om", 0, 96), A.mult)
    spread_s(0, 1, 2, 3)
    spread_u(0, 1)
    scan(P("ob", 0, 96), P("aa", 0, 96), P("b0", 0, 96), 0.0, A.mult, A.add)
    spread_u(1, 2)
    scores_in()
    base_lists(0)
    spread_u(2, 3)
    lin(P("cm1", 0, 12, 4), P("x3", 0, 3), 1.0, col(I6))
    act(P("cc", TK, TK + 7), P("cc", BIT, BIT + 7), scale=TINY)

    def first_columns():
        cols((T2, 1, -6.0, 1.0), (T3, 2, -12.0, -1.0), (H4, 3, -24.0, 0.0), (PAD2, IS + 1, 1.0, 1.0), (H3, JS + 2, 13.0, 0.0))
        lin(col(PB5), bit(5), 96.0, col(PB6))
        lin(col(T2 + 1), col(JS + 1), -7.0, col(T2))
        lin(col(T3 + 1), col(JS + 2), -13.0, col(T3))
        lin(heads("c2"), P("x3", 0, 3), 0.0, col(JS + 1))
        lin(heads("c3"), P("x3", 0, 3), 0.0, col(H3))
        lin(col(PB4), bit(6), 48.0, col(PB5))
        lin(col(T2), col(IS + 2), 1.0, col(T2 + 1))
        lin(col(T3), col(IS + 2), -1.0, col(T3 + 1))
        lin(col(H3), col(IS + 2), -1.0, col(PB4))

    def later_columns():
        cols((TL6, 4, 192.0, 2064.0))
        for k, n in ((6, 48), (7, 96)):
            lin(P("cm%d" % (k - 1), 0, 3 * ROW["c%d" % (k - 1)][1], ROW["c%d" % (k - 1)][1]), P("x3", 0, 3), 0.0, n + 15.0)
            lin(P("w%d" % k, 7, 8), P("x3", 0, 1), 0.0, -BIG)
            for a in (0, n + 8):
                lin(P("pr%d" % k, a, a + 7), P("fi", 0, 7), 0.0, 0.0)
        lin(P("ad6", 0, 1), bit(4), 192.0, -2064.0)
        lin(col(P2), col(H3), 1.0, -1.0)
        lin(P("cm6", 98, 300, 100), P("x3", 0, 3), 0.0, col(TL6))
        lin(P("cm7", 193, 585, 195), P("x3", 0, 3), 0.0, 2256.0)
        for n, w in (("cm6", 100), ("cm7", 195)):
            lin(P(n, w - 1, 3 * w, w), P("x3", 0, 3), 0.0, -7.5)
        lin(P("pg", 0, 3), P("lpl", 0, 3), 1.0, col(PB4))

    mode["defer"] = True
    mark = {}
    for k in range(2, 8):
        if k > 2:
            spread_u(k, k + 1)
        if k in (2, 4, 5):
            masks(max(2, k - 1))
        mark[k] = len(late)
    for b in range(4):
        a = 516 * (b % 2) + 2 - 2 * (b // 2)
        quant(P("eac", 128 * b, 128 * b + 128), P("eas", 128 * b, 128 * b + 128), P("ea", a, a + 512))
    mark[8] = len(late)
    mode["defer"], mode["mix"] = False, True

    def flush(k):
        mode["mix"] = False
        while len(late) > mark[8] - mark[k]:
            op(*late.pop(0))
        mode["mix"] = True

    SGR = lambda k: P("sgb", 384 * k, 384 * k + 384)
    BANK = {2: 5, 3: 6, 4: 7, 5: 0, 6: 1, 7: 2}
    nxt = T.cores[(rank + 1) % len(T.cores)]
    rid, pid = topo.addr(nxt)[0], topo.addr(nxt)[1]
    eng = topo.engines(core, nxt)
    half = len(eng)
    mask_c = mask_s = topo.mask(core, nxt)
    ends = lambda cn, q=0, n=4: QD(cn, ROW[cn][0], 3 * ROW[cn][1], ROW[cn][1], q, n)
    end = lambda cn, t, o=0: P(cn, ROW[cn][1] * t + ROW[cn][0] + o, ROW[cn][1] * t + ROW[cn][0] + o + 1)
    heads = lambda cn: P("cm" + cn[1], 0, 3 * ROW[cn][1], ROW[cn][1])
    lp = P("lbp", 0, 3)
    row = lambda n, k: P("%s%d" % (n, k), 0, 48)

    def scores_out(k):
        flush(k)
        smm(k, BANK[k])
        act(SGR(k), PS(BANK[k], 0, 384))

    def masked(k, which="no"):
        src = IND(SGR(k), lp) if k > 1 else IND(P("g1", 0, 96), P("l1", 0, 3))
        if "n" in which:
            tt(row("sn", k), src, P("mn%d" % k, 0, 48), A.add)
        if "o" in which:
            tt(row("so", k), src, P("mo%d" % k, 0, 48), A.add)

    def after(k, places, to, bias, among):
        lin(to, places, 1.0, bias)
        lin(P("pg", 3 * k, 3 * k + 3), places, 1.0, col(among))

    def compare(k, cn, keys, own):
        w, n = ROW[cn]
        for t in range(3):
            ts(P("cm" + cn[1], n * t + 1, n * t + w + 1), keys, own(t), col(TK + SIDE[k]), A.subtract, A.is_lt)

    def count(cn, parts):
        n = 3 * ROW[cn][1] // parts
        for a in range(0, n * parts, n):
            scan(P(cn, a, a + n), P("m5" if ROW[cn][1] == 50 else "m" + cn[1], a, a + n), P("cm" + cn[1], a, a + n), 0.0, A.mult, A.add)

    tails = lambda cn, q=0, n=4: QD(cn, 49, 150, 50, q, n)
    padded = lambda n, k: P("%s%d" % (n, k), 0, 48 + 96 // W[k])
    lay = lambda k: tc(IND(padded("w", k), P("plp", 0, 3)), row("so", k))
    upto = lambda k: scan(padded("pr", k), padded("r", k), padded("w", k), -BIG, A.add, A.max)
    mine = lambda k: tt(P("gm", 0, 48), IND(padded("pr", k), P("plp", 0, 3)), P("mn1", 0, 48), A.add)
    theirs = lambda k: tt(P("ar", 0, 48), IND(padded("pr", k), P("plp", 0, 3)), P("mo%d" % k, 0, 48), A.add)

    def merge_on(k, gaps):
        lst = P("xl", 0, 3)
        tc(lst, ends("c%d" % (k - 1)))
        gaps[0]()
        tt(P("gg", 0, 48), IND(padded("pr", k), lst), P("mn1", 0, 48), A.add)
        tt(P("key", 0, 48), IND(padded("pr", k), lst), P("ar", 0, 48), A.max)
        gaps[1]()
        for t in range(3):
            scan(P("own", 16 * t, 16 * t + 16), P("gm", 16 * t, 16 * t + 16), P("gg", 16 * t, 16 * t + 16), -BIG, A.max, A.max)
        gaps[2]()
        compare(k, "c%d" % k, P("key", 0, 48), lambda t: P("own", 16 * t + 15, 16 * t + 16))
        gaps[3]()
        count("c%d" % k, 1)
        gaps[4]()

    def merge(k, cn, gaps):
        n, co, lst = 48, "c%d" % k, P("pl", 0, 3)
        tc(lst, ends(cn))
        if k == 2:
            ts(P("plp", 0, 3), ends(cn), col(PAD2), None, A.add)
        reset = lambda t: ts(P("rr", 96 * t, 96 * t + n), P("posr", 0, n), end(cn, t), -BIG, A.is_equal, A.mult)
        for t in range(3):
            reset(t)
        tc(IND(P("wo", 0, n), lst), row("so", k))
        if k < 5:
            tc(IND(P("wp", 0, n), lst), row("sn", k))
        gaps[0]()
        m, x = (2, 2) if k == 5 else (4, 0)
        for q in range(0, 4, m):
            wo = QD("wo", 0, n, 1, q, m)
            scan(QD("key", 0, n, 1, q ^ x, m), wo, wo, -9 * BIG, A.max, A.max)
        for t in range(3):
            scan(P("own", 96 * t, 96 * t + n), REV("rr", 96 * t, 96 * t + n), REV("wp" if k < 5 else "wo", 0, n), -BIG, A.add, A.max)
        gaps[1]()
        compare(k, co, P("key", 0, n), lambda t: P("own", 96 * t + n - 1, 96 * t + n))
        gaps[2]()
        count(co, 1)
        gaps[3]()

    def address(a, b):
        ts(P("hm", a, b), P("pg", a, b), MAG, MAG, A.add, A.subtract)
        return lambda: tt(P("ad", a, b), P("hm", a, b), P("pg", a, b), A.add)

    nothing = lambda: None
    for r in range(NR):
        last = r == NR - 1
        for h in range(3):
            smm(0, h, 128 * h, 128 * h + 128)
        smm(1, 3, 0, 256)
        smm(1, 4, 256, 384)
        if r:
            base_lists(r)
        act(P("sgb", 0, 128), PS(0, 0, 128))
        act(P("sgb", 128, 256), PS(1, 0, 128))
        tc(P("sgb", 256, 384), PS(2, 0, 128))
        act(P("sgb", 384, 640), PS(3, 0, 256))
        act(P("sgb", 640, 768), PS(4, 0, 128))
        for h in range(2):
            act(P("g1", h, 96, 2), IND(SGR(1), P("lbo", 4 * h, 4 * h + 3)))
        tt(P("b0", 0, 96), IND(SGR(0), P("lbox", 0, 6)), P("om0", 0, 96), A.mult)
        scan(P("o0", 0, 96), P("aa0", 0, 96), P("b0", 0, 96), 0.0, A.mult, A.add)
        for t in range(3):
            ts(P("l1", t, t + 1), P("o0", 32 * t + 31, 32 * t + 32), 0.0, col(J2 + t), A.is_gt, A.add)
        ts(P("dd", 0, 3), P("o0", 31, 96, 32), 0.0, None, A.is_gt)
        scores_out(2)
        if r == 0:
            spread_s(4)
        masked(1)
        for t in range(3):
            ts(P("lbp", t, t + 1), P("dd", t, t + 1), P("bdf", t, t + 1), base(r, 0, t, t + 1), A.mult, A.add)
        for n, o in (("sn", 0), ("so", 96)):
            scan(P("own", o, o + 48), row(n, 1), row(n, 1), -BIG, A.max, A.max)
        scores_out(3)
        act(row("so", 3), IND(SGR(3), lp))
        if r == 0:
            first_columns()
        tc(P("gs", 0, 12, 4), lp)
        compare(1, "c1", P("own", 111, 144, 16), lambda t: P("own", 16 * t + 15, 16 * t + 16))
        masked(2, "o")
        ts(P("hid", 0, 3), P("gs", 0, 12, 4), -7.5, MAG, A.add, A.add)
        count("c1", 1)
        masked(2, "n")
        after(1, ends("c1"), tails("cm2"), col(T2), PB4)
        scores_out(4)
        act(row("so", 4), IND(SGR(4), lp))
        if r == 0:
            spread_s(5)
            later_columns()
            spread_s(6, 7)

        def ids_out():
            tt(P("gs", 12, 24, 4), P("hid", 0, 3), P("gs", 0, 12, 4), A.add)
            for q in (0, 2):
                act(QD("gs", 1, 24, 4, q, 2), QD("gs", 0, 24, 4, 2 - q, 2))
            for rr in (2, 3):
                for q in range(4):
                    act(QD("gs", rr, 24, 4, q), QD("gs", 0, 24, 4, q ^ QX[rr]))

        merge(2, "c1", (lambda: lay(3), lambda: upto(3), lambda: (mine(3), theirs(3)), lambda: ts(P("hid", 0, 3), P("hid", 0, 3), MAG, None, A.subtract)))
        after(2, tails("c2"), tails("cm3"), col(T3), P2)
        scores_out(5)
        act(row("so", 5), IND(SGR(5), lp))
        merge_on(3, (lambda: (tc(P("plp", 0, 3), tails("c2")), ids_out()), lambda: lay(4), lambda: upto(4), lambda: mine(4), lambda: theirs(4)))
        after(3, tails("c3"), heads("c4"), col(H4), PB4)
        scores_out(6)
        act(row("so", 6), IND(SGR(6), lp))
        some = lambda *z: [tc(P("lb7", 3 * rr, 3 * rr + 3), P("gs", rr, 12, 4)) for rr in z]
        merge_on(4, (nothing, nothing, nothing, lambda: some(0, 1), lambda: tc(P("lbt", 0, 12), P("gs", 0, 12))))
        after(4, ends("c4"), tails("cm5"), -63.0, PB4)
        scores_out(7)
        flush(8)
        for b in range(4):
            fmm(b, b + 3)
        act(P("so7", 0, 96), IND(SGR(7), P("lb7", 0, 6)))
        add = []

        def lists_out(*qs):
            for q in qs:
                for rr in range(4):
                    act(QD("ldm", rr, 24, 4, q), QD("ad", 6 * q, 6 * q + 6, 1, q ^ QX[rr]))

        def maxima(k, n, m, x, lst):
            w, pr = P("w%d" % k, 7, n + 8), "pr%d" % k
            scan(P(pr, 7, n + 8), w, w, -BIG, A.max, A.max)
            for q in range(0, 4, m):
                act(QD(pr, n + 15, 2 * n + 16, 1, q, m), QD(pr, 7, n + 8, 1, q ^ x, m))
            act(P("ar%d" % k, 0, n), IND(P(pr, 8, n + 8), lst))

        def lists_in(h):
            ts(QD("plu", 12 * h, 12 * h + 12, 1, 0, 3), QD("ldm", 12 * h, 12 * h + 12, 1, 0, 3), 7.5 + 16 * h, None, A.add)

        merge(5, "c4", (lambda: (tc(IND(P("w6", 8, 56), P("pl", 0, 3)), row("so", 6)), add.append(address(0, 15))), lambda: maxima(6, 48, 2, 2, P("pl", 0, 3)), lambda: add[0](),
                        lambda: [ts(P("lida", 12 * h, 12 * h + 12), P("gs", 12, 24), 16.0 * h, None, A.add) for h in range(2)]))
        places = lambda q=0, n=4: QD("c5", 49, 150, 50, q, n)
        lin(P("cm6", 97, 300, 100), places(), 1.0, -111.0)
        lin(P("pg", 15, 18), places(), 1.0, col(PB5))
        tc(P("l6", 0, 3), ends("c5"))
        tc(P("pl6", 0, 3), places())
        for q in (0, 2):
            tc(QD("pl6", 3, 6, 1, q, 2), places(2 - q, 2))
        tt(P("kr6", 0, 48), IND(P("pr6", 0, 112), P("l6", 0, 3)), P("ar6", 0, 48), A.max)
        tc(IND(P("w7", 8, 104), P("pl6", 0, 6)), P("so7", 0, 96))
        for q in range(4):
            act(QD("key", 48, 96, 1, q), QD("kr6", 0, 48, 1, q ^ 3))
        tt(P("b0", 0, 48), P("kr6", 0, 48), P("om", 0, 48), A.mult)
        for q in range(4):
            tc(QD("key", 0, 48, 1, q), QD("kr6", 0, 48, 1, q ^ 1))
        scan(P("o0", 0, 48), P("aa", 0, 48), P("b0", 0, 48), 0.0, A.mult, A.add)
        maxima(7, 96, 1, 1, P("pl6", 0, 6))
        add.append(address(15, 18))
        compare(6, "c6", P("key", 0, 96), lambda t: P("o0", 16 * t + 15, 16 * t + 16))
        add[1]()
        lists_out(0, 1, 2)
        count("c6", 3)
        lin(heads("c7"), P("c6", 97, 300, 100), 1.0, -192.0)
        act(P("bc", 0, 192), IND(P("ioc", 0, 384), P("lbt", 0, 12)))
        tc(P("l7", 0, 3), ends("c6"))
        for q in (0, 2):
            tc(QD("l7", 3, 6, 1, q, 2), ends("c6", 2 - q, 2))
        for t in range(3):
            ts(P("ad", 18 + t, 19 + t), end("c6", t, 3), end("c6", t, 1), P("ad6", 0, 1), A.add, A.add)
        tt(P("key7", 0, 96), IND(P("pr7", 0, 208), P("l7", 0, 6)), P("ar7", 0, 96), A.max)
        for rr in range(4):
            tc(QD("plu", rr, 12, 4, 3), QD("ad", 18, 21, 1, 3 ^ QX[rr]))
        lists_in(0)
        act(P("val", 0, 192), IND(P("kma", 0, 768), P("plu", 0, 12)))
        for b in range(4):
            act(P("fb", 384 * b, 384 * b + 384), PS(b + 3, 0, 384))
            act(P("fh", 384 * b, 384 * b + 384), PS(b + 3, 0, 384), scale=0.5)
        piece = lambda j: tc(IND(P("w1", 0, 768), P("plu", 6 * j, 6 * j + 6)), P("bc", 96 * j, 96 * j + 96))
        back = lambda j: tc(IND(P("w2", 0, 768), P("lida", 4 * j, 4 * j + 4)), P("val", 64 * j, 64 * j + 64))
        tt(P("b0", 0, 48), P("key7", 0, 48), P("om", 0, 48), A.mult)
        tr(P("tk", 0, 96), P("key7", 0, 96))
        tr(P("tk", 96, 128), P("key7", 0, 32))
        piece(0)
        scan(P("o0", 0, 48), P("aa", 0, 48), P("b0", 0, 48), 0.0, A.mult, A.add)
        tr(P("uk", 0, 96), P("tk", 16, 112))
        for q in range(4):
            tr(QD("uk", 96, 192, 1, q), QD("tk", 16, 112, 1, q ^ 1))
        for h in (0, 96):
            for t in range(3):
                ts(P("cm7", 195 * t + 1 + h, 195 * t + 97 + h), P("uk", h, h + 96), P("o0", 16 * t + 15, 16 * t + 16), col(TK + SIDE[7]), A.subtract, A.is_lt)
        lists_in(1)
        count("c7", 3)
        for t in range(3):
            ts(P("h7", t, t + 1), end("c7", t, 2), end("c7", t), -1856.0, A.add, A.add)
        piece(1)
        for rr in range(4):
            tc(QD("plu", 12 + rr, 24, 4, 3), QD("h7", 0, 3, 1, 3 ^ QX[rr]))
        back(0)
        tc(IND(P("w1", 0, 768), P("plu", 12, 24)), P("bc", 0, 192))
        act(P("val", 192, 384), IND(P("kma", 0, 768), P("plu", 12, 24)))
        back(1)
        for h in range(2):
            tr(P("t1", 384 * h, 384 * h + 384), P("w1", 384 * h, 384 * h + 384))
        for h in range(2):
            tt(P("ow", 12 * h, 12 * h + 12), P("t1", 384 * h, 384 * h + 384, 32), P("t1", 384 * h + 16, 384 * h + 384, 32), A.add)
        for h in range(2):
            ts(P("lz", 12 * h, 12 * h + 12), P("ow", 12 * h, 12 * h + 12), 192.0, None, A.add)
        tc(P("az", 0, 192), IND(P("fh", 0, 384), P("lz", 0, 12)))
        back(2)
        for b in range(1, 4):
            act(P("az", 192 * b, 192 * b + 192), IND(P("fb", 384 * b, 384 * b + 384), P("lz", 0, 12)), scale=0.5)
        for b in range(4):
            tt(P("zt", b, 768, 4), IND(P("fh", 384 * b, 384 * b + 384), P("lz", 12, 24)), P("az", 192 * b, 192 * b + 192), A.add)
        back(3)
        zc, zs = P("zc%d" % r, 0, H), P("zs%d" % r, 0, H)
        quant(zc, zs, P("zt", 0, 768))
        need("g", "sv", cnt["sv"])
        g.remote_dma(T["lc%d" % r][:, 0:H].bitcast(dt.uint8), zc[0].bitcast(dt.uint8), T.sem["ar%d" % r], T.sem.lsem, pid, rid, mask_c)
        g.remote_dma(T["ls%d" % r][:, 0:H], zs[0], T.sem["ar%d" % r], T.sem.lsem, pid, rid, mask_s)
        tc(IND(P("w2", 0, 768), P("lida", 16, 24)), P("val", 256, 384))
        if r == 0:
            for h in range(2):
                ts(P("stl", 24 * h, 24 * h + 24), P("st", 0, 24), col(JS if h else IS), None, A.add)
        act(P("odf", 0, 384), IND(P("ioc", 0, 384), P("lz", 0, 24)), F_.Identity, bias=192.0)
        if last:
            dma("y", "dout", T.od[:, :], T.odf[0:128:16, :], [], P("odf", 0, 384)[1])
        else:
            for n, a, to, sem in (("odp", 0, "bof", "dbo"), ("odx", 24, "bxf", "dbx")):
                act(P(n, 0, 384), IND(P("odf", 0, 384), P("stl", a, a + 24)))
                dma("y", sem, T[to][:, :], T[n][112:113, :], P(to, 0, 3)[1], P(n, 0, 384)[1])
        tr(P("t2", 0, 768), P("w2", 0, 768))
        if r == 0:
            quant(P("vc", 0, 128), P("vs", 0, 128), P("vt", 0, 512))
        tt(P("iw", 0, 24), P("t2", 0, 768, 32), P("t2", 16, 768, 32), A.add)
        tc(P("lr", 0, 24), P("iw", 0, 24))
        if not last:
            io(P("w1", 0, 768), [[0, 768]])
            io(P("w2", 0, 768), [[0, 768]])
        pb = lambda b: P("psb", 192 * b, 192 * b + 192)
        for b in range(4):
            mm(PS(b, 0, H), P("wq", 128 * b, 128 * b + 128), P("wsc", 128 * b, 128 * b + 128), P("lc%d" % r, 0, H), P("ls%d" % r, 0, H), pre=[("ar%d" % r, 2 * half)])
        ts(pb(0), PS(0, 0, H), 0.03125, None, A.mult)
        for b in range(1, 4):
            act(pb(b), PS(b, 0, H), scale=0.03125)
        act(P("g3", 0, 384), IND(pb(3), P("lr", 0, 24)))
        for b in range(3):
            tt(P("xt", b, 1536, 4), IND(pb(b), P("lr", 0, 24)), P("fb", 384 * b, 384 * b + 384), A.add)
        for a in (0, 128, 256):
            tt(P("xt", 4 * a + 3, 4 * a + 512, 4), P("g3", a, a + 128), PS(6, a, a + 128), A.add)
        scores_in()
    q = P("xc", 0, 384)
    dma("y", "dout", T.oc[:, :], q[0].bitcast(dt.uint8), [], q[1])
    for k in range(4):
        dma("y", "dout", T.osc[4 * k:4 * k + 4, :], T.xs[32 * k:32 * k + 4, :], [], P("xs", 0, 384)[1])
    for a in (0, 128, 256):
        mm(PS(a // 128, 0, 128), P("vc", 0, 128), P("vs", 0, 128), P("xc", a, a + 128), P("xs", a, a + 128))
        (act if a == 128 else tc)(P("yb", a, a + 128), PS(a // 128, 0, 128))
    dma("s", "dout", T.y[:, :], T.yb[:, :], [], P("yb", 0, 384)[1])
    g.wait_ge(T.sem.lsem, 2 * half * NR)
    for s in list(cnt):
        need("g", s, cnt[s])
